import numpy as np
import ml_dtypes


def mxq(x, axis, fmt="e4m3"):
    dtype, down = {"e4m3": (ml_dtypes.float8_e4m3fn, 7), "e5m2": (ml_dtypes.float8_e5m2, 14)}[fmt]
    v = np.moveaxis(np.asarray(x, np.float32).astype(ml_dtypes.bfloat16).astype(np.float64), axis, -1)
    blocks = v.reshape(v.shape[:-1] + (-1, 32))
    amax = np.abs(blocks).max(-1, keepdims=True)
    byte = np.maximum(np.where(amax > 0, np.frexp(amax)[1] - 1 + 127, 0) - down, 1)
    scale = np.exp2(byte - 127.0)
    codes = (blocks / scale).astype(np.float32).astype(dtype).astype(np.float64)
    return np.moveaxis((codes * scale).reshape(v.shape), -1, axis)


WIDE = False


def mx_kscale(k):
    if not WIDE:
        return np.ones(k)
    levels = np.array([10, -10, 5, -5, 0])
    if k % 512:
        return np.exp2(np.random.permutation(np.resize(levels, k // 32))).repeat(32)
    a = np.empty((k // 512, 16))
    for p in range(k // 512):
        a[p, :8] = np.random.permutation(np.resize(levels, 8))
        for g in range(8):
            far = levels[np.abs(levels - a[p, g]) >= 10]
            a[p, g + 8] = far[np.random.randint(len(far))]
    return np.exp2(a.ravel()).repeat(32)


def f64(x):
    return np.asarray(x).astype(np.float64)


def striped(idx):
    return np.tile(np.asarray(idx).reshape(-1, 16).T, (8, 1)).astype(np.uint16)


def unstriped(offs):
    return offs[:16].T.reshape(-1).astype(np.int64)


E2M1 = np.array([0.0, 0.5, 1.0, 1.5, 2.0, 3.0, 4.0, 6.0, -0.0, -0.5, -1.0, -1.5, -2.0, -3.0, -4.0, -6.0])


def pack_weight(w, fmt):
    k, n = w.shape
    w = f64(np.asarray(w, np.float32).astype(ml_dtypes.bfloat16)).reshape(k // 32, 32, n)
    amax = np.abs(w).max(1)
    if fmt == "e4m3":
        byte = np.frexp(amax)[1] - 1 + 127 - 7
    else:
        mant, ex = np.frexp(amax / 6.0)
        byte = np.where(mant > 0.5, ex, ex - 1) + 127
    byte = np.clip(np.where(amax > 0, byte, 1), 1, 254)
    scaled = (w * np.exp2(127.0 - byte)[:, None, :]).reshape(k, n).astype(np.float32)
    by_word = np.ascontiguousarray(scaled.reshape(k // 512, 128, 4, n).transpose(0, 1, 3, 2))
    if fmt == "e4m3":
        words = by_word.astype(ml_dtypes.float8_e4m3fn).view(np.uint8)
    else:
        c = by_word.astype(ml_dtypes.float4_e2m1fn).view(np.uint8) & 0xF
        words = (c[..., 0::2] | (c[..., 1::2] << 4)).reshape(k // 512, 128, 2 * n)
    return np.ascontiguousarray(words), np.ascontiguousarray(byte.astype(np.uint8).reshape(k // 512, 16, n))


def unpack_weight(words, scales, fmt):
    g, _, n = scales.shape
    words = np.ascontiguousarray(words).reshape(g, 128, n, -1)
    if fmt == "e4m3":
        vals = words.view(ml_dtypes.float8_e4m3fn).astype(np.float64)
    else:
        nib = np.empty((g, 128, n, 4), np.uint8)
        nib[..., 0::2] = words & 0xF
        nib[..., 1::2] = words >> 4
        vals = E2M1[nib]
    vals = vals * np.repeat(np.exp2(scales.astype(np.float64) - 127.0), 8, axis=1)[..., None]
    return vals.transpose(0, 1, 3, 2).reshape(g * 512, n)


B, N, T, D, DV, NQ = 1, 1536, 4096, 1024, 256, 128
PAGE = 512


def setup_inputs():
    n = np.random.standard_normal
    pages = np.random.permutation(T // PAGE)[:B * N // PAGE]
    idx = (pages[:, None] * PAGE + np.arange(PAGE)[None, :]).reshape(-1)
    s = mx_kscale(D)[:, None]
    u = np.ones(T)
    u[idx] = mx_kscale(B * N)
    r = np.random.uniform(0.5, 2.0, T)
    qp = [pack_weight(x, "e4m3") for x in n((B, D, NQ)) * s * (0.80 / np.sqrt(D))]
    k = n((D, T)) / s
    v = n((DV, T)) / (u * r)
    kp = pack_weight(k, "e2m1")
    vp = pack_weight(v.T, "e4m3")
    return {
        "q_words": np.stack([x[0] for x in qp]),
        "q_scales": np.stack([x[1] for x in qp]),
        "k_words": np.ascontiguousarray(kp[0].reshape(D // 1024, 2, 128, T, 2).transpose(0, 2, 3, 1, 4)).reshape(D // 1024, 128, T, 4),
        "k_scales": kp[1],
        "v_words": vp[0],
        "v_scales": vp[1],
        "vs": np.tile(u * r, (128, 1)).astype(np.float32),
        "offs": striped(idx),
        "voffs": striped((pages[:, None] * DV + np.arange(DV)[None, :]).reshape(-1)),
    }


def reference(q_words, q_scales, k_words, k_scales, v_words, v_scales, vs, offs, voffs):
    idx = unstriped(offs)
    k = unpack_weight(k_words.reshape(D // 1024, 128, T, 2, 2).transpose(0, 3, 1, 2, 4).reshape(D // 512, 128, 2 * T), k_scales, "e2m1")
    v = unpack_weight(v_words, v_scales, "e4m3")
    v = v.reshape(T // 512, 512, DV)[unstriped(voffs)[::DV] // DV].reshape(B, N, DV)
    pick = lambda x: x[:, idx].reshape(x.shape[0], B, N).transpose(1, 0, 2)
    q = np.stack([unpack_weight(q_words[b], q_scales[b], "e4m3") for b in range(B)])
    score = q.transpose(0, 2, 1) @ pick(k)
    p = score / (1.0 + np.exp(-score))
    w = p * pick(f64(vs))[:, :1, :]
    y = mxq(w, 2, "e4m3") @ v
    y = y / 16.0
    return y

@@ -1,0 +1,153 @@
+from contextlib import ExitStack
+
+import concourse.mybir as mybir
+from concourse.masks import make_identity
+
+NQ, N, T, D, DV = 128, 1536, 4096, 1024, 256
+PAGE = 512
+PAGES = N // PAGE
+POOL_PAGES = T // PAGE
+PASSES = D // 512
+P = 128
+FLOPS = 2 * NQ * N * (D + DV)
+
+F32 = mybir.dt.float32
+BF16 = mybir.dt.bfloat16
+I32 = mybir.dt.int32
+U32 = mybir.dt.uint32
+U16 = mybir.dt.uint16
+U8 = mybir.dt.uint8
+FP8X4 = mybir.dt.float8_e4m3fn_x4
+FP4X4 = mybir.dt.float4_e2m1fn_x4
+ACT = mybir.ActivationFunctionType
+MULT = mybir.AluOpType.mult
+
+
+def tile_attend_pkv4q_silu_kernel(tc, q_words, q_scales, k_words, k_scales, v_words, v_scales, vs, offs, voffs, out):
+    nc = tc.nc
+    with ExitStack() as ctx:
+        keep = ctx.enter_context(tc.tile_pool(name="keep", bufs=1))
+        ring = ctx.enter_context(tc.tile_pool(name="ring", bufs=3))
+        psum = ctx.enter_context(tc.psum_pool(name="psum", bufs=1))
+
+        offs_sb = keep.tile([P, N // 16], U16, name="offs_sb")
+        voffs_sb = keep.tile([P, PAGES * DV // 16], U16, name="voffs_sb")
+        vs_rows = keep.tile([P, T // P], F32, name="vs_rows")
+        k_pool = keep.tile([P, T], I32, name="k_pool")
+        ks_pool = keep.tile([P, T], U8, name="ks_pool", tag="shared")
+        ks_low = keep.tile([P, N], U8, name="ks_low", align_bytes=64)
+        vsc_pool = keep.tile([P, POOL_PAGES * DV], U8, name="vsc_pool")
+        vs_pool = keep.tile([P, T], F32, name="vs_pool")
+        q_codes = keep.tile([P, PASSES, NQ], I32, name="q_codes", align_bytes=64)
+        q_sc = keep.tile([P, PASSES * NQ], U8, name="q_sc", align_bytes=64)
+        ident = keep.tile([P, P], F32, name="ident")
+        warm = keep.tile([P, 1], F32, name="warm")
+
+        nc.vector.memset(ks_pool[:].bitcast(I32), 0)
+        nc.vector.memset(q_sc[:].bitcast(I32), 0)
+        nc.vector.memset(vsc_pool[:].bitcast(I32), 0)
+        nc.vector.memset(ks_low[:].bitcast(I32), 0)
+        make_identity(nc, ident[:])
+
+        nc.sync.dma_start(offs_sb[:], offs)
+        nc.sync.dma_start(vs_rows[:], vs[0].rearrange("(p c) -> p c", p=P))
+        nc.sync.dma_start(k_pool[:], k_words[0].rearrange("g t b -> g (t b)").bitcast(I32))
+        nc.sync.dma_start(voffs_sb[:], voffs)
+        ks_rows = k_scales.bitcast(I32).rearrange("o (quad j) t -> j quad o t", j=4)
+        for j in range(4):
+            nc.scalar.dma_start(ks_pool[j:P:16, :].bitcast(I32), ks_rows[j])
+        nc.scalar.activation(warm[:], ident[:, 0:1], ACT.Silu)
+        nc.gpsimd.dma_start(q_codes[:], q_words[0].rearrange("o g q r -> g o (q r)").bitcast(I32))
+        for quad in range(4):
+            nc.gpsimd.dma_start(
+                q_sc[32 * quad : 32 * quad + 4, :].bitcast(I32).rearrange("f (o q) -> f o q", o=PASSES),
+                q_scales[0, :, 4 * quad : 4 * quad + 4, :].bitcast(I32).rearrange("o f q -> f o q"),
+            )
+        for quad in range(4):
+            nc.gpsimd.dma_start(
+                vsc_pool[32 * quad : 32 * quad + 4, :].bitcast(I32).rearrange("f (u e) -> f u e", u=POOL_PAGES),
+                v_scales[:, 4 * quad : 4 * quad + 4, :].bitcast(I32).rearrange("u f e -> f u e"),
+            )
+
+        per_row = T // P
+        vs_view = vs_pool[:].rearrange("p (n b m) -> p b n m", b=per_row // 4, m=4)
+        for b in range(per_row // 4):
+            spread = psum.tile([P, 4, P], F32, name="spread", bufs=3)
+            for m in range(4):
+                c = 4 * b + m
+                nc.tensor.transpose(spread[:, m, :], vs_rows[:, c : c + 1].to_broadcast([P, P]), ident[:])
+            nc.scalar.activation(vs_view[:, b], spread[:].rearrange("p m n -> p n m"), ACT.Copy)
+
+        ks_both = keep.tile([P, N], U8, name="ks_both", align_bytes=64)
+        nc.vector.tensor_copy(ks_both[:], ks_pool[:].indirect(offs_sb[:]))
+        nc.sync.dma_start(ks_low[0 : P - 16, :].bitcast(I32), ks_both[16:P, :].bitcast(I32))
+        ks_got = [ks_both, ks_low]
+        v_pool = keep.tile([P, POOL_PAGES * DV], I32, name="v_pool", tag="shared")
+        nc.sync.dma_start(v_pool[:].rearrange("p (u e) -> p u e", e=DV), v_words.rearrange("u g e r -> g u (e r)").bitcast(I32))
+
+        cols = PAGE // 16
+        p_tiles = []
+        k_gots = []
+
+        def gather_keys(pg):
+            k_got = ring.tile([P, PAGE], U32, name="k_got")
+            nc.vector.tensor_copy(k_got[:], k_pool[:].bitcast(U32).indirect(offs_sb[:, pg * cols : (pg + 1) * cols]))
+            k_gots.append(k_got)
+
+        gather_keys(0)
+        for pg in range(PAGES):
+            if pg + 1 < PAGES:
+                gather_keys(pg + 1)
+            k_got = k_gots[pg]
+            k_codes = ring.tile([P, PASSES, 2 * PAGE], U8, name="k_codes", align_bytes=64)
+            nc.vector.tensor_copy(k_codes[:].bitcast(U16), k_got[:].bitcast(U16).rearrange("p (n o) -> p o n", o=PASSES))
+            scores = psum.tile([P, PAGE], F32, name="scores", bufs=2)
+            for o in range(PASSES):
+                nc.tensor.matmul_mx(
+                    out=scores[:],
+                    lhsT=q_codes[:, o, :].bitcast(FP8X4),
+                    lhsT_scale=q_sc[:, o * NQ : (o + 1) * NQ],
+                    rhs=k_codes[:, o, :].bitcast(FP4X4),
+                    rhs_scale=ks_got[o][:, pg * PAGE : (pg + 1) * PAGE],
+                    start=(o == 0),
+                    stop=(o == PASSES - 1),
+                )
+            p_sb = ring.tile([P, PAGE], F32, name="p_sb")
+            nc.scalar.activation(p_sb[:], scores[:], ACT.Silu)
+            p_tiles.append(p_sb)
+
+        w_grouped = []
+        for pg in range(PAGES):
+            w_f32 = ring.tile([P, PAGE], F32, name="w_f32")
+            nc.vector.tensor_tensor(w_f32[:], vs_pool[:].indirect(offs_sb[:, pg * cols : (pg + 1) * cols]), p_tiles[pg][:], MULT)
+            w_bf = ring.tile([P, 2, P, 2], BF16, name="w_bf")
+            nc.scalar.activation(w_bf[:], w_f32[:].rearrange("p (s u e) -> p u s e", u=2, e=2), ACT.Copy)
+            turned = psum.tile([P, 2, NQ], F32, name="turned", bufs=2)
+            for u in range(2):
+                nc.tensor.transpose(turned[:, u, :], w_bf[:, u].rearrange("p s e -> p (s e)").bitcast(F32), ident[:])
+            grouped = ring.tile([P, NQ * 4], BF16, name="grouped", align_bytes=64)
+            nc.scalar.copy(grouped[:].bitcast(F32).rearrange("p (q u) -> p q u", u=2), turned[:].rearrange("p u q -> p q u"))
+            w_grouped.append(grouped)
+
+        vsc_got = keep.tile([P, PAGES * DV], U8, name="vsc_got", align_bytes=64)
+        nc.vector.tensor_copy(vsc_got[:], vsc_pool[:].indirect(voffs_sb[:]))
+        v_got = keep.tile([P, PAGES * DV], U32, name="v_got", align_bytes=64)
+        nc.vector.tensor_copy(v_got[:], v_pool[:].bitcast(U32).indirect(voffs_sb[:]))
+
+        acc = psum.tile([P, DV], F32, name="acc")
+        for pg in range(PAGES):
+            w_codes = ring.tile([P, NQ], U32, name="w_codes", align_bytes=64)
+            w_sc = ring.tile([P, NQ], U8, name="w_sc", align_bytes=64)
+            nc.vector.quantize_mx(out=w_codes[:].bitcast(FP8X4), scales=w_sc[:], in_=w_grouped[pg][:])
+            nc.tensor.matmul_mx(
+                out=acc[:],
+                lhsT=w_codes[:].bitcast(FP8X4),
+                lhsT_scale=w_sc[:],
+                rhs=v_got[:, pg * DV : (pg + 1) * DV].bitcast(FP8X4),
+                rhs_scale=vsc_got[:, pg * DV : (pg + 1) * DV],
+                start=(pg == 0),
+                stop=(pg == PAGES - 1),
+            )
+        result = keep.tile([P, DV], F32, name="result")
+        nc.scalar.activation(result[:], acc[:], ACT.Copy, scale=1.0 / 16.0)
+        nc.sync.dma_start(out[0], result[:])

@@ -27,6 +27,7 @@ def tile_attend_pkv4q_silu_kernel(tc, q_words, q_scales, k_words, k_scales, v_wo
     nc = tc.nc
     with ExitStack() as ctx:
         keep = ctx.enter_context(tc.tile_pool(name="keep", bufs=1))
+        reuse = ctx.enter_context(tc.tile_pool(name="reuse", bufs=1))
         ring = ctx.enter_context(tc.tile_pool(name="ring", bufs=3))
         psum = ctx.enter_context(tc.psum_pool(name="psum", bufs=1))
 
@@ -34,39 +35,41 @@ def tile_attend_pkv4q_silu_kernel(tc, q_words, q_scales, k_words, k_scales, v_wo
         voffs_sb = keep.tile([P, PAGES * DV // 16], U16, name="voffs_sb")
         vs_rows = keep.tile([P, T // P], F32, name="vs_rows")
         k_pool = keep.tile([P, T], I32, name="k_pool")
-        ks_pool = keep.tile([P, T], U8, name="ks_pool", tag="shared")
-        ks_low = keep.tile([P, N], U8, name="ks_low", align_bytes=64)
-        vsc_pool = keep.tile([P, POOL_PAGES * DV], U8, name="vsc_pool")
+        ks_pool = keep.tile([P, T], U8, name="ks_pool")
+        vsc_pool = reuse.tile([P, POOL_PAGES * DV], U8, name="vsc_pool", tag="pool")
+        vsc_plane = keep.tile([P, PAGES * DV], U8, name="vsc_plane", align_bytes=64)
+        ks_planes = keep.tile([P, PASSES, N], U8, name="ks_planes", align_bytes=64)
         vs_pool = keep.tile([P, T], F32, name="vs_pool")
         q_codes = keep.tile([P, PASSES, NQ], I32, name="q_codes", align_bytes=64)
         q_sc = keep.tile([P, PASSES * NQ], U8, name="q_sc", align_bytes=64)
         ident = keep.tile([P, P], F32, name="ident")
         warm = keep.tile([P, 1], F32, name="warm")
 
-        nc.vector.memset(ks_pool[:].bitcast(I32), 0)
         nc.vector.memset(q_sc[:].bitcast(I32), 0)
-        nc.vector.memset(vsc_pool[:].bitcast(I32), 0)
-        nc.vector.memset(ks_low[:].bitcast(I32), 0)
+        nc.vector.memset(ks_pool[32:64, :].bitcast(I32), 0)
+        nc.vector.memset(ks_pool[64:128, :].bitcast(I32), 0)
+        nc.vector.memset(vsc_pool[32:64, :].bitcast(I32), 0)
+        nc.vector.memset(vsc_pool[64:128, :].bitcast(I32), 0)
         make_identity(nc, ident[:])
+        nc.gpsimd.memset(ks_planes[:].bitcast(I32), 0)
+        nc.gpsimd.memset(vsc_plane[:].bitcast(I32), 0)
 
         nc.sync.dma_start(offs_sb[:], offs)
+        nc.sync.dma_start(ks_pool[0:32, :].bitcast(I32), k_scales.bitcast(I32).rearrange("o f t -> (o f) t"))
         nc.sync.dma_start(vs_rows[:], vs[0].rearrange("(p c) -> p c", p=P))
-        nc.sync.dma_start(k_pool[:], k_words[0].rearrange("g t b -> g (t b)").bitcast(I32))
         nc.sync.dma_start(voffs_sb[:], voffs)
-        ks_rows = k_scales.bitcast(I32).rearrange("o (quad j) t -> j quad o t", j=4)
-        for j in range(4):
-            nc.scalar.dma_start(ks_pool[j:P:16, :].bitcast(I32), ks_rows[j])
+        for half in range(2):
+            nc.sync.dma_start(
+                vsc_pool[16 * half : 16 * half + 16, :].bitcast(I32).rearrange("f (u e) -> f u e", u=POOL_PAGES),
+                v_scales.bitcast(I32).rearrange("u f e -> f u e"),
+            )
+        nc.sync.dma_start(k_pool[:], k_words[0].rearrange("g t b -> g (t b)").bitcast(I32))
+        nc.sync.dma_start(q_codes[:], q_words[0].rearrange("o g q r -> g o (q r)").bitcast(I32))
         nc.scalar.activation(warm[:], ident[:, 0:1], ACT.Silu)
-        nc.gpsimd.dma_start(q_codes[:], q_words[0].rearrange("o g q r -> g o (q r)").bitcast(I32))
         for quad in range(4):
             nc.gpsimd.dma_start(
                 q_sc[32 * quad : 32 * quad + 4, :].bitcast(I32).rearrange("f (o q) -> f o q", o=PASSES),
                 q_scales[0, :, 4 * quad : 4 * quad + 4, :].bitcast(I32).rearrange("o f q -> f o q"),
-            )
-        for quad in range(4):
-            nc.gpsimd.dma_start(
-                vsc_pool[32 * quad : 32 * quad + 4, :].bitcast(I32).rearrange("f (u e) -> f u e", u=POOL_PAGES),
-                v_scales[:, 4 * quad : 4 * quad + 4, :].bitcast(I32).rearrange("u f e -> f u e"),
             )
 
         per_row = T // P
@@ -80,9 +83,15 @@ def tile_attend_pkv4q_silu_kernel(tc, q_words, q_scales, k_words, k_scales, v_wo
 
         ks_both = keep.tile([P, N], U8, name="ks_both", align_bytes=64)
         nc.vector.tensor_copy(ks_both[:], ks_pool[:].indirect(offs_sb[:]))
-        nc.sync.dma_start(ks_low[0 : P - 16, :].bitcast(I32), ks_both[16:P, :].bitcast(I32))
-        ks_got = [ks_both, ks_low]
-        v_pool = keep.tile([P, POOL_PAGES * DV], I32, name="v_pool", tag="shared")
+        for quad in range(4):
+            for o in range(PASSES):
+                row = 16 * o + 4 * quad
+                nc.sync.dma_start(ks_planes[32 * quad : 32 * quad + 4, o, :].bitcast(I32), ks_both[row : row + 4, :].bitcast(I32))
+        vsc_got = keep.tile([P, PAGES * DV], U8, name="vsc_got", align_bytes=64)
+        nc.vector.tensor_copy(vsc_got[:], vsc_pool[:].indirect(voffs_sb[:]))
+        for quad in range(4):
+            nc.sync.dma_start(vsc_plane[32 * quad : 32 * quad + 4, :].bitcast(I32), vsc_got[4 * quad : 4 * quad + 4, :].bitcast(I32))
+        v_pool = reuse.tile([P, POOL_PAGES * DV], I32, name="v_pool", tag="pool")
         nc.sync.dma_start(v_pool[:].rearrange("p (u e) -> p u e", e=DV), v_words.rearrange("u g e r -> g u (e r)").bitcast(I32))
 
         cols = PAGE // 16
@@ -94,25 +103,31 @@ def tile_attend_pkv4q_silu_kernel(tc, q_words, q_scales, k_words, k_scales, v_wo
             nc.vector.tensor_copy(k_got[:], k_pool[:].bitcast(U32).indirect(offs_sb[:, pg * cols : (pg + 1) * cols]))
             k_gots.append(k_got)
 
-        gather_keys(0)
         for pg in range(PAGES):
-            if pg + 1 < PAGES:
-                gather_keys(pg + 1)
+            if pg < 2:
+                gather_keys(pg)
+            if pg == 1:
+                gather_keys(2)
             k_got = k_gots[pg]
-            k_codes = ring.tile([P, PASSES, 2 * PAGE], U8, name="k_codes", align_bytes=64)
-            nc.vector.tensor_copy(k_codes[:].bitcast(U16), k_got[:].bitcast(U16).rearrange("p (n o) -> p o n", o=PASSES))
+            halves = k_got[:].bitcast(U16).rearrange("p (n o) -> p o n", o=PASSES)
+            k_codes = []
+            for o in range(PASSES):
+                slot = "k_codes_%d_%d" % (pg // 2 if o == 0 else pg, o)
+                codes = keep.tile([P, 2 * PAGE], U8, name="codes", tag=slot, align_bytes=64)
+                nc.vector.tensor_copy(codes[:].bitcast(U16), halves[:, o, :])
+                k_codes.append(codes)
             scores = psum.tile([P, PAGE], F32, name="scores", bufs=2)
             for o in range(PASSES):
                 nc.tensor.matmul_mx(
                     out=scores[:],
                     lhsT=q_codes[:, o, :].bitcast(FP8X4),
                     lhsT_scale=q_sc[:, o * NQ : (o + 1) * NQ],
-                    rhs=k_codes[:, o, :].bitcast(FP4X4),
-                    rhs_scale=ks_got[o][:, pg * PAGE : (pg + 1) * PAGE],
+                    rhs=k_codes[o][:].bitcast(FP4X4),
+                    rhs_scale=ks_planes[:, o, pg * PAGE : (pg + 1) * PAGE],
                     start=(o == 0),
                     stop=(o == PASSES - 1),
                 )
-            p_sb = ring.tile([P, PAGE], F32, name="p_sb")
+            p_sb = ring.tile([P, PAGE], F32, name="p_sb", tag="late", align_bytes=64)
             nc.scalar.activation(p_sb[:], scores[:], ACT.Silu)
             p_tiles.append(p_sb)
 
@@ -129,12 +144,14 @@ def tile_attend_pkv4q_silu_kernel(tc, q_words, q_scales, k_words, k_scales, v_wo
             nc.scalar.copy(grouped[:].bitcast(F32).rearrange("p (q u) -> p q u", u=2), turned[:].rearrange("p u q -> p q u"))
             w_grouped.append(grouped)
 
-        vsc_got = keep.tile([P, PAGES * DV], U8, name="vsc_got", align_bytes=64)
-        nc.vector.tensor_copy(vsc_got[:], vsc_pool[:].indirect(voffs_sb[:]))
-        v_got = keep.tile([P, PAGES * DV], U32, name="v_got", align_bytes=64)
-        nc.vector.tensor_copy(v_got[:], v_pool[:].bitcast(U32).indirect(voffs_sb[:]))
+        vcols = DV // 16
+        v_gots = []
+        for pg in range(PAGES):
+            v_got = ring.tile([P, DV], U32, name="v_got", tag="late", align_bytes=64)
+            nc.vector.tensor_copy(v_got[:], v_pool[:].bitcast(U32).indirect(voffs_sb[:, pg * vcols : (pg + 1) * vcols]))
+            v_gots.append(v_got)
 
-        acc = psum.tile([P, DV], F32, name="acc")
+        acc = psum.tile([P, DV], F32, name="acc", tag="turned", bufs=2)
         for pg in range(PAGES):
             w_codes = ring.tile([P, NQ], U32, name="w_codes", align_bytes=64)
             w_sc = ring.tile([P, NQ], U8, name="w_sc", align_bytes=64)
@@ -143,8 +160,8 @@ def tile_attend_pkv4q_silu_kernel(tc, q_words, q_scales, k_words, k_scales, v_wo
                 out=acc[:],
                 lhsT=w_codes[:].bitcast(FP8X4),
                 lhsT_scale=w_sc[:],
-                rhs=v_got[:, pg * DV : (pg + 1) * DV].bitcast(FP8X4),
-                rhs_scale=vsc_got[:, pg * DV : (pg + 1) * DV],
+                rhs=v_gots[pg][:].bitcast(FP8X4),
+                rhs_scale=vsc_plane[:, pg * DV : (pg + 1) * DV],
                 start=(pg == 0),
                 stop=(pg == PAGES - 1),
             )

@@ -4,11 +4,17 @@ import concourse.mybir as mybir
 from concourse.masks import make_identity
 
 NQ, N, T, D, DV = 128, 1536, 4096, 1024, 256
+P = 128
 PAGE = 512
 PAGES = N // PAGE
 POOL_PAGES = T // PAGE
 PASSES = D // 512
-P = 128
+QUADS = 4
+BLOCKS = 16
+LIST_ROWS = 16
+BANK_TURNS = 4
+OUT_SCALE = 1.0 / 16.0
+CODE_PLACES = ((1, 4), (0, 2))
 FLOPS = 2 * NQ * N * (D + DV)
 
 F32 = mybir.dt.float32
@@ -25,117 +31,120 @@ MULT = mybir.AluOpType.mult
 
 def tile_attend_pkv4q_silu_kernel(tc, q_words, q_scales, k_words, k_scales, v_words, v_scales, vs, offs, voffs, out):
     nc = tc.nc
+    last = PAGES - 1
     with ExitStack() as ctx:
         keep = ctx.enter_context(tc.tile_pool(name="keep", bufs=1))
         reuse = ctx.enter_context(tc.tile_pool(name="reuse", bufs=1))
-        ring = ctx.enter_context(tc.tile_pool(name="ring", bufs=3))
+        split = ctx.enter_context(tc.tile_pool(name="split", bufs=1))
+        ring = ctx.enter_context(tc.tile_pool(name="ring", bufs=PAGES))
         psum = ctx.enter_context(tc.psum_pool(name="psum", bufs=1))
 
-        offs_sb = keep.tile([P, N // 16], U16, name="offs_sb")
-        voffs_sb = keep.tile([P, PAGES * DV // 16], U16, name="voffs_sb")
+        offs_sb = keep.tile([P, N // LIST_ROWS], U16, name="offs_sb")
+        voffs_sb = keep.tile([P, PAGES * DV // LIST_ROWS], U16, name="voffs_sb")
         vs_rows = keep.tile([P, T // P], F32, name="vs_rows")
         k_pool = keep.tile([P, T], I32, name="k_pool")
         ks_pool = keep.tile([P, T], U8, name="ks_pool")
-        vsc_pool = reuse.tile([P, POOL_PAGES * DV], U8, name="vsc_pool", tag="pool")
+        vsc_pool = reuse.tile([P, POOL_PAGES * DV], U8, name="vsc_pool", tag="value_pool")
         vsc_plane = keep.tile([P, PAGES * DV], U8, name="vsc_plane", align_bytes=64)
         ks_planes = keep.tile([P, PASSES, N], U8, name="ks_planes", align_bytes=64)
         vs_pool = keep.tile([P, T], F32, name="vs_pool")
         q_codes = keep.tile([P, PASSES, NQ], I32, name="q_codes", align_bytes=64)
-        q_sc = keep.tile([P, PASSES * NQ], U8, name="q_sc", align_bytes=64)
+        q_planes = keep.tile([P, PASSES * NQ], U8, name="q_planes", align_bytes=64)
         ident = keep.tile([P, P], F32, name="ident")
-        warm = keep.tile([P, 1], F32, name="warm")
 
-        nc.vector.memset(q_sc[:].bitcast(I32), 0)
-        nc.vector.memset(ks_pool[32:64, :].bitcast(I32), 0)
+        nc.vector.memset(q_planes[:].bitcast(I32), 0)
         nc.vector.memset(ks_pool[64:128, :].bitcast(I32), 0)
         nc.vector.memset(vsc_pool[32:64, :].bitcast(I32), 0)
         nc.vector.memset(vsc_pool[64:128, :].bitcast(I32), 0)
+        nc.gpsimd.memset(ks_pool[32:64, :].bitcast(I32), 0)
         make_identity(nc, ident[:])
         nc.gpsimd.memset(ks_planes[:].bitcast(I32), 0)
-        nc.gpsimd.memset(vsc_plane[:].bitcast(I32), 0)
 
         nc.sync.dma_start(offs_sb[:], offs)
         nc.sync.dma_start(ks_pool[0:32, :].bitcast(I32), k_scales.bitcast(I32).rearrange("o f t -> (o f) t"))
         nc.sync.dma_start(vs_rows[:], vs[0].rearrange("(p c) -> p c", p=P))
         nc.sync.dma_start(voffs_sb[:], voffs)
-        for half in range(2):
+        for copy in range(2):
             nc.sync.dma_start(
-                vsc_pool[16 * half : 16 * half + 16, :].bitcast(I32).rearrange("f (u e) -> f u e", u=POOL_PAGES),
+                vsc_pool[BLOCKS * copy : BLOCKS * (copy + 1), :].bitcast(I32).rearrange("f (u e) -> f u e", u=POOL_PAGES),
                 v_scales.bitcast(I32).rearrange("u f e -> f u e"),
             )
         nc.sync.dma_start(k_pool[:], k_words[0].rearrange("g t b -> g (t b)").bitcast(I32))
         nc.sync.dma_start(q_codes[:], q_words[0].rearrange("o g q r -> g o (q r)").bitcast(I32))
-        nc.scalar.activation(warm[:], ident[:, 0:1], ACT.Silu)
-        for quad in range(4):
+        for quad in range(QUADS):
             nc.gpsimd.dma_start(
-                q_sc[32 * quad : 32 * quad + 4, :].bitcast(I32).rearrange("f (o q) -> f o q", o=PASSES),
+                q_planes[32 * quad : 32 * quad + 4, :].bitcast(I32).rearrange("f (o q) -> f o q", o=PASSES),
                 q_scales[0, :, 4 * quad : 4 * quad + 4, :].bitcast(I32).rearrange("o f q -> f o q"),
             )
 
-        per_row = T // P
-        vs_view = vs_pool[:].rearrange("p (n b m) -> p b n m", b=per_row // 4, m=4)
-        for b in range(per_row // 4):
-            spread = psum.tile([P, 4, P], F32, name="spread", bufs=3)
-            for m in range(4):
-                c = 4 * b + m
+        vs_by_bank = vs_pool[:].rearrange("p (n b m) -> p b n m", b=T // P // BANK_TURNS, m=BANK_TURNS)
+        for bank in range(T // P // BANK_TURNS):
+            spread = psum.tile([P, BANK_TURNS, P], F32, name="spread", bufs=3)
+            for m in range(BANK_TURNS):
+                c = BANK_TURNS * bank + m
                 nc.tensor.transpose(spread[:, m, :], vs_rows[:, c : c + 1].to_broadcast([P, P]), ident[:])
-            nc.scalar.activation(vs_view[:, b], spread[:].rearrange("p m n -> p n m"), ACT.Copy)
+            nc.scalar.activation(vs_by_bank[:, bank], spread[:].rearrange("p m n -> p n m"), ACT.Copy)
 
-        ks_both = keep.tile([P, N], U8, name="ks_both", align_bytes=64)
-        nc.vector.tensor_copy(ks_both[:], ks_pool[:].indirect(offs_sb[:]))
-        for quad in range(4):
+        ks_got = keep.tile([P, N], U8, name="ks_got", align_bytes=64)
+        nc.vector.tensor_copy(ks_got[:], ks_pool[:].indirect(offs_sb[:]))
+        for quad in range(QUADS):
             for o in range(PASSES):
-                row = 16 * o + 4 * quad
-                nc.sync.dma_start(ks_planes[32 * quad : 32 * quad + 4, o, :].bitcast(I32), ks_both[row : row + 4, :].bitcast(I32))
+                row = BLOCKS * o + 4 * quad
+                nc.sync.dma_start(ks_planes[32 * quad : 32 * quad + 4, o, :].bitcast(I32), ks_got[row : row + 4, :].bitcast(I32))
         vsc_got = keep.tile([P, PAGES * DV], U8, name="vsc_got", align_bytes=64)
         nc.vector.tensor_copy(vsc_got[:], vsc_pool[:].indirect(voffs_sb[:]))
-        for quad in range(4):
-            nc.sync.dma_start(vsc_plane[32 * quad : 32 * quad + 4, :].bitcast(I32), vsc_got[4 * quad : 4 * quad + 4, :].bitcast(I32))
-        v_pool = reuse.tile([P, POOL_PAGES * DV], I32, name="v_pool", tag="pool")
+        for quad in range(QUADS):
+            nc.sync.dma_start(vsc_plane[32 * quad : 32 * quad + 32, :].bitcast(I32), vsc_got[4 * quad : 4 * quad + 32, :].bitcast(I32))
+        v_pool = reuse.tile([P, POOL_PAGES * DV], I32, name="v_pool", tag="value_pool")
         nc.sync.dma_start(v_pool[:].rearrange("p (u e) -> p u e", e=DV), v_words.rearrange("u g e r -> g u (e r)").bitcast(I32))
 
-        cols = PAGE // 16
-        p_tiles = []
-        k_gots = []
+        def page_of(list_sb, pg):
+            width = list_sb.shape[1] // PAGES
+            return list_sb[:, pg * width : (pg + 1) * width]
 
         def gather_keys(pg):
-            k_got = ring.tile([P, PAGE], U32, name="k_got")
-            nc.vector.tensor_copy(k_got[:], k_pool[:].bitcast(U32).indirect(offs_sb[:, pg * cols : (pg + 1) * cols]))
-            k_gots.append(k_got)
+            k_got = keep.tile([P, PAGE], U32, name="k_got", tag="k_got%d" % pg, align_bytes=64)
+            nc.vector.tensor_copy(k_got[:], k_pool[:].bitcast(U32).indirect(page_of(offs_sb, pg)))
+            return k_got
 
+        k_gots = []
+        p_tiles = []
         for pg in range(PAGES):
-            if pg < 2:
-                gather_keys(pg)
-            if pg == 1:
-                gather_keys(2)
-            k_got = k_gots[pg]
-            halves = k_got[:].bitcast(U16).rearrange("p (n o) -> p o n", o=PASSES)
-            k_codes = []
-            for o in range(PASSES):
-                slot = "k_codes_%d_%d" % (pg // 2 if o == 0 else pg, o)
-                codes = keep.tile([P, 2 * PAGE], U8, name="codes", tag=slot, align_bytes=64)
-                nc.vector.tensor_copy(codes[:].bitcast(U16), halves[:, o, :])
-                k_codes.append(codes)
+            if pg < last:
+                k_gots.append(gather_keys(pg))
+            if pg == last - 1:
+                k_gots.append(gather_keys(last))
+            by_pass = k_gots[pg][:].bitcast(U16).rearrange("p (n o) -> p o n", o=PASSES)
+            if pg == last:
+                both = keep.tile([P, PASSES, 2 * PAGE], U8, name="both", tag="k_got%d" % (last - 1), align_bytes=64)
+                nc.vector.tensor_copy(both[:].bitcast(U16), by_pass)
+                k_codes = [both[:, o, :] for o in range(PASSES)]
+            else:
+                k_codes = []
+                for o in range(PASSES):
+                    codes = split.tile([P, 2 * PAGE], U8, name="codes%d%d" % (pg, o), offset=PAGE * CODE_PLACES[pg][o], align_bytes=64)
+                    nc.vector.tensor_copy(codes[:].bitcast(U16), by_pass[:, o, :])
+                    k_codes.append(codes[:])
             scores = psum.tile([P, PAGE], F32, name="scores", bufs=2)
             for o in range(PASSES):
                 nc.tensor.matmul_mx(
                     out=scores[:],
                     lhsT=q_codes[:, o, :].bitcast(FP8X4),
-                    lhsT_scale=q_sc[:, o * NQ : (o + 1) * NQ],
-                    rhs=k_codes[o][:].bitcast(FP4X4),
+                    lhsT_scale=q_planes[:, o * NQ : (o + 1) * NQ],
+                    rhs=k_codes[o].bitcast(FP4X4),
                     rhs_scale=ks_planes[:, o, pg * PAGE : (pg + 1) * PAGE],
                     start=(o == 0),
                     stop=(o == PASSES - 1),
                 )
-            p_sb = ring.tile([P, PAGE], F32, name="p_sb", tag="late", align_bytes=64)
+            p_sb = keep.tile([P, PAGE], F32, name="p_sb", tag="p%d" % pg, align_bytes=64)
             nc.scalar.activation(p_sb[:], scores[:], ACT.Silu)
             p_tiles.append(p_sb)
 
         w_grouped = []
         for pg in range(PAGES):
             w_f32 = ring.tile([P, PAGE], F32, name="w_f32")
-            nc.vector.tensor_tensor(w_f32[:], vs_pool[:].indirect(offs_sb[:, pg * cols : (pg + 1) * cols]), p_tiles[pg][:], MULT)
-            w_bf = ring.tile([P, 2, P, 2], BF16, name="w_bf")
+            nc.vector.tensor_tensor(w_f32[:], vs_pool[:].indirect(page_of(offs_sb, pg)), p_tiles[pg][:], MULT)
+            w_bf = keep.tile([P, 2, P, 2], BF16, name="w_bf", tag="w_bf%d" % pg, align_bytes=64)
             nc.scalar.activation(w_bf[:], w_f32[:].rearrange("p (s u e) -> p u s e", u=2, e=2), ACT.Copy)
             turned = psum.tile([P, 2, NQ], F32, name="turned", bufs=2)
             for u in range(2):
@@ -144,27 +153,22 @@ def tile_attend_pkv4q_silu_kernel(tc, q_words, q_scales, k_words, k_scales, v_wo
             nc.scalar.copy(grouped[:].bitcast(F32).rearrange("p (q u) -> p q u", u=2), turned[:].rearrange("p u q -> p q u"))
             w_grouped.append(grouped)
 
-        vcols = DV // 16
-        v_gots = []
+        v_got = keep.tile([P, PAGES, DV], U32, name="v_got", tag="p%d" % last, align_bytes=64)
+        acc = psum.tile([P, DV], F32, name="acc")
         for pg in range(PAGES):
-            v_got = ring.tile([P, DV], U32, name="v_got", tag="late", align_bytes=64)
-            nc.vector.tensor_copy(v_got[:], v_pool[:].bitcast(U32).indirect(voffs_sb[:, pg * vcols : (pg + 1) * vcols]))
-            v_gots.append(v_got)
-
-        acc = psum.tile([P, DV], F32, name="acc", tag="turned", bufs=2)
-        for pg in range(PAGES):
-            w_codes = ring.tile([P, NQ], U32, name="w_codes", align_bytes=64)
-            w_sc = ring.tile([P, NQ], U8, name="w_sc", align_bytes=64)
-            nc.vector.quantize_mx(out=w_codes[:].bitcast(FP8X4), scales=w_sc[:], in_=w_grouped[pg][:])
+            nc.vector.tensor_copy(v_got[:, pg, :], v_pool[:].bitcast(U32).indirect(page_of(voffs_sb, pg)))
+            w_codes = keep.tile([P, NQ], U32, name="w_codes", tag="w_bf%d" % ((pg + 1) % PAGES), align_bytes=64)
+            w_plane = ring.tile([P, NQ], U8, name="w_plane", align_bytes=64)
+            nc.vector.quantize_mx(out=w_codes[:].bitcast(FP8X4), scales=w_plane[:], in_=w_grouped[pg][:])
             nc.tensor.matmul_mx(
                 out=acc[:],
                 lhsT=w_codes[:].bitcast(FP8X4),
-                lhsT_scale=w_sc[:],
-                rhs=v_gots[pg][:].bitcast(FP8X4),
+                lhsT_scale=w_plane[:],
+                rhs=v_got[:, pg, :].bitcast(FP8X4),
                 rhs_scale=vsc_plane[:, pg * DV : (pg + 1) * DV],
                 start=(pg == 0),
-                stop=(pg == PAGES - 1),
+                stop=(pg == last),
             )
         result = keep.tile([P, DV], F32, name="result")
-        nc.scalar.activation(result[:], acc[:], ACT.Copy, scale=1.0 / 16.0)
+        nc.scalar.activation(result[:], acc[:], ACT.Copy, scale=OUT_SCALE)
         nc.sync.dma_start(out[0], result[:])

@@ -13,8 +13,8 @@ QUADS = 4
 BLOCKS = 16
 LIST_ROWS = 16
 BANK_TURNS = 4
+TOP = 96
 OUT_SCALE = 1.0 / 16.0
-CODE_PLACES = ((1, 4), (0, 2))
 FLOPS = 2 * NQ * N * (D + DV)
 
 F32 = mybir.dt.float32
@@ -34,9 +34,7 @@ def tile_attend_pkv4q_silu_kernel(tc, q_words, q_scales, k_words, k_scales, v_wo
     last = PAGES - 1
     with ExitStack() as ctx:
         keep = ctx.enter_context(tc.tile_pool(name="keep", bufs=1))
-        reuse = ctx.enter_context(tc.tile_pool(name="reuse", bufs=1))
-        split = ctx.enter_context(tc.tile_pool(name="split", bufs=1))
-        ring = ctx.enter_context(tc.tile_pool(name="ring", bufs=PAGES))
+        late = ctx.enter_context(tc.tile_pool(name="late", bufs=1))
         psum = ctx.enter_context(tc.psum_pool(name="psum", bufs=1))
 
         offs_sb = keep.tile([P, N // LIST_ROWS], U16, name="offs_sb")
@@ -44,33 +42,24 @@ def tile_attend_pkv4q_silu_kernel(tc, q_words, q_scales, k_words, k_scales, v_wo
         vs_rows = keep.tile([P, T // P], F32, name="vs_rows")
         k_pool = keep.tile([P, T], I32, name="k_pool")
         ks_pool = keep.tile([P, T], U8, name="ks_pool")
-        vsc_pool = reuse.tile([P, POOL_PAGES * DV], U8, name="vsc_pool", tag="value_pool")
-        vsc_plane = keep.tile([P, PAGES * DV], U8, name="vsc_plane", align_bytes=64)
+        vsc_pool = late.tile([P, POOL_PAGES * DV], U8, name="vsc_pool", offset=0, align_bytes=64)
         ks_planes = keep.tile([P, PASSES, N], U8, name="ks_planes", align_bytes=64)
-        vs_pool = keep.tile([P, T], F32, name="vs_pool")
+        vs_pool = keep.tile([P, T], F32, name="vs_pool", tag="vs_pool", align_bytes=64)
         q_codes = keep.tile([P, PASSES, NQ], I32, name="q_codes", align_bytes=64)
         q_planes = keep.tile([P, PASSES * NQ], U8, name="q_planes", align_bytes=64)
         ident = keep.tile([P, P], F32, name="ident")
 
         nc.vector.memset(q_planes[:].bitcast(I32), 0)
-        nc.vector.memset(ks_pool[64:128, :].bitcast(I32), 0)
-        nc.vector.memset(vsc_pool[32:64, :].bitcast(I32), 0)
-        nc.vector.memset(vsc_pool[64:128, :].bitcast(I32), 0)
-        nc.gpsimd.memset(ks_pool[32:64, :].bitcast(I32), 0)
+        nc.vector.memset(ks_pool[0:TOP, :].bitcast(I32), 0)
+        nc.vector.memset(ks_planes[:].bitcast(I32), 0)
         make_identity(nc, ident[:])
-        nc.gpsimd.memset(ks_planes[:].bitcast(I32), 0)
 
         nc.sync.dma_start(offs_sb[:], offs)
-        nc.sync.dma_start(ks_pool[0:32, :].bitcast(I32), k_scales.bitcast(I32).rearrange("o f t -> (o f) t"))
+        nc.sync.dma_start(ks_pool[TOP:P, :].bitcast(I32), k_scales.bitcast(I32).rearrange("o f t -> f o t"))
         nc.sync.dma_start(vs_rows[:], vs[0].rearrange("(p c) -> p c", p=P))
-        nc.sync.dma_start(voffs_sb[:], voffs)
-        for copy in range(2):
-            nc.sync.dma_start(
-                vsc_pool[BLOCKS * copy : BLOCKS * (copy + 1), :].bitcast(I32).rearrange("f (u e) -> f u e", u=POOL_PAGES),
-                v_scales.bitcast(I32).rearrange("u f e -> f u e"),
-            )
         nc.sync.dma_start(k_pool[:], k_words[0].rearrange("g t b -> g (t b)").bitcast(I32))
         nc.sync.dma_start(q_codes[:], q_words[0].rearrange("o g q r -> g o (q r)").bitcast(I32))
+        nc.sync.dma_start(voffs_sb[:], voffs)
         for quad in range(QUADS):
             nc.gpsimd.dma_start(
                 q_planes[32 * quad : 32 * quad + 4, :].bitcast(I32).rearrange("f (o q) -> f o q", o=PASSES),
@@ -85,53 +74,48 @@ def tile_attend_pkv4q_silu_kernel(tc, q_words, q_scales, k_words, k_scales, v_wo
                 nc.tensor.transpose(spread[:, m, :], vs_rows[:, c : c + 1].to_broadcast([P, P]), ident[:])
             nc.scalar.activation(vs_by_bank[:, bank], spread[:].rearrange("p m n -> p n m"), ACT.Copy)
 
-        ks_got = keep.tile([P, N], U8, name="ks_got", align_bytes=64)
+        ks_got = keep.tile([P, N], U8, name="ks_got", tag="ks_then_v", align_bytes=64)
         nc.vector.tensor_copy(ks_got[:], ks_pool[:].indirect(offs_sb[:]))
         for quad in range(QUADS):
-            for o in range(PASSES):
-                row = BLOCKS * o + 4 * quad
-                nc.sync.dma_start(ks_planes[32 * quad : 32 * quad + 4, o, :].bitcast(I32), ks_got[row : row + 4, :].bitcast(I32))
-        vsc_got = keep.tile([P, PAGES * DV], U8, name="vsc_got", align_bytes=64)
-        nc.vector.tensor_copy(vsc_got[:], vsc_pool[:].indirect(voffs_sb[:]))
-        for quad in range(QUADS):
-            nc.sync.dma_start(vsc_plane[32 * quad : 32 * quad + 32, :].bitcast(I32), vsc_got[4 * quad : 4 * quad + 32, :].bitcast(I32))
-        v_pool = reuse.tile([P, POOL_PAGES * DV], I32, name="v_pool", tag="value_pool")
+            nc.sync.dma_start(ks_planes[32 * quad : 32 * quad + 4].bitcast(I32), ks_got[TOP + 8 * quad : TOP + 8 * quad + 8, :].bitcast(I32))
+        v_pool = keep.tile([P, POOL_PAGES * DV], I32, name="v_pool", tag="ks_then_v", align_bytes=64)
         nc.sync.dma_start(v_pool[:].rearrange("p (u e) -> p u e", e=DV), v_words.rearrange("u g e r -> g u (e r)").bitcast(I32))
 
-        def page_of(list_sb, pg):
+        nc.gpsimd.memset(vsc_pool[:].bitcast(I32), 0)
+        for quad in range(QUADS):
+            nc.sync.dma_start(
+                vsc_pool[32 * quad : 32 * quad + 4, :].bitcast(I32).rearrange("f (u e) -> f u e", u=POOL_PAGES),
+                v_scales[:, 4 * quad : 4 * quad + 4, :].bitcast(I32).rearrange("u f e -> f u e"),
+            )
+
+        def page_of(list_sb, pg, count=1):
             width = list_sb.shape[1] // PAGES
-            return list_sb[:, pg * width : (pg + 1) * width]
+            return list_sb[:, pg * width : (pg + count) * width]
 
         def gather_keys(pg):
-            k_got = keep.tile([P, PAGE], U32, name="k_got", tag="k_got%d" % pg, align_bytes=64)
+            k_got = keep.tile([P, PAGE], U32, name="k_got", tag="k_got%d" % (pg % 2), align_bytes=64)
             nc.vector.tensor_copy(k_got[:], k_pool[:].bitcast(U32).indirect(page_of(offs_sb, pg)))
             return k_got
 
-        k_gots = []
         p_tiles = []
+        k_gots = [gather_keys(0), gather_keys(1)]
         for pg in range(PAGES):
-            if pg < last:
-                k_gots.append(gather_keys(pg))
-            if pg == last - 1:
-                k_gots.append(gather_keys(last))
-            by_pass = k_gots[pg][:].bitcast(U16).rearrange("p (n o) -> p o n", o=PASSES)
             if pg == last:
-                both = keep.tile([P, PASSES, 2 * PAGE], U8, name="both", tag="k_got%d" % (last - 1), align_bytes=64)
-                nc.vector.tensor_copy(both[:].bitcast(U16), by_pass)
-                k_codes = [both[:, o, :] for o in range(PASSES)]
-            else:
-                k_codes = []
+                k_gots.append(gather_keys(pg))
+            by_pass = k_gots[pg][:].bitcast(U16).rearrange("p (n o) -> p o n", o=PASSES)
+            k_codes = keep.tile([P, PASSES, 2 * PAGE], U8, name="k_codes", tag="k_codes%d" % pg, align_bytes=64)
+            if pg == 0:
                 for o in range(PASSES):
-                    codes = split.tile([P, 2 * PAGE], U8, name="codes%d%d" % (pg, o), offset=PAGE * CODE_PLACES[pg][o], align_bytes=64)
-                    nc.vector.tensor_copy(codes[:].bitcast(U16), by_pass[:, o, :])
-                    k_codes.append(codes[:])
+                    nc.vector.tensor_copy(k_codes[:, o, :].bitcast(U16), by_pass[:, o, :])
+            else:
+                nc.vector.tensor_copy(k_codes[:].bitcast(U16), by_pass)
             scores = psum.tile([P, PAGE], F32, name="scores", bufs=2)
             for o in range(PASSES):
                 nc.tensor.matmul_mx(
                     out=scores[:],
                     lhsT=q_codes[:, o, :].bitcast(FP8X4),
                     lhsT_scale=q_planes[:, o * NQ : (o + 1) * NQ],
-                    rhs=k_codes[o].bitcast(FP4X4),
+                    rhs=k_codes[:, o, :].bitcast(FP4X4),
                     rhs_scale=ks_planes[:, o, pg * PAGE : (pg + 1) * PAGE],
                     start=(o == 0),
                     stop=(o == PASSES - 1),
@@ -140,35 +124,56 @@ def tile_attend_pkv4q_silu_kernel(tc, q_words, q_scales, k_words, k_scales, v_wo
             nc.scalar.activation(p_sb[:], scores[:], ACT.Silu)
             p_tiles.append(p_sb)
 
-        w_grouped = []
+        grouped_head = keep.tile([P, last, NQ * 4], BF16, name="grouped_head", tag="grouped_head", align_bytes=64)
+        grouped_last = keep.tile([P, 1, NQ * 4], BF16, name="grouped_last", align_bytes=64)
+        v_gots = []
+
+        def gather_values(pg, tag):
+            if tag:
+                v_got = keep.tile([P, DV], U32, name="v_got", tag=tag, align_bytes=64)
+            else:
+                v_got = late.tile([P, DV], U32, name="v_got1", offset=0, align_bytes=64)
+            nc.vector.tensor_copy(v_got[:], v_pool[:].bitcast(U32).indirect(page_of(voffs_sb, pg)))
+            v_gots.append(v_got)
+
         for pg in range(PAGES):
-            w_f32 = ring.tile([P, PAGE], F32, name="w_f32")
+            if pg == last:
+                gather_values(0, "p%d" % (last - 1))
+            w_f32 = keep.tile([P, PAGE], F32, name="w_f32_%d" % pg)
             nc.vector.tensor_tensor(w_f32[:], vs_pool[:].indirect(page_of(offs_sb, pg)), p_tiles[pg][:], MULT)
-            w_bf = keep.tile([P, 2, P, 2], BF16, name="w_bf", tag="w_bf%d" % pg, align_bytes=64)
+            if pg == last:
+                w_bf = late.tile([P, 2, P, 2], BF16, name="w_bf_last", offset=2048, align_bytes=64)
+            else:
+                w_bf = keep.tile([P, 2, P, 2], BF16, name="w_bf", tag="w_bf%d" % pg if pg else "k_codes%d" % last, align_bytes=64)
             nc.scalar.activation(w_bf[:], w_f32[:].rearrange("p (s u e) -> p u s e", u=2, e=2), ACT.Copy)
             turned = psum.tile([P, 2, NQ], F32, name="turned", bufs=2)
             for u in range(2):
                 nc.tensor.transpose(turned[:, u, :], w_bf[:, u].rearrange("p s e -> p (s e)").bitcast(F32), ident[:])
-            grouped = ring.tile([P, NQ * 4], BF16, name="grouped", align_bytes=64)
-            nc.scalar.copy(grouped[:].bitcast(F32).rearrange("p (q u) -> p q u", u=2), turned[:].rearrange("p u q -> p q u"))
-            w_grouped.append(grouped)
+            grouped = grouped_head[:, pg, :] if pg < last else grouped_last[:, 0, :]
+            nc.scalar.copy(grouped.bitcast(F32).rearrange("p (q u) -> p q u", u=2), turned[:].rearrange("p u q -> p q u"))
 
-        v_got = keep.tile([P, PAGES, DV], U32, name="v_got", tag="p%d" % last, align_bytes=64)
         acc = psum.tile([P, DV], F32, name="acc")
-        for pg in range(PAGES):
-            nc.vector.tensor_copy(v_got[:, pg, :], v_pool[:].bitcast(U32).indirect(page_of(voffs_sb, pg)))
-            w_codes = keep.tile([P, NQ], U32, name="w_codes", tag="w_bf%d" % ((pg + 1) % PAGES), align_bytes=64)
-            w_plane = ring.tile([P, NQ], U8, name="w_plane", align_bytes=64)
-            nc.vector.quantize_mx(out=w_codes[:].bitcast(FP8X4), scales=w_plane[:], in_=w_grouped[pg][:])
-            nc.tensor.matmul_mx(
-                out=acc[:],
-                lhsT=w_codes[:].bitcast(FP8X4),
-                lhsT_scale=w_plane[:],
-                rhs=v_got[:, pg, :].bitcast(FP8X4),
-                rhs_scale=vsc_plane[:, pg * DV : (pg + 1) * DV],
-                start=(pg == 0),
-                stop=(pg == last),
-            )
+        vsc_plane = keep.tile([P, PAGES * DV], U8, name="vsc_plane", tag="p%d" % last, align_bytes=64)
+        nc.vector.tensor_copy(vsc_plane[:], vsc_pool[:].indirect(voffs_sb[:]))
+        for first, count, grouped, v_tag, w_tag in ((0, last, grouped_head, None, None), (last, 1, grouped_last, "grouped_head", "ks_then_v")):
+            gather_values(first + count - 1, v_tag)
+            if w_tag:
+                w_codes = keep.tile([P, count * NQ], U32, name="w_codes", tag=w_tag, align_bytes=64)
+            else:
+                w_codes = late.tile([P, count * NQ], U32, name="w_codes_head", offset=1536, align_bytes=64)
+            w_plane = keep.tile([P, count * NQ], U8, name="w_plane%d" % first, align_bytes=64)
+            nc.vector.quantize_mx(out=w_codes[:].bitcast(FP8X4), scales=w_plane[:], in_=grouped[:].rearrange("p g x -> p (g x)"))
+            for i in range(count):
+                pg = first + i
+                nc.tensor.matmul_mx(
+                    out=acc[:],
+                    lhsT=w_codes[:, i * NQ : (i + 1) * NQ].bitcast(FP8X4),
+                    lhsT_scale=w_plane[:, i * NQ : (i + 1) * NQ],
+                    rhs=v_gots[pg][:].bitcast(FP8X4),
+                    rhs_scale=vsc_plane[:, pg * DV : (pg + 1) * DV],
+                    start=(pg == 0),
+                    stop=(pg == last),
+                )
         result = keep.tile([P, DV], F32, name="result")
         nc.scalar.activation(result[:], acc[:], ACT.Copy, scale=OUT_SCALE)
         nc.sync.dma_start(out[0], result[:])

@@ -42,33 +42,40 @@ def tile_attend_pkv4q_silu_kernel(tc, q_words, q_scales, k_words, k_scales, v_wo
         vs_rows = keep.tile([P, T // P], F32, name="vs_rows")
         k_pool = keep.tile([P, T], I32, name="k_pool")
         ks_pool = keep.tile([P, T], U8, name="ks_pool")
-        vsc_pool = late.tile([P, POOL_PAGES * DV], U8, name="vsc_pool", offset=0, align_bytes=64)
+        vsc_pool = keep.tile([P, POOL_PAGES * DV], U8, name="vsc_pool")
+        vsc_plane = keep.tile([P, PAGES * DV], U8, name="vsc_plane", align_bytes=64)
         ks_planes = keep.tile([P, PASSES, N], U8, name="ks_planes", align_bytes=64)
         vs_pool = keep.tile([P, T], F32, name="vs_pool", tag="vs_pool", align_bytes=64)
         q_codes = keep.tile([P, PASSES, NQ], I32, name="q_codes", align_bytes=64)
         q_planes = keep.tile([P, PASSES * NQ], U8, name="q_planes", align_bytes=64)
         ident = keep.tile([P, P], F32, name="ident")
 
-        nc.vector.memset(q_planes[:].bitcast(I32), 0)
         nc.vector.memset(ks_pool[0:TOP, :].bitcast(I32), 0)
-        nc.vector.memset(ks_planes[:].bitcast(I32), 0)
+        nc.vector.memset(vsc_pool[0 : P - BLOCKS, :].bitcast(I32), 0)
+        nc.vector.memset(q_planes[:].bitcast(I32), 0)
         make_identity(nc, ident[:])
+        nc.gpsimd.memset(ks_planes[:].bitcast(I32), 0)
+        nc.gpsimd.memset(vsc_plane[:].bitcast(I32), 0)
 
         nc.sync.dma_start(offs_sb[:], offs)
-        nc.sync.dma_start(ks_pool[TOP:P, :].bitcast(I32), k_scales.bitcast(I32).rearrange("o f t -> f o t"))
+        nc.scalar.dma_start(ks_pool[TOP:P, :].bitcast(I32), k_scales.bitcast(I32).rearrange("o f t -> f o t"))
+        nc.sync.dma_start(voffs_sb[:], voffs)
+        nc.scalar.dma_start(
+            vsc_pool[P - BLOCKS : P, :].bitcast(I32).rearrange("f (u e) -> f u e", u=POOL_PAGES),
+            v_scales.bitcast(I32).rearrange("u f e -> f u e"),
+        )
         nc.sync.dma_start(vs_rows[:], vs[0].rearrange("(p c) -> p c", p=P))
         nc.sync.dma_start(k_pool[:], k_words[0].rearrange("g t b -> g (t b)").bitcast(I32))
         nc.sync.dma_start(q_codes[:], q_words[0].rearrange("o g q r -> g o (q r)").bitcast(I32))
-        nc.sync.dma_start(voffs_sb[:], voffs)
         for quad in range(QUADS):
-            nc.gpsimd.dma_start(
+            nc.sync.dma_start(
                 q_planes[32 * quad : 32 * quad + 4, :].bitcast(I32).rearrange("f (o q) -> f o q", o=PASSES),
                 q_scales[0, :, 4 * quad : 4 * quad + 4, :].bitcast(I32).rearrange("o f q -> f o q"),
             )
 
         vs_by_bank = vs_pool[:].rearrange("p (n b m) -> p b n m", b=T // P // BANK_TURNS, m=BANK_TURNS)
         for bank in range(T // P // BANK_TURNS):
-            spread = psum.tile([P, BANK_TURNS, P], F32, name="spread", bufs=3)
+            spread = psum.tile([P, BANK_TURNS, P], F32, name="spread", tag="turn", bufs=3)
             for m in range(BANK_TURNS):
                 c = BANK_TURNS * bank + m
                 nc.tensor.transpose(spread[:, m, :], vs_rows[:, c : c + 1].to_broadcast([P, P]), ident[:])
@@ -81,12 +88,11 @@ def tile_attend_pkv4q_silu_kernel(tc, q_words, q_scales, k_words, k_scales, v_wo
         v_pool = keep.tile([P, POOL_PAGES * DV], I32, name="v_pool", tag="ks_then_v", align_bytes=64)
         nc.sync.dma_start(v_pool[:].rearrange("p (u e) -> p u e", e=DV), v_words.rearrange("u g e r -> g u (e r)").bitcast(I32))
 
-        nc.gpsimd.memset(vsc_pool[:].bitcast(I32), 0)
+
+        vsc_got = keep.tile([P, PAGES * DV], U8, name="vsc_got", align_bytes=64)
+        nc.vector.tensor_copy(vsc_got[:], vsc_pool[:].indirect(voffs_sb[:]))
         for quad in range(QUADS):
-            nc.sync.dma_start(
-                vsc_pool[32 * quad : 32 * quad + 4, :].bitcast(I32).rearrange("f (u e) -> f u e", u=POOL_PAGES),
-                v_scales[:, 4 * quad : 4 * quad + 4, :].bitcast(I32).rearrange("u f e -> f u e"),
-            )
+            nc.gpsimd.dma_start(vsc_plane[32 * quad : 32 * quad + 4, :].bitcast(I32), vsc_got[P - BLOCKS + 4 * quad : P - BLOCKS + 4 * quad + 4, :].bitcast(I32))
 
         def page_of(list_sb, pg, count=1):
             width = list_sb.shape[1] // PAGES
@@ -104,7 +110,7 @@ def tile_attend_pkv4q_silu_kernel(tc, q_words, q_scales, k_words, k_scales, v_wo
                 k_gots.append(gather_keys(pg))
             by_pass = k_gots[pg][:].bitcast(U16).rearrange("p (n o) -> p o n", o=PASSES)
             k_codes = keep.tile([P, PASSES, 2 * PAGE], U8, name="k_codes", tag="k_codes%d" % pg, align_bytes=64)
-            if pg == 0:
+            if pg != 1:
                 for o in range(PASSES):
                     nc.vector.tensor_copy(k_codes[:, o, :].bitcast(U16), by_pass[:, o, :])
             else:
@@ -124,56 +130,45 @@ def tile_attend_pkv4q_silu_kernel(tc, q_words, q_scales, k_words, k_scales, v_wo
             nc.scalar.activation(p_sb[:], scores[:], ACT.Silu)
             p_tiles.append(p_sb)
 
-        grouped_head = keep.tile([P, last, NQ * 4], BF16, name="grouped_head", tag="grouped_head", align_bytes=64)
-        grouped_last = keep.tile([P, 1, NQ * 4], BF16, name="grouped_last", align_bytes=64)
-        v_gots = []
-
-        def gather_values(pg, tag):
-            if tag:
-                v_got = keep.tile([P, DV], U32, name="v_got", tag=tag, align_bytes=64)
-            else:
-                v_got = late.tile([P, DV], U32, name="v_got1", offset=0, align_bytes=64)
-            nc.vector.tensor_copy(v_got[:], v_pool[:].bitcast(U32).indirect(page_of(voffs_sb, pg)))
-            v_gots.append(v_got)
-
+        turned = []
         for pg in range(PAGES):
-            if pg == last:
-                gather_values(0, "p%d" % (last - 1))
-            w_f32 = keep.tile([P, PAGE], F32, name="w_f32_%d" % pg)
+            w_f32 = late.tile([P, PAGE], F32, name="w_f32_%d" % pg, offset=4096 * (pg + 1), align_bytes=64)
             nc.vector.tensor_tensor(w_f32[:], vs_pool[:].indirect(page_of(offs_sb, pg)), p_tiles[pg][:], MULT)
             if pg == last:
-                w_bf = late.tile([P, 2, P, 2], BF16, name="w_bf_last", offset=2048, align_bytes=64)
+                w_bf = late.tile([P, 2, P, 2], BF16, name="w_bf_last", offset=0, align_bytes=64)
             else:
                 w_bf = keep.tile([P, 2, P, 2], BF16, name="w_bf", tag="w_bf%d" % pg if pg else "k_codes%d" % last, align_bytes=64)
             nc.scalar.activation(w_bf[:], w_f32[:].rearrange("p (s u e) -> p u s e", u=2, e=2), ACT.Copy)
-            turned = psum.tile([P, 2, NQ], F32, name="turned", bufs=2)
+            bank = psum.tile([P, 2, NQ], F32, name="bank", tag="turn", bufs=3)
             for u in range(2):
-                nc.tensor.transpose(turned[:, u, :], w_bf[:, u].rearrange("p s e -> p (s e)").bitcast(F32), ident[:])
-            grouped = grouped_head[:, pg, :] if pg < last else grouped_last[:, 0, :]
-            nc.scalar.copy(grouped.bitcast(F32).rearrange("p (q u) -> p q u", u=2), turned[:].rearrange("p u q -> p q u"))
+                nc.tensor.transpose(bank[:, u, :], w_bf[:, u].rearrange("p s e -> p (s e)").bitcast(F32), ident[:])
+            turned.append(bank)
 
+        v_head = keep.tile([P, last * DV], U32, name="v_head", tag="vs_pool", align_bytes=64)
+        nc.vector.tensor_copy(v_head[:], v_pool[:].bitcast(U32).indirect(page_of(voffs_sb, 0, last)))
         acc = psum.tile([P, DV], F32, name="acc")
-        vsc_plane = keep.tile([P, PAGES * DV], U8, name="vsc_plane", tag="p%d" % last, align_bytes=64)
-        nc.vector.tensor_copy(vsc_plane[:], vsc_pool[:].indirect(voffs_sb[:]))
-        for first, count, grouped, v_tag, w_tag in ((0, last, grouped_head, None, None), (last, 1, grouped_last, "grouped_head", "ks_then_v")):
-            gather_values(first + count - 1, v_tag)
-            if w_tag:
-                w_codes = keep.tile([P, count * NQ], U32, name="w_codes", tag=w_tag, align_bytes=64)
+        for pg in range(PAGES):
+            grouped = late.tile([P, NQ * 4], BF16, name="grouped%d" % pg, offset=4096 * PAGES + 1024 * pg, align_bytes=64)
+            nc.scalar.copy(grouped[:].bitcast(F32).rearrange("p (q u) -> p q u", u=2), turned[pg][:].rearrange("p u q -> p q u"))
+            if pg < last:
+                v_got = v_head[:, pg * DV : (pg + 1) * DV]
+                w_codes = keep.tile([P, NQ], U32, name="w_codes%d" % pg, align_bytes=64)
             else:
-                w_codes = late.tile([P, count * NQ], U32, name="w_codes_head", offset=1536, align_bytes=64)
-            w_plane = keep.tile([P, count * NQ], U8, name="w_plane%d" % first, align_bytes=64)
-            nc.vector.quantize_mx(out=w_codes[:].bitcast(FP8X4), scales=w_plane[:], in_=grouped[:].rearrange("p g x -> p (g x)"))
-            for i in range(count):
-                pg = first + i
-                nc.tensor.matmul_mx(
-                    out=acc[:],
-                    lhsT=w_codes[:, i * NQ : (i + 1) * NQ].bitcast(FP8X4),
-                    lhsT_scale=w_plane[:, i * NQ : (i + 1) * NQ],
-                    rhs=v_gots[pg][:].bitcast(FP8X4),
-                    rhs_scale=vsc_plane[:, pg * DV : (pg + 1) * DV],
-                    start=(pg == 0),
-                    stop=(pg == last),
-                )
+                v_last = late.tile([P, DV], U32, name="v_last", offset=4096 * PAGES, align_bytes=64)
+                nc.vector.tensor_copy(v_last[:], v_pool[:].bitcast(U32).indirect(page_of(voffs_sb, last)))
+                v_got = v_last[:]
+                w_codes = keep.tile([P, NQ], U32, name="w_codes_last", align_bytes=64)
+            w_plane = keep.tile([P, NQ], U8, name="w_plane%d" % pg, align_bytes=64)
+            nc.vector.quantize_mx(out=w_codes[:].bitcast(FP8X4), scales=w_plane[:], in_=grouped[:])
+            nc.tensor.matmul_mx(
+                out=acc[:],
+                lhsT=w_codes[:].bitcast(FP8X4),
+                lhsT_scale=w_plane[:],
+                rhs=v_got.bitcast(FP8X4),
+                rhs_scale=vsc_plane[:, pg * DV : (pg + 1) * DV],
+                start=(pg == 0),
+                stop=(pg == last),
+            )
         result = keep.tile([P, DV], F32, name="result")
         nc.scalar.activation(result[:], acc[:], ACT.Copy, scale=OUT_SCALE)
         nc.sync.dma_start(out[0], result[:])

@@ -42,7 +42,7 @@ def tile_attend_pkv4q_silu_kernel(tc, q_words, q_scales, k_words, k_scales, v_wo
         vs_rows = keep.tile([P, T // P], F32, name="vs_rows")
         k_pool = keep.tile([P, T], I32, name="k_pool")
         ks_pool = keep.tile([P, T], U8, name="ks_pool")
-        vsc_pool = keep.tile([P, POOL_PAGES * DV], U8, name="vsc_pool")
+        vsc_pool = keep.tile([P, POOL_PAGES * DV], U8, name="vsc_pool", tag="ks_then_v", align_bytes=64)
         vsc_plane = keep.tile([P, PAGES * DV], U8, name="vsc_plane", align_bytes=64)
         ks_planes = keep.tile([P, PASSES, N], U8, name="ks_planes", align_bytes=64)
         vs_pool = keep.tile([P, T], F32, name="vs_pool", tag="vs_pool", align_bytes=64)
@@ -81,18 +81,18 @@ def tile_attend_pkv4q_silu_kernel(tc, q_words, q_scales, k_words, k_scales, v_wo
                 nc.tensor.transpose(spread[:, m, :], vs_rows[:, c : c + 1].to_broadcast([P, P]), ident[:])
             nc.scalar.activation(vs_by_bank[:, bank], spread[:].rearrange("p m n -> p n m"), ACT.Copy)
 
-        ks_got = keep.tile([P, N], U8, name="ks_got", tag="ks_then_v", align_bytes=64)
+        ks_got = keep.tile([P, N], U8, name="ks_got", align_bytes=64)
         nc.vector.tensor_copy(ks_got[:], ks_pool[:].indirect(offs_sb[:]))
         for quad in range(QUADS):
             nc.sync.dma_start(ks_planes[32 * quad : 32 * quad + 4].bitcast(I32), ks_got[TOP + 8 * quad : TOP + 8 * quad + 8, :].bitcast(I32))
+        vsc_got = keep.tile([P, PAGES * DV], U8, name="vsc_got", align_bytes=64)
+        nc.vector.tensor_copy(vsc_got[:], vsc_pool[:].indirect(voffs_sb[:]))
         v_pool = keep.tile([P, POOL_PAGES * DV], I32, name="v_pool", tag="ks_then_v", align_bytes=64)
         nc.sync.dma_start(v_pool[:].rearrange("p (u e) -> p u e", e=DV), v_words.rearrange("u g e r -> g u (e r)").bitcast(I32))
 
 
-        vsc_got = keep.tile([P, PAGES * DV], U8, name="vsc_got", align_bytes=64)
-        nc.vector.tensor_copy(vsc_got[:], vsc_pool[:].indirect(voffs_sb[:]))
         for quad in range(QUADS):
-            nc.gpsimd.dma_start(vsc_plane[32 * quad : 32 * quad + 4, :].bitcast(I32), vsc_got[P - BLOCKS + 4 * quad : P - BLOCKS + 4 * quad + 4, :].bitcast(I32))
+            nc.sync.dma_start(vsc_plane[32 * quad : 32 * quad + 4, :].bitcast(I32), vsc_got[P - BLOCKS + 4 * quad : P - BLOCKS + 4 * quad + 4, :].bitcast(I32))
 
         def page_of(list_sb, pg, count=1):
             width = list_sb.shape[1] // PAGES
@@ -103,11 +103,16 @@ def tile_attend_pkv4q_silu_kernel(tc, q_words, q_scales, k_words, k_scales, v_wo
             nc.vector.tensor_copy(k_got[:], k_pool[:].bitcast(U32).indirect(page_of(offs_sb, pg)))
             return k_got
 
+        def gather_vs(pg):
+            nc.vector.tensor_copy(vs_got[:, pg, :], vs_pool[:].indirect(page_of(offs_sb, pg)))
+
         p_tiles = []
         k_gots = [gather_keys(0), gather_keys(1)]
         for pg in range(PAGES):
             if pg == last:
                 k_gots.append(gather_keys(pg))
+                vs_got = keep.tile([P, PAGES, PAGE], F32, name="vs_got", tag="k_got1", align_bytes=64)
+                gather_vs(0)
             by_pass = k_gots[pg][:].bitcast(U16).rearrange("p (n o) -> p o n", o=PASSES)
             k_codes = keep.tile([P, PASSES, 2 * PAGE], U8, name="k_codes", tag="k_codes%d" % pg, align_bytes=64)
             if pg != 1:
@@ -126,45 +131,48 @@ def tile_attend_pkv4q_silu_kernel(tc, q_words, q_scales, k_words, k_scales, v_wo
                     start=(o == 0),
                     stop=(o == PASSES - 1),
                 )
-            p_sb = keep.tile([P, PAGE], F32, name="p_sb", tag="p%d" % pg, align_bytes=64)
+            p_sb = late.tile([P, PAGE], F32, name="p%d" % pg, offset=4 * PAGE * (last - pg), align_bytes=64)
             nc.scalar.activation(p_sb[:], scores[:], ACT.Silu)
             p_tiles.append(p_sb)
 
+        def gather_values(v_got, pg):
+            nc.vector.tensor_copy(v_got[:], v_pool[:].bitcast(U32).indirect(page_of(voffs_sb, pg)))
+            return v_got
+
+        for pg in range(1, PAGES):
+            gather_vs(pg)
         turned = []
+        v_gots = []
         for pg in range(PAGES):
-            w_f32 = late.tile([P, PAGE], F32, name="w_f32_%d" % pg, offset=4096 * (pg + 1), align_bytes=64)
-            nc.vector.tensor_tensor(w_f32[:], vs_pool[:].indirect(page_of(offs_sb, pg)), p_tiles[pg][:], MULT)
             if pg == last:
-                w_bf = late.tile([P, 2, P, 2], BF16, name="w_bf_last", offset=0, align_bytes=64)
-            else:
-                w_bf = keep.tile([P, 2, P, 2], BF16, name="w_bf", tag="w_bf%d" % pg if pg else "k_codes%d" % last, align_bytes=64)
-            nc.scalar.activation(w_bf[:], w_f32[:].rearrange("p (s u e) -> p u s e", u=2, e=2), ACT.Copy)
+                v_gots.append(gather_values(late.tile([P, DV], U32, name="v_got0", offset=4 * PAGE * last, align_bytes=64), 0))
+            w_bf = keep.tile([P, PAGE], BF16, name="w_bf", tag="w_bf%d" % pg if pg else "k_got0", align_bytes=64)
+            engine = nc.vector if pg == last else nc.gpsimd
+            engine.tensor_tensor(w_bf[:], p_tiles[pg][:], vs_got[:, pg, :], MULT)
+            words = w_bf[:].bitcast(F32).rearrange("p (s u) -> p u s", u=2)
             bank = psum.tile([P, 2, NQ], F32, name="bank", tag="turn", bufs=3)
             for u in range(2):
-                nc.tensor.transpose(bank[:, u, :], w_bf[:, u].rearrange("p s e -> p (s e)").bitcast(F32), ident[:])
+                nc.tensor.transpose(bank[:, u, :], words[:, u, :], ident[:])
             turned.append(bank)
 
-        v_head = keep.tile([P, last * DV], U32, name="v_head", tag="vs_pool", align_bytes=64)
-        nc.vector.tensor_copy(v_head[:], v_pool[:].bitcast(U32).indirect(page_of(voffs_sb, 0, last)))
         acc = psum.tile([P, DV], F32, name="acc")
         for pg in range(PAGES):
-            grouped = late.tile([P, NQ * 4], BF16, name="grouped%d" % pg, offset=4096 * PAGES + 1024 * pg, align_bytes=64)
+            grouped = keep.tile([P, NQ * 4], BF16, name="grouped", tag="grouped%d" % pg if pg else "k_codes%d" % last, align_bytes=64)
             nc.scalar.copy(grouped[:].bitcast(F32).rearrange("p (q u) -> p q u", u=2), turned[pg][:].rearrange("p u q -> p q u"))
-            if pg < last:
-                v_got = v_head[:, pg * DV : (pg + 1) * DV]
-                w_codes = keep.tile([P, NQ], U32, name="w_codes%d" % pg, align_bytes=64)
+            if pg == 0:
+                w_codes = late.tile([P, NQ], U32, name="w_codes0", offset=4 * PAGE, align_bytes=64)
             else:
-                v_last = late.tile([P, DV], U32, name="v_last", offset=4096 * PAGES, align_bytes=64)
-                nc.vector.tensor_copy(v_last[:], v_pool[:].bitcast(U32).indirect(page_of(voffs_sb, last)))
-                v_got = v_last[:]
-                w_codes = keep.tile([P, NQ], U32, name="w_codes_last", align_bytes=64)
+                w_codes = keep.tile([P, NQ], U32, name="w_codes%d" % pg, align_bytes=64)
+            if pg == 1:
+                v_gots.append(gather_values(late.tile([P, DV], U32, name="v_got1", offset=4 * PAGE + 4 * DV, align_bytes=64), pg))
+                v_gots.append(gather_values(keep.tile([P, DV], U32, name="v_got2", tag="k_codes%d" % last, align_bytes=64), last))
             w_plane = keep.tile([P, NQ], U8, name="w_plane%d" % pg, align_bytes=64)
             nc.vector.quantize_mx(out=w_codes[:].bitcast(FP8X4), scales=w_plane[:], in_=grouped[:])
             nc.tensor.matmul_mx(
                 out=acc[:],
                 lhsT=w_codes[:].bitcast(FP8X4),
                 lhsT_scale=w_plane[:],
-                rhs=v_got.bitcast(FP8X4),
+                rhs=v_gots[pg][:].bitcast(FP8X4),
                 rhs_scale=vsc_plane[:, pg * DV : (pg + 1) * DV],
                 start=(pg == 0),
                 stop=(pg == last),

@@ -12,8 +12,10 @@ PASSES = D // 512
 QUADS = 4
 BLOCKS = 16
 LIST_ROWS = 16
+QUAD = P // QUADS
+ROWS = BLOCKS // QUADS
 BANK_TURNS = 4
-TOP = 96
+TURN_BANKS = PAGES
 OUT_SCALE = 1.0 / 16.0
 FLOPS = 2 * NQ * N * (D + DV)
 
@@ -34,7 +36,6 @@ def tile_attend_pkv4q_silu_kernel(tc, q_words, q_scales, k_words, k_scales, v_wo
     last = PAGES - 1
     with ExitStack() as ctx:
         keep = ctx.enter_context(tc.tile_pool(name="keep", bufs=1))
-        late = ctx.enter_context(tc.tile_pool(name="late", bufs=1))
         psum = ctx.enter_context(tc.psum_pool(name="psum", bufs=1))
 
         offs_sb = keep.tile([P, N // LIST_ROWS], U16, name="offs_sb")
@@ -42,69 +43,72 @@ def tile_attend_pkv4q_silu_kernel(tc, q_words, q_scales, k_words, k_scales, v_wo
         vs_rows = keep.tile([P, T // P], F32, name="vs_rows")
         k_pool = keep.tile([P, T], I32, name="k_pool")
         ks_pool = keep.tile([P, T], U8, name="ks_pool")
-        vsc_pool = keep.tile([P, POOL_PAGES * DV], U8, name="vsc_pool", tag="ks_then_v", align_bytes=64)
+        vsc_pool = keep.tile([P, POOL_PAGES * DV], U8, name="vsc_pool", tag="value_pool", align_bytes=64)
         vsc_plane = keep.tile([P, PAGES * DV], U8, name="vsc_plane", align_bytes=64)
         ks_planes = keep.tile([P, PASSES, N], U8, name="ks_planes", align_bytes=64)
-        vs_pool = keep.tile([P, T], F32, name="vs_pool", tag="vs_pool", align_bytes=64)
+        vs_pool = keep.tile([P, T], F32, name="vs_pool", align_bytes=64)
         q_codes = keep.tile([P, PASSES, NQ], I32, name="q_codes", align_bytes=64)
         q_planes = keep.tile([P, PASSES * NQ], U8, name="q_planes", align_bytes=64)
         ident = keep.tile([P, P], F32, name="ident")
 
-        nc.vector.memset(ks_pool[0:TOP, :].bitcast(I32), 0)
-        nc.vector.memset(vsc_pool[0 : P - BLOCKS, :].bitcast(I32), 0)
+        vsc_first = P - BLOCKS
         nc.vector.memset(q_planes[:].bitcast(I32), 0)
+        nc.vector.memset(ks_pool[QUAD : 2 * QUAD, :].bitcast(I32), 0)
+        nc.vector.memset(ks_pool[2 * QUAD : P, :].bitcast(I32), 0)
+        nc.vector.memset(vsc_pool[0:vsc_first, :].bitcast(I32), 0)
         make_identity(nc, ident[:])
         nc.gpsimd.memset(ks_planes[:].bitcast(I32), 0)
         nc.gpsimd.memset(vsc_plane[:].bitcast(I32), 0)
 
         nc.sync.dma_start(offs_sb[:], offs)
-        nc.scalar.dma_start(ks_pool[TOP:P, :].bitcast(I32), k_scales.bitcast(I32).rearrange("o f t -> f o t"))
+        nc.scalar.dma_start(ks_pool[0:QUAD, :].bitcast(I32), k_scales.bitcast(I32).rearrange("o f t -> f o t"))
         nc.sync.dma_start(voffs_sb[:], voffs)
         nc.scalar.dma_start(
-            vsc_pool[P - BLOCKS : P, :].bitcast(I32).rearrange("f (u e) -> f u e", u=POOL_PAGES),
+            vsc_pool[vsc_first:P, :].bitcast(I32).rearrange("f (u e) -> f u e", u=POOL_PAGES),
             v_scales.bitcast(I32).rearrange("u f e -> f u e"),
         )
         nc.sync.dma_start(vs_rows[:], vs[0].rearrange("(p c) -> p c", p=P))
         nc.sync.dma_start(k_pool[:], k_words[0].rearrange("g t b -> g (t b)").bitcast(I32))
         nc.sync.dma_start(q_codes[:], q_words[0].rearrange("o g q r -> g o (q r)").bitcast(I32))
         for quad in range(QUADS):
-            nc.sync.dma_start(
-                q_planes[32 * quad : 32 * quad + 4, :].bitcast(I32).rearrange("f (o q) -> f o q", o=PASSES),
-                q_scales[0, :, 4 * quad : 4 * quad + 4, :].bitcast(I32).rearrange("o f q -> f o q"),
+            queue = nc.sync if quad % 2 else nc.gpsimd
+            queue.dma_start(
+                q_planes[QUAD * quad : QUAD * quad + ROWS, :].bitcast(I32).rearrange("f (o q) -> f o q", o=PASSES),
+                q_scales[0, :, ROWS * quad : ROWS * (quad + 1), :].bitcast(I32).rearrange("o f q -> f o q"),
             )
 
         vs_by_bank = vs_pool[:].rearrange("p (n b m) -> p b n m", b=T // P // BANK_TURNS, m=BANK_TURNS)
-        for bank in range(T // P // BANK_TURNS):
-            spread = psum.tile([P, BANK_TURNS, P], F32, name="spread", tag="turn", bufs=3)
+        for b in range(T // P // BANK_TURNS):
+            spread = psum.tile([P, BANK_TURNS, P], F32, name="spread", tag="turn", bufs=TURN_BANKS)
             for m in range(BANK_TURNS):
-                c = BANK_TURNS * bank + m
+                c = BANK_TURNS * b + m
                 nc.tensor.transpose(spread[:, m, :], vs_rows[:, c : c + 1].to_broadcast([P, P]), ident[:])
-            nc.scalar.activation(vs_by_bank[:, bank], spread[:].rearrange("p m n -> p n m"), ACT.Copy)
+            nc.scalar.activation(vs_by_bank[:, b], spread[:].rearrange("p m n -> p n m"), ACT.Copy)
 
         ks_got = keep.tile([P, N], U8, name="ks_got", align_bytes=64)
         nc.vector.tensor_copy(ks_got[:], ks_pool[:].indirect(offs_sb[:]))
         for quad in range(QUADS):
-            nc.sync.dma_start(ks_planes[32 * quad : 32 * quad + 4].bitcast(I32), ks_got[TOP + 8 * quad : TOP + 8 * quad + 8, :].bitcast(I32))
+            rows = slice(PASSES * ROWS * quad, PASSES * ROWS * (quad + 1))
+            nc.sync.dma_start(ks_planes[QUAD * quad : QUAD * quad + ROWS].bitcast(I32), ks_got[rows, :].bitcast(I32))
         vsc_got = keep.tile([P, PAGES * DV], U8, name="vsc_got", align_bytes=64)
         nc.vector.tensor_copy(vsc_got[:], vsc_pool[:].indirect(voffs_sb[:]))
-        v_pool = keep.tile([P, POOL_PAGES * DV], I32, name="v_pool", tag="ks_then_v", align_bytes=64)
+        v_pool = keep.tile([P, POOL_PAGES * DV], I32, name="v_pool", tag="value_pool", align_bytes=64)
         nc.sync.dma_start(v_pool[:].rearrange("p (u e) -> p u e", e=DV), v_words.rearrange("u g e r -> g u (e r)").bitcast(I32))
-
-
         for quad in range(QUADS):
-            nc.sync.dma_start(vsc_plane[32 * quad : 32 * quad + 4, :].bitcast(I32), vsc_got[P - BLOCKS + 4 * quad : P - BLOCKS + 4 * quad + 4, :].bitcast(I32))
+            rows = slice(vsc_first + ROWS * quad, vsc_first + ROWS * (quad + 1))
+            nc.sync.dma_start(vsc_plane[QUAD * quad : QUAD * quad + ROWS, :].bitcast(I32), vsc_got[rows, :].bitcast(I32))
 
-        def page_of(list_sb, pg, count=1):
+        def entries_of(list_sb, pg, count=1):
             width = list_sb.shape[1] // PAGES
             return list_sb[:, pg * width : (pg + count) * width]
 
         def gather_keys(pg):
             k_got = keep.tile([P, PAGE], U32, name="k_got", tag="k_got%d" % (pg % 2), align_bytes=64)
-            nc.vector.tensor_copy(k_got[:], k_pool[:].bitcast(U32).indirect(page_of(offs_sb, pg)))
+            nc.vector.tensor_copy(k_got[:], k_pool[:].bitcast(U32).indirect(entries_of(offs_sb, pg)))
             return k_got
 
         def gather_vs(pg):
-            nc.vector.tensor_copy(vs_got[:, pg, :], vs_pool[:].indirect(page_of(offs_sb, pg)))
+            nc.vector.tensor_copy(vs_got[:, pg, :], vs_pool[:].indirect(entries_of(offs_sb, pg)))
 
         p_tiles = []
         k_gots = [gather_keys(0), gather_keys(1)]
@@ -115,7 +119,7 @@ def tile_attend_pkv4q_silu_kernel(tc, q_words, q_scales, k_words, k_scales, v_wo
                 gather_vs(0)
             by_pass = k_gots[pg][:].bitcast(U16).rearrange("p (n o) -> p o n", o=PASSES)
             k_codes = keep.tile([P, PASSES, 2 * PAGE], U8, name="k_codes", tag="k_codes%d" % pg, align_bytes=64)
-            if pg != 1:
+            if pg in (0, last):
                 for o in range(PASSES):
                     nc.vector.tensor_copy(k_codes[:, o, :].bitcast(U16), by_pass[:, o, :])
             else:
@@ -131,48 +135,46 @@ def tile_attend_pkv4q_silu_kernel(tc, q_words, q_scales, k_words, k_scales, v_wo
                     start=(o == 0),
                     stop=(o == PASSES - 1),
                 )
-            p_sb = late.tile([P, PAGE], F32, name="p%d" % pg, offset=4 * PAGE * (last - pg), align_bytes=64)
+            p_sb = keep.tile([P, PAGE], F32, name="p_sb", tag="p%d" % pg, align_bytes=64)
             nc.scalar.activation(p_sb[:], scores[:], ACT.Silu)
             p_tiles.append(p_sb)
-
-        def gather_values(v_got, pg):
-            nc.vector.tensor_copy(v_got[:], v_pool[:].bitcast(U32).indirect(page_of(voffs_sb, pg)))
-            return v_got
 
         for pg in range(1, PAGES):
             gather_vs(pg)
         turned = []
-        v_gots = []
         for pg in range(PAGES):
-            if pg == last:
-                v_gots.append(gather_values(late.tile([P, DV], U32, name="v_got0", offset=4 * PAGE * last, align_bytes=64), 0))
             w_bf = keep.tile([P, PAGE], BF16, name="w_bf", tag="w_bf%d" % pg if pg else "k_got0", align_bytes=64)
-            engine = nc.vector if pg == last else nc.gpsimd
+            engine = nc.vector if pg else nc.gpsimd
             engine.tensor_tensor(w_bf[:], p_tiles[pg][:], vs_got[:, pg, :], MULT)
             words = w_bf[:].bitcast(F32).rearrange("p (s u) -> p u s", u=2)
-            bank = psum.tile([P, 2, NQ], F32, name="bank", tag="turn", bufs=3)
+            bank = psum.tile([P, 2, NQ], F32, name="bank", tag="turn", bufs=TURN_BANKS)
             for u in range(2):
                 nc.tensor.transpose(bank[:, u, :], words[:, u, :], ident[:])
             turned.append(bank)
 
+        v_head = keep.tile([P, last * DV], U32, name="v_head", tag="p%d" % last, align_bytes=64)
+        nc.vector.tensor_copy(v_head[:], v_pool[:].bitcast(U32).indirect(entries_of(voffs_sb, 0, last)))
+        w_head = keep.tile([P, last, NQ], U32, name="w_head", tag="k_got1", align_bytes=64)
         acc = psum.tile([P, DV], F32, name="acc")
         for pg in range(PAGES):
             grouped = keep.tile([P, NQ * 4], BF16, name="grouped", tag="grouped%d" % pg if pg else "k_codes%d" % last, align_bytes=64)
             nc.scalar.copy(grouped[:].bitcast(F32).rearrange("p (q u) -> p q u", u=2), turned[pg][:].rearrange("p u q -> p q u"))
-            if pg == 0:
-                w_codes = late.tile([P, NQ], U32, name="w_codes0", offset=4 * PAGE, align_bytes=64)
+            if pg < last:
+                v_got = v_head[:, pg * DV : (pg + 1) * DV]
+                w_codes = w_head[:, pg, :]
             else:
-                w_codes = keep.tile([P, NQ], U32, name="w_codes%d" % pg, align_bytes=64)
-            if pg == 1:
-                v_gots.append(gather_values(late.tile([P, DV], U32, name="v_got1", offset=4 * PAGE + 4 * DV, align_bytes=64), pg))
-                v_gots.append(gather_values(keep.tile([P, DV], U32, name="v_got2", tag="k_codes%d" % last, align_bytes=64), last))
+                v_last = keep.tile([P, DV], U32, name="v_last", tag="k_codes%d" % last, align_bytes=64)
+                nc.vector.tensor_copy(v_last[:], v_pool[:].bitcast(U32).indirect(entries_of(voffs_sb, last)))
+                v_got = v_last[:]
+                w_last = keep.tile([P, NQ], U32, name="w_last", align_bytes=64)
+                w_codes = w_last[:]
             w_plane = keep.tile([P, NQ], U8, name="w_plane%d" % pg, align_bytes=64)
-            nc.vector.quantize_mx(out=w_codes[:].bitcast(FP8X4), scales=w_plane[:], in_=grouped[:])
+            nc.vector.quantize_mx(out=w_codes.bitcast(FP8X4), scales=w_plane[:], in_=grouped[:])
             nc.tensor.matmul_mx(
                 out=acc[:],
-                lhsT=w_codes[:].bitcast(FP8X4),
+                lhsT=w_codes.bitcast(FP8X4),
                 lhsT_scale=w_plane[:],
-                rhs=v_gots[pg][:].bitcast(FP8X4),
+                rhs=v_got.bitcast(FP8X4),
                 rhs_scale=vsc_plane[:, pg * DV : (pg + 1) * DV],
                 start=(pg == 0),
                 stop=(pg == last),

@@ -16,6 +16,7 @@ QUAD = P // QUADS
 ROWS = BLOCKS // QUADS
 BANK_TURNS = 4
 TURN_BANKS = PAGES
+VS_TAIL = 256
 OUT_SCALE = 1.0 / 16.0
 FLOPS = 2 * NQ * N * (D + DV)
 
@@ -46,25 +47,25 @@ def tile_attend_pkv4q_silu_kernel(tc, q_words, q_scales, k_words, k_scales, v_wo
         vsc_pool = keep.tile([P, POOL_PAGES * DV], U8, name="vsc_pool", tag="value_pool", align_bytes=64)
         vsc_plane = keep.tile([P, PAGES * DV], U8, name="vsc_plane", align_bytes=64)
         ks_planes = keep.tile([P, PASSES, N], U8, name="ks_planes", align_bytes=64)
-        vs_pool = keep.tile([P, T], F32, name="vs_pool", align_bytes=64)
+        vs_pool = keep.tile([P, T], F32, name="vs_pool", tag="vs_pool", align_bytes=64)
         q_codes = keep.tile([P, PASSES, NQ], I32, name="q_codes", align_bytes=64)
         q_planes = keep.tile([P, PASSES * NQ], U8, name="q_planes", align_bytes=64)
         ident = keep.tile([P, P], F32, name="ident")
 
-        vsc_first = P - BLOCKS
-        nc.vector.memset(q_planes[:].bitcast(I32), 0)
-        nc.vector.memset(ks_pool[QUAD : 2 * QUAD, :].bitcast(I32), 0)
-        nc.vector.memset(ks_pool[2 * QUAD : P, :].bitcast(I32), 0)
+        ks_first = P - PASSES * BLOCKS
+        vsc_first = P // 2 - BLOCKS
+        warm_in = keep.tile([P, 1], F32, name="warm_in")
+        nc.vector.memset(warm_in[:], 0.0)
+        nc.vector.memset(ks_pool[0:ks_first, :].bitcast(I32), 0)
         nc.vector.memset(vsc_pool[0:vsc_first, :].bitcast(I32), 0)
+        nc.vector.memset(vsc_pool[P // 2 : P, :].bitcast(I32), 0)
         make_identity(nc, ident[:])
-        nc.gpsimd.memset(ks_planes[:].bitcast(I32), 0)
-        nc.gpsimd.memset(vsc_plane[:].bitcast(I32), 0)
 
         nc.sync.dma_start(offs_sb[:], offs)
-        nc.scalar.dma_start(ks_pool[0:QUAD, :].bitcast(I32), k_scales.bitcast(I32).rearrange("o f t -> f o t"))
+        nc.scalar.dma_start(ks_pool[ks_first:P, :].bitcast(I32), k_scales.bitcast(I32).rearrange("o f t -> f o t"))
         nc.sync.dma_start(voffs_sb[:], voffs)
         nc.scalar.dma_start(
-            vsc_pool[vsc_first:P, :].bitcast(I32).rearrange("f (u e) -> f u e", u=POOL_PAGES),
+            vsc_pool[vsc_first : P // 2, :].bitcast(I32).rearrange("f (u e) -> f u e", u=POOL_PAGES),
             v_scales.bitcast(I32).rearrange("u f e -> f u e"),
         )
         nc.sync.dma_start(vs_rows[:], vs[0].rearrange("(p c) -> p c", p=P))
@@ -77,9 +78,12 @@ def tile_attend_pkv4q_silu_kernel(tc, q_words, q_scales, k_words, k_scales, v_wo
                 q_scales[0, :, ROWS * quad : ROWS * (quad + 1), :].bitcast(I32).rearrange("o f q -> f o q"),
             )
 
+        warm = keep.tile([P, 1], F32, name="warm")
+        nc.scalar.activation(warm[:], warm_in[:], ACT.Silu)
+
         vs_by_bank = vs_pool[:].rearrange("p (n b m) -> p b n m", b=T // P // BANK_TURNS, m=BANK_TURNS)
         for b in range(T // P // BANK_TURNS):
-            spread = psum.tile([P, BANK_TURNS, P], F32, name="spread", tag="turn", bufs=TURN_BANKS)
+            spread = psum.tile([P, BANK_TURNS, P], F32, name="spread", tag="bank%d" % (b % TURN_BANKS))
             for m in range(BANK_TURNS):
                 c = BANK_TURNS * b + m
                 nc.tensor.transpose(spread[:, m, :], vs_rows[:, c : c + 1].to_broadcast([P, P]), ident[:])
@@ -88,7 +92,7 @@ def tile_attend_pkv4q_silu_kernel(tc, q_words, q_scales, k_words, k_scales, v_wo
         ks_got = keep.tile([P, N], U8, name="ks_got", align_bytes=64)
         nc.vector.tensor_copy(ks_got[:], ks_pool[:].indirect(offs_sb[:]))
         for quad in range(QUADS):
-            rows = slice(PASSES * ROWS * quad, PASSES * ROWS * (quad + 1))
+            rows = slice(ks_first + PASSES * ROWS * quad, ks_first + PASSES * ROWS * (quad + 1))
             nc.sync.dma_start(ks_planes[QUAD * quad : QUAD * quad + ROWS].bitcast(I32), ks_got[rows, :].bitcast(I32))
         vsc_got = keep.tile([P, PAGES * DV], U8, name="vsc_got", align_bytes=64)
         nc.vector.tensor_copy(vsc_got[:], vsc_pool[:].indirect(voffs_sb[:]))
@@ -107,16 +111,18 @@ def tile_attend_pkv4q_silu_kernel(tc, q_words, q_scales, k_words, k_scales, v_wo
             nc.vector.tensor_copy(k_got[:], k_pool[:].bitcast(U32).indirect(entries_of(offs_sb, pg)))
             return k_got
 
-        def gather_vs(pg):
-            nc.vector.tensor_copy(vs_got[:, pg, :], vs_pool[:].indirect(entries_of(offs_sb, pg)))
+        head = N - VS_TAIL
+        vs_head = keep.tile([P, head], F32, name="vs_head", align_bytes=64)
+        nc.scalar.activation(vs_head[:], vs_pool[:].indirect(offs_sb[:, : head // LIST_ROWS]), ACT.Copy)
 
-        p_tiles = []
+        score_banks = []
+
         k_gots = [gather_keys(0), gather_keys(1)]
         for pg in range(PAGES):
             if pg == last:
-                k_gots.append(gather_keys(pg))
-                vs_got = keep.tile([P, PAGES, PAGE], F32, name="vs_got", tag="k_got1", align_bytes=64)
-                gather_vs(0)
+                k_gots.append(gather_keys(last))
+                vs_tail = keep.tile([P, VS_TAIL], F32, name="vs_tail", tag="k_got1", align_bytes=64)
+                nc.vector.tensor_copy(vs_tail[:], vs_pool[:].indirect(offs_sb[:, head // LIST_ROWS :]))
             by_pass = k_gots[pg][:].bitcast(U16).rearrange("p (n o) -> p o n", o=PASSES)
             k_codes = keep.tile([P, PASSES, 2 * PAGE], U8, name="k_codes", tag="k_codes%d" % pg, align_bytes=64)
             if pg in (0, last):
@@ -124,7 +130,7 @@ def tile_attend_pkv4q_silu_kernel(tc, q_words, q_scales, k_words, k_scales, v_wo
                     nc.vector.tensor_copy(k_codes[:, o, :].bitcast(U16), by_pass[:, o, :])
             else:
                 nc.vector.tensor_copy(k_codes[:].bitcast(U16), by_pass)
-            scores = psum.tile([P, PAGE], F32, name="scores", bufs=2)
+            scores = psum.tile([P, PAGE], F32, name="scores", tag="scores%d" % pg)
             for o in range(PASSES):
                 nc.tensor.matmul_mx(
                     out=scores[:],
@@ -135,44 +141,48 @@ def tile_attend_pkv4q_silu_kernel(tc, q_words, q_scales, k_words, k_scales, v_wo
                     start=(o == 0),
                     stop=(o == PASSES - 1),
                 )
-            p_sb = keep.tile([P, PAGE], F32, name="p_sb", tag="p%d" % pg, align_bytes=64)
-            nc.scalar.activation(p_sb[:], scores[:], ACT.Silu)
-            p_tiles.append(p_sb)
+            score_banks.append(scores)
 
-        for pg in range(1, PAGES):
-            gather_vs(pg)
-        turned = []
+        p_all = keep.tile([P, PAGES, PAGE], F32, name="p_all", tag="vs_pool", align_bytes=64)
         for pg in range(PAGES):
-            w_bf = keep.tile([P, PAGE], BF16, name="w_bf", tag="w_bf%d" % pg if pg else "k_got0", align_bytes=64)
-            engine = nc.vector if pg else nc.gpsimd
-            engine.tensor_tensor(w_bf[:], p_tiles[pg][:], vs_got[:, pg, :], MULT)
-            words = w_bf[:].bitcast(F32).rearrange("p (s u) -> p u s", u=2)
-            bank = psum.tile([P, 2, NQ], F32, name="bank", tag="turn", bufs=TURN_BANKS)
+            nc.scalar.activation(p_all[:, pg, :], score_banks[pg][:], ACT.Silu)
+
+        turned = []
+        w_all = keep.tile([P, PAGES, PAGE], BF16, name="w_all", tag="k_got0", align_bytes=64)
+        for pg in range(PAGES):
+            w_bf = w_all[:, pg, :]
+            if pg < last:
+                nc.vector.tensor_tensor(w_bf, p_all[:, pg, :], vs_head[:, pg * PAGE : (pg + 1) * PAGE], MULT)
+            else:
+                cut = PAGE - VS_TAIL
+                nc.vector.tensor_tensor(w_bf[:, :cut], p_all[:, pg, :cut], vs_head[:, pg * PAGE :], MULT)
+                nc.vector.tensor_tensor(w_bf[:, cut:], p_all[:, pg, cut:], vs_tail[:], MULT)
+            words = w_bf.bitcast(F32).rearrange("p (s u) -> p u s", u=2)
+            bank = psum.tile([P, 2, NQ], F32, name="bank", tag="bank%d" % pg)
             for u in range(2):
                 nc.tensor.transpose(bank[:, u, :], words[:, u, :], ident[:])
             turned.append(bank)
+            if pg == 1:
+                v_first = keep.tile([P, DV], U32, name="v_first", tag="k_codes1", align_bytes=64)
+                nc.vector.tensor_copy(v_first[:], v_pool[:].bitcast(U32).indirect(entries_of(voffs_sb, 0)))
 
-        v_head = keep.tile([P, last * DV], U32, name="v_head", tag="p%d" % last, align_bytes=64)
-        nc.vector.tensor_copy(v_head[:], v_pool[:].bitcast(U32).indirect(entries_of(voffs_sb, 0, last)))
-        w_head = keep.tile([P, last, NQ], U32, name="w_head", tag="k_got1", align_bytes=64)
         acc = psum.tile([P, DV], F32, name="acc")
         for pg in range(PAGES):
             grouped = keep.tile([P, NQ * 4], BF16, name="grouped", tag="grouped%d" % pg if pg else "k_codes%d" % last, align_bytes=64)
             nc.scalar.copy(grouped[:].bitcast(F32).rearrange("p (q u) -> p q u", u=2), turned[pg][:].rearrange("p u q -> p q u"))
-            if pg < last:
-                v_got = v_head[:, pg * DV : (pg + 1) * DV]
-                w_codes = w_head[:, pg, :]
+            if pg == 0:
+                v_got = v_first[:]
             else:
-                v_last = keep.tile([P, DV], U32, name="v_last", tag="k_codes%d" % last, align_bytes=64)
-                nc.vector.tensor_copy(v_last[:], v_pool[:].bitcast(U32).indirect(entries_of(voffs_sb, last)))
-                v_got = v_last[:]
-                w_last = keep.tile([P, NQ], U32, name="w_last", align_bytes=64)
-                w_codes = w_last[:]
+                if pg == 1:
+                    v_rest = keep.tile([P, last * DV], U32, name="v_rest", tag="vs_pool", align_bytes=64)
+                    nc.vector.tensor_copy(v_rest[:], v_pool[:].bitcast(U32).indirect(entries_of(voffs_sb, 1, last)))
+                v_got = v_rest[:, (pg - 1) * DV : pg * DV]
+            w_codes = keep.tile([P, NQ], U32, name="w_codes%d" % pg, align_bytes=64)
             w_plane = keep.tile([P, NQ], U8, name="w_plane%d" % pg, align_bytes=64)
-            nc.vector.quantize_mx(out=w_codes.bitcast(FP8X4), scales=w_plane[:], in_=grouped[:])
+            nc.vector.quantize_mx(out=w_codes[:].bitcast(FP8X4), scales=w_plane[:], in_=grouped[:])
             nc.tensor.matmul_mx(
                 out=acc[:],
-                lhsT=w_codes.bitcast(FP8X4),
+                lhsT=w_codes[:].bitcast(FP8X4),
                 lhsT_scale=w_plane[:],
                 rhs=v_got.bitcast(FP8X4),
                 rhs_scale=vsc_plane[:, pg * DV : (pg + 1) * DV],

@@ -16,7 +16,9 @@ QUAD = P // QUADS
 ROWS = BLOCKS // QUADS
 BANK_TURNS = 4
 TURN_BANKS = PAGES
-VS_TAIL = 256
+VS_TAIL = PAGE
+AT_VS = 4096
+AT_LAST = AT_VS + 4 * N
 OUT_SCALE = 1.0 / 16.0
 FLOPS = 2 * NQ * N * (D + DV)
 
@@ -37,6 +39,7 @@ def tile_attend_pkv4q_silu_kernel(tc, q_words, q_scales, k_words, k_scales, v_wo
     last = PAGES - 1
     with ExitStack() as ctx:
         keep = ctx.enter_context(tc.tile_pool(name="keep", bufs=1))
+        laid = ctx.enter_context(tc.tile_pool(name="laid", bufs=1))
         psum = ctx.enter_context(tc.psum_pool(name="psum", bufs=1))
 
         offs_sb = keep.tile([P, N // LIST_ROWS], U16, name="offs_sb")
@@ -47,28 +50,28 @@ def tile_attend_pkv4q_silu_kernel(tc, q_words, q_scales, k_words, k_scales, v_wo
         vsc_pool = keep.tile([P, POOL_PAGES * DV], U8, name="vsc_pool", tag="value_pool", align_bytes=64)
         vsc_plane = keep.tile([P, PAGES * DV], U8, name="vsc_plane", align_bytes=64)
         ks_planes = keep.tile([P, PASSES, N], U8, name="ks_planes", align_bytes=64)
-        vs_pool = keep.tile([P, T], F32, name="vs_pool", tag="vs_pool", align_bytes=64)
+        vs_pool = laid.tile([P, T], F32, name="vs_pool", offset=AT_VS, align_bytes=64)
         q_codes = keep.tile([P, PASSES, NQ], I32, name="q_codes", align_bytes=64)
         q_planes = keep.tile([P, PASSES * NQ], U8, name="q_planes", align_bytes=64)
         ident = keep.tile([P, P], F32, name="ident")
 
-        ks_first = P - PASSES * BLOCKS
-        vsc_first = P // 2 - BLOCKS
+        vsc_first = P - BLOCKS
         warm_in = keep.tile([P, 1], F32, name="warm_in")
         nc.vector.memset(warm_in[:], 0.0)
-        nc.vector.memset(ks_pool[0:ks_first, :].bitcast(I32), 0)
+        nc.vector.memset(q_planes[:].bitcast(I32), 0)
+        nc.vector.memset(ks_pool[QUAD : 2 * QUAD, :].bitcast(I32), 0)
+        nc.vector.memset(ks_pool[2 * QUAD : P, :].bitcast(I32), 0)
         nc.vector.memset(vsc_pool[0:vsc_first, :].bitcast(I32), 0)
-        nc.vector.memset(vsc_pool[P // 2 : P, :].bitcast(I32), 0)
         make_identity(nc, ident[:])
 
+        nc.sync.dma_start(vs_rows[:], vs[0].rearrange("(p c) -> p c", p=P))
         nc.sync.dma_start(offs_sb[:], offs)
-        nc.scalar.dma_start(ks_pool[ks_first:P, :].bitcast(I32), k_scales.bitcast(I32).rearrange("o f t -> f o t"))
+        nc.scalar.dma_start(ks_pool[0:QUAD, :].bitcast(I32), k_scales.bitcast(I32).rearrange("o f t -> f o t"))
         nc.sync.dma_start(voffs_sb[:], voffs)
         nc.scalar.dma_start(
-            vsc_pool[vsc_first : P // 2, :].bitcast(I32).rearrange("f (u e) -> f u e", u=POOL_PAGES),
+            vsc_pool[vsc_first:P, :].bitcast(I32).rearrange("f (u e) -> f u e", u=POOL_PAGES),
             v_scales.bitcast(I32).rearrange("u f e -> f u e"),
         )
-        nc.sync.dma_start(vs_rows[:], vs[0].rearrange("(p c) -> p c", p=P))
         nc.sync.dma_start(k_pool[:], k_words[0].rearrange("g t b -> g (t b)").bitcast(I32))
         nc.sync.dma_start(q_codes[:], q_words[0].rearrange("o g q r -> g o (q r)").bitcast(I32))
         for quad in range(QUADS):
@@ -92,7 +95,7 @@ def tile_attend_pkv4q_silu_kernel(tc, q_words, q_scales, k_words, k_scales, v_wo
         ks_got = keep.tile([P, N], U8, name="ks_got", align_bytes=64)
         nc.vector.tensor_copy(ks_got[:], ks_pool[:].indirect(offs_sb[:]))
         for quad in range(QUADS):
-            rows = slice(ks_first + PASSES * ROWS * quad, ks_first + PASSES * ROWS * (quad + 1))
+            rows = slice(PASSES * ROWS * quad, PASSES * ROWS * (quad + 1))
             nc.sync.dma_start(ks_planes[QUAD * quad : QUAD * quad + ROWS].bitcast(I32), ks_got[rows, :].bitcast(I32))
         vsc_got = keep.tile([P, PAGES * DV], U8, name="vsc_got", align_bytes=64)
         nc.vector.tensor_copy(vsc_got[:], vsc_pool[:].indirect(voffs_sb[:]))
@@ -107,7 +110,10 @@ def tile_attend_pkv4q_silu_kernel(tc, q_words, q_scales, k_words, k_scales, v_wo
             return list_sb[:, pg * width : (pg + count) * width]
 
         def gather_keys(pg):
-            k_got = keep.tile([P, PAGE], U32, name="k_got", tag="k_got%d" % (pg % 2), align_bytes=64)
+            if pg % 2:
+                k_got = keep.tile([P, PAGE], U32, name="k_got1", align_bytes=64)
+            else:
+                k_got = laid.tile([P, PAGE], U32, name="k_got%d" % pg, offset=0, align_bytes=64)
             nc.vector.tensor_copy(k_got[:], k_pool[:].bitcast(U32).indirect(entries_of(offs_sb, pg)))
             return k_got
 
@@ -121,10 +127,13 @@ def tile_attend_pkv4q_silu_kernel(tc, q_words, q_scales, k_words, k_scales, v_wo
         for pg in range(PAGES):
             if pg == last:
                 k_gots.append(gather_keys(last))
-                vs_tail = keep.tile([P, VS_TAIL], F32, name="vs_tail", tag="k_got1", align_bytes=64)
+                vs_tail = keep.tile([P, VS_TAIL], F32, name="vs_tail", tag="k_codes0", align_bytes=64)
                 nc.vector.tensor_copy(vs_tail[:], vs_pool[:].indirect(offs_sb[:, head // LIST_ROWS :]))
             by_pass = k_gots[pg][:].bitcast(U16).rearrange("p (n o) -> p o n", o=PASSES)
-            k_codes = keep.tile([P, PASSES, 2 * PAGE], U8, name="k_codes", tag="k_codes%d" % pg, align_bytes=64)
+            if pg < last:
+                k_codes = keep.tile([P, PASSES, 2 * PAGE], U8, name="k_codes%d" % pg, align_bytes=64)
+            else:
+                k_codes = laid.tile([P, PASSES, 2 * PAGE], U8, name="k_codes%d" % pg, offset=AT_LAST, align_bytes=64)
             if pg in (0, last):
                 for o in range(PASSES):
                     nc.vector.tensor_copy(k_codes[:, o, :].bitcast(U16), by_pass[:, o, :])
@@ -143,20 +152,16 @@ def tile_attend_pkv4q_silu_kernel(tc, q_words, q_scales, k_words, k_scales, v_wo
                 )
             score_banks.append(scores)
 
-        p_all = keep.tile([P, PAGES, PAGE], F32, name="p_all", tag="vs_pool", align_bytes=64)
+        p_all = laid.tile([P, PAGES, PAGE], F32, name="p_all", offset=AT_VS, align_bytes=64)
         for pg in range(PAGES):
             nc.scalar.activation(p_all[:, pg, :], score_banks[pg][:], ACT.Silu)
 
         turned = []
-        w_all = keep.tile([P, PAGES, PAGE], BF16, name="w_all", tag="k_got0", align_bytes=64)
         for pg in range(PAGES):
-            w_bf = w_all[:, pg, :]
-            if pg < last:
-                nc.vector.tensor_tensor(w_bf, p_all[:, pg, :], vs_head[:, pg * PAGE : (pg + 1) * PAGE], MULT)
-            else:
-                cut = PAGE - VS_TAIL
-                nc.vector.tensor_tensor(w_bf[:, :cut], p_all[:, pg, :cut], vs_head[:, pg * PAGE :], MULT)
-                nc.vector.tensor_tensor(w_bf[:, cut:], p_all[:, pg, cut:], vs_tail[:], MULT)
+            w_tile = laid.tile([P, PAGE], BF16, name="w_bf%d" % pg, offset=2 * PAGE * pg, align_bytes=64)
+            w_bf = w_tile[:]
+            vs_page = vs_head[:, pg * PAGE : (pg + 1) * PAGE] if pg < last else vs_tail[:]
+            nc.vector.tensor_tensor(w_bf, p_all[:, pg, :], vs_page, MULT)
             words = w_bf.bitcast(F32).rearrange("p (s u) -> p u s", u=2)
             bank = psum.tile([P, 2, NQ], F32, name="bank", tag="bank%d" % pg)
             for u in range(2):
@@ -168,15 +173,17 @@ def tile_attend_pkv4q_silu_kernel(tc, q_words, q_scales, k_words, k_scales, v_wo
 
         acc = psum.tile([P, DV], F32, name="acc")
         for pg in range(PAGES):
-            grouped = keep.tile([P, NQ * 4], BF16, name="grouped", tag="grouped%d" % pg if pg else "k_codes%d" % last, align_bytes=64)
+            if pg:
+                grouped = keep.tile([P, NQ * 4], BF16, name="grouped%d" % pg, align_bytes=64)
+            else:
+                grouped = laid.tile([P, NQ * 4], BF16, name="grouped0", offset=AT_LAST, align_bytes=64)
             nc.scalar.copy(grouped[:].bitcast(F32).rearrange("p (q u) -> p q u", u=2), turned[pg][:].rearrange("p u q -> p q u"))
             if pg == 0:
                 v_got = v_first[:]
             else:
-                if pg == 1:
-                    v_rest = keep.tile([P, last * DV], U32, name="v_rest", tag="vs_pool", align_bytes=64)
-                    nc.vector.tensor_copy(v_rest[:], v_pool[:].bitcast(U32).indirect(entries_of(voffs_sb, 1, last)))
-                v_got = v_rest[:, (pg - 1) * DV : pg * DV]
+                v_next = laid.tile([P, DV], U32, name="v_next%d" % pg, offset=AT_VS if pg < last else AT_LAST, align_bytes=64)
+                nc.vector.tensor_copy(v_next[:], v_pool[:].bitcast(U32).indirect(entries_of(voffs_sb, pg)))
+                v_got = v_next[:]
             w_codes = keep.tile([P, NQ], U32, name="w_codes%d" % pg, align_bytes=64)
             w_plane = keep.tile([P, NQ], U8, name="w_plane%d" % pg, align_bytes=64)
             nc.vector.quantize_mx(out=w_codes[:].bitcast(FP8X4), scales=w_plane[:], in_=grouped[:])

@@ -16,9 +16,8 @@ QUAD = P // QUADS
 ROWS = BLOCKS // QUADS
 BANK_TURNS = 4
 TURN_BANKS = PAGES
-VS_TAIL = PAGE
 AT_VS = 4096
-AT_LAST = AT_VS + 4 * N
+AT_FIRST = AT_VS + 4 * T
 OUT_SCALE = 1.0 / 16.0
 FLOPS = 2 * NQ * N * (D + DV)
 
@@ -45,7 +44,7 @@ def tile_attend_pkv4q_silu_kernel(tc, q_words, q_scales, k_words, k_scales, v_wo
         offs_sb = keep.tile([P, N // LIST_ROWS], U16, name="offs_sb")
         voffs_sb = keep.tile([P, PAGES * DV // LIST_ROWS], U16, name="voffs_sb")
         vs_rows = keep.tile([P, T // P], F32, name="vs_rows")
-        k_pool = keep.tile([P, T], I32, name="k_pool")
+        k_pool = keep.tile([P, T], I32, name="k_pool", tag="key_pool", align_bytes=64)
         ks_pool = keep.tile([P, T], U8, name="ks_pool")
         vsc_pool = keep.tile([P, POOL_PAGES * DV], U8, name="vsc_pool", tag="value_pool", align_bytes=64)
         vsc_plane = keep.tile([P, PAGES * DV], U8, name="vsc_plane", align_bytes=64)
@@ -109,31 +108,24 @@ def tile_attend_pkv4q_silu_kernel(tc, q_words, q_scales, k_words, k_scales, v_wo
             width = list_sb.shape[1] // PAGES
             return list_sb[:, pg * width : (pg + count) * width]
 
-        def gather_keys(pg):
-            if pg % 2:
-                k_got = keep.tile([P, PAGE], U32, name="k_got1", align_bytes=64)
+        k_gots = []
+        for pg in range(PAGES):
+            if pg < last:
+                k_got = keep.tile([P, PAGE], U32, name="k_got%d" % pg, align_bytes=64)
             else:
                 k_got = laid.tile([P, PAGE], U32, name="k_got%d" % pg, offset=0, align_bytes=64)
             nc.vector.tensor_copy(k_got[:], k_pool[:].bitcast(U32).indirect(entries_of(offs_sb, pg)))
-            return k_got
-
-        head = N - VS_TAIL
-        vs_head = keep.tile([P, head], F32, name="vs_head", align_bytes=64)
-        nc.scalar.activation(vs_head[:], vs_pool[:].indirect(offs_sb[:, : head // LIST_ROWS]), ACT.Copy)
+            k_gots.append(k_got)
+        vs_head = keep.tile([P, last, PAGE], F32, name="vs_head", tag="key_pool", align_bytes=64)
+        nc.scalar.activation(vs_head[:].rearrange("p g s -> p (g s)"), vs_pool[:].indirect(entries_of(offs_sb, 0, last)), ACT.Copy)
 
         score_banks = []
-
-        k_gots = [gather_keys(0), gather_keys(1)]
         for pg in range(PAGES):
-            if pg == last:
-                k_gots.append(gather_keys(last))
-                vs_tail = keep.tile([P, VS_TAIL], F32, name="vs_tail", tag="k_codes0", align_bytes=64)
-                nc.vector.tensor_copy(vs_tail[:], vs_pool[:].indirect(offs_sb[:, head // LIST_ROWS :]))
             by_pass = k_gots[pg][:].bitcast(U16).rearrange("p (n o) -> p o n", o=PASSES)
-            if pg < last:
+            if pg:
                 k_codes = keep.tile([P, PASSES, 2 * PAGE], U8, name="k_codes%d" % pg, align_bytes=64)
             else:
-                k_codes = laid.tile([P, PASSES, 2 * PAGE], U8, name="k_codes%d" % pg, offset=AT_LAST, align_bytes=64)
+                k_codes = laid.tile([P, PASSES, 2 * PAGE], U8, name="k_codes0", offset=AT_FIRST, align_bytes=64)
             if pg in (0, last):
                 for o in range(PASSES):
                     nc.vector.tensor_copy(k_codes[:, o, :].bitcast(U16), by_pass[:, o, :])
@@ -152,38 +144,39 @@ def tile_attend_pkv4q_silu_kernel(tc, q_words, q_scales, k_words, k_scales, v_wo
                 )
             score_banks.append(scores)
 
-        p_all = laid.tile([P, PAGES, PAGE], F32, name="p_all", offset=AT_VS, align_bytes=64)
+        p_tiles = []
         for pg in range(PAGES):
-            nc.scalar.activation(p_all[:, pg, :], score_banks[pg][:], ACT.Silu)
+            if pg == 0:
+                p_sb = keep.tile([P, PAGE], F32, name="p0", align_bytes=64)
+            else:
+                p_sb = laid.tile([P, PAGE], F32, name="p%d" % pg, offset=AT_VS + 4 * PAGE * pg, align_bytes=64)
+            nc.scalar.activation(p_sb[:], score_banks[pg][:], ACT.Silu)
+            p_tiles.append(p_sb)
+            if pg == 0:
+                vs_last = laid.tile([P, PAGE], F32, name="vs_last", offset=AT_FIRST, align_bytes=64)
+                nc.scalar.activation(vs_last[:], vs_pool[:].indirect(entries_of(offs_sb, last)), ACT.Copy)
 
         turned = []
         for pg in range(PAGES):
             w_tile = laid.tile([P, PAGE], BF16, name="w_bf%d" % pg, offset=2 * PAGE * pg, align_bytes=64)
             w_bf = w_tile[:]
-            vs_page = vs_head[:, pg * PAGE : (pg + 1) * PAGE] if pg < last else vs_tail[:]
-            nc.vector.tensor_tensor(w_bf, p_all[:, pg, :], vs_page, MULT)
+            nc.vector.tensor_tensor(w_bf, p_tiles[pg][:], vs_head[:, pg, :] if pg < last else vs_last[:], MULT)
             words = w_bf.bitcast(F32).rearrange("p (s u) -> p u s", u=2)
             bank = psum.tile([P, 2, NQ], F32, name="bank", tag="bank%d" % pg)
             for u in range(2):
                 nc.tensor.transpose(bank[:, u, :], words[:, u, :], ident[:])
             turned.append(bank)
-            if pg == 1:
-                v_first = keep.tile([P, DV], U32, name="v_first", tag="k_codes1", align_bytes=64)
-                nc.vector.tensor_copy(v_first[:], v_pool[:].bitcast(U32).indirect(entries_of(voffs_sb, 0)))
+            if pg == 0:
+                v_head = keep.tile([P, last * DV], U32, name="v_head", align_bytes=64)
+                nc.vector.tensor_copy(v_head[:], v_pool[:].bitcast(U32).indirect(entries_of(voffs_sb, 0, last)))
 
+        v_last = laid.tile([P, DV], U32, name="v_last", offset=AT_VS + 4 * PAGE * last, align_bytes=64)
+        nc.vector.tensor_copy(v_last[:], v_pool[:].bitcast(U32).indirect(entries_of(voffs_sb, last)))
         acc = psum.tile([P, DV], F32, name="acc")
         for pg in range(PAGES):
-            if pg:
-                grouped = keep.tile([P, NQ * 4], BF16, name="grouped%d" % pg, align_bytes=64)
-            else:
-                grouped = laid.tile([P, NQ * 4], BF16, name="grouped0", offset=AT_LAST, align_bytes=64)
+            grouped = laid.tile([P, NQ * 4], BF16, name="grouped%d" % pg, offset=AT_FIRST + 8 * NQ * pg if pg < last else AT_VS + 4 * PAGE * last + 4 * DV, align_bytes=64)
             nc.scalar.copy(grouped[:].bitcast(F32).rearrange("p (q u) -> p q u", u=2), turned[pg][:].rearrange("p u q -> p q u"))
-            if pg == 0:
-                v_got = v_first[:]
-            else:
-                v_next = laid.tile([P, DV], U32, name="v_next%d" % pg, offset=AT_VS if pg < last else AT_LAST, align_bytes=64)
-                nc.vector.tensor_copy(v_next[:], v_pool[:].bitcast(U32).indirect(entries_of(voffs_sb, pg)))
-                v_got = v_next[:]
+            v_got = v_head[:, pg * DV : (pg + 1) * DV] if pg < last else v_last[:]
             w_codes = keep.tile([P, NQ], U32, name="w_codes%d" % pg, align_bytes=64)
             w_plane = keep.tile([P, NQ], U8, name="w_plane%d" % pg, align_bytes=64)
             nc.vector.quantize_mx(out=w_codes[:].bitcast(FP8X4), scales=w_plane[:], in_=grouped[:])

@@ -9,6 +9,7 @@ PAGE = 512
 PAGES = N // PAGE
 POOL_PAGES = T // PAGE
 PASSES = D // 512
+PARTS = 4
 QUADS = 4
 BLOCKS = 16
 LIST_ROWS = 16
@@ -16,8 +17,7 @@ QUAD = P // QUADS
 ROWS = BLOCKS // QUADS
 BANK_TURNS = 4
 TURN_BANKS = PAGES
-AT_VS = 4096
-AT_FIRST = AT_VS + 4 * T
+VS_HEAD = N // 2
 OUT_SCALE = 1.0 / 16.0
 FLOPS = 2 * NQ * N * (D + DV)
 
@@ -38,7 +38,6 @@ def tile_attend_pkv4q_silu_kernel(tc, q_words, q_scales, k_words, k_scales, v_wo
     last = PAGES - 1
     with ExitStack() as ctx:
         keep = ctx.enter_context(tc.tile_pool(name="keep", bufs=1))
-        laid = ctx.enter_context(tc.tile_pool(name="laid", bufs=1))
         psum = ctx.enter_context(tc.psum_pool(name="psum", bufs=1))
 
         offs_sb = keep.tile([P, N // LIST_ROWS], U16, name="offs_sb")
@@ -49,7 +48,7 @@ def tile_attend_pkv4q_silu_kernel(tc, q_words, q_scales, k_words, k_scales, v_wo
         vsc_pool = keep.tile([P, POOL_PAGES * DV], U8, name="vsc_pool", tag="value_pool", align_bytes=64)
         vsc_plane = keep.tile([P, PAGES * DV], U8, name="vsc_plane", align_bytes=64)
         ks_planes = keep.tile([P, PASSES, N], U8, name="ks_planes", align_bytes=64)
-        vs_pool = laid.tile([P, T], F32, name="vs_pool", offset=AT_VS, align_bytes=64)
+        vs_pool = keep.tile([P, T], F32, name="vs_pool", align_bytes=64)
         q_codes = keep.tile([P, PASSES, NQ], I32, name="q_codes", align_bytes=64)
         q_planes = keep.tile([P, PASSES * NQ], U8, name="q_planes", align_bytes=64)
         ident = keep.tile([P, P], F32, name="ident")
@@ -110,22 +109,16 @@ def tile_attend_pkv4q_silu_kernel(tc, q_words, q_scales, k_words, k_scales, v_wo
 
         k_gots = []
         for pg in range(PAGES):
-            if pg < last:
-                k_got = keep.tile([P, PAGE], U32, name="k_got%d" % pg, align_bytes=64)
-            else:
-                k_got = laid.tile([P, PAGE], U32, name="k_got%d" % pg, offset=0, align_bytes=64)
+            k_got = keep.tile([P, PAGE], U32, name="k_got%d" % pg, align_bytes=64)
             nc.vector.tensor_copy(k_got[:], k_pool[:].bitcast(U32).indirect(entries_of(offs_sb, pg)))
             k_gots.append(k_got)
-        vs_head = keep.tile([P, last, PAGE], F32, name="vs_head", tag="key_pool", align_bytes=64)
-        nc.scalar.activation(vs_head[:].rearrange("p g s -> p (g s)"), vs_pool[:].indirect(entries_of(offs_sb, 0, last)), ACT.Copy)
+        vs_head = keep.tile([P, VS_HEAD], F32, name="vs_head", tag="key_pool", align_bytes=64)
+        nc.scalar.activation(vs_head[:], vs_pool[:].indirect(offs_sb[:, : VS_HEAD // LIST_ROWS]), ACT.Copy)
 
-        score_banks = []
+        p_tiles = []
         for pg in range(PAGES):
             by_pass = k_gots[pg][:].bitcast(U16).rearrange("p (n o) -> p o n", o=PASSES)
-            if pg:
-                k_codes = keep.tile([P, PASSES, 2 * PAGE], U8, name="k_codes%d" % pg, align_bytes=64)
-            else:
-                k_codes = laid.tile([P, PASSES, 2 * PAGE], U8, name="k_codes0", offset=AT_FIRST, align_bytes=64)
+            k_codes = keep.tile([P, PASSES, 2 * PAGE], U8, name="k_codes%d" % pg, align_bytes=64)
             if pg in (0, last):
                 for o in range(PASSES):
                     nc.vector.tensor_copy(k_codes[:, o, :].bitcast(U16), by_pass[:, o, :])
@@ -142,49 +135,50 @@ def tile_attend_pkv4q_silu_kernel(tc, q_words, q_scales, k_words, k_scales, v_wo
                     start=(o == 0),
                     stop=(o == PASSES - 1),
                 )
-            score_banks.append(scores)
-
-        p_tiles = []
-        for pg in range(PAGES):
-            if pg == 0:
-                p_sb = keep.tile([P, PAGE], F32, name="p0", align_bytes=64)
-            else:
-                p_sb = laid.tile([P, PAGE], F32, name="p%d" % pg, offset=AT_VS + 4 * PAGE * pg, align_bytes=64)
-            nc.scalar.activation(p_sb[:], score_banks[pg][:], ACT.Silu)
+            p_sb = keep.tile([P, PAGE], F32, name="p%d" % pg, align_bytes=64)
+            nc.scalar.activation(p_sb[:], scores[:], ACT.Silu)
             p_tiles.append(p_sb)
-            if pg == 0:
-                vs_last = laid.tile([P, PAGE], F32, name="vs_last", offset=AT_FIRST, align_bytes=64)
-                nc.scalar.activation(vs_last[:], vs_pool[:].indirect(entries_of(offs_sb, last)), ACT.Copy)
+
+        vs_tail = keep.tile([P, N - VS_HEAD], F32, name="vs_tail", tag="k_got1", align_bytes=64)
+        nc.vector.tensor_copy(vs_tail[:], vs_pool[:].indirect(offs_sb[:, VS_HEAD // LIST_ROWS :]))
 
         turned = []
         for pg in range(PAGES):
-            w_tile = laid.tile([P, PAGE], BF16, name="w_bf%d" % pg, offset=2 * PAGE * pg, align_bytes=64)
-            w_bf = w_tile[:]
-            nc.vector.tensor_tensor(w_bf, p_tiles[pg][:], vs_head[:, pg, :] if pg < last else vs_last[:], MULT)
-            words = w_bf.bitcast(F32).rearrange("p (s u) -> p u s", u=2)
+            w_bf = keep.tile([P, PAGE], BF16, name="w_bf", tag="w_bf%d" % pg if pg else "k_got%d" % last, align_bytes=64)
+            first, end = pg * PAGE, (pg + 1) * PAGE
+            cut = min(max(VS_HEAD, first), end)
+            if cut > first:
+                nc.vector.tensor_tensor(w_bf[:, : cut - first], p_tiles[pg][:, : cut - first], vs_head[:, first:cut], MULT)
+            if cut < end:
+                nc.vector.tensor_tensor(w_bf[:, cut - first :], p_tiles[pg][:, cut - first :], vs_tail[:, cut - VS_HEAD : end - VS_HEAD], MULT)
+            words = w_bf[:].bitcast(F32).rearrange("p (s u) -> p u s", u=2)
             bank = psum.tile([P, 2, NQ], F32, name="bank", tag="bank%d" % pg)
             for u in range(2):
                 nc.tensor.transpose(bank[:, u, :], words[:, u, :], ident[:])
             turned.append(bank)
-            if pg == 0:
-                v_head = keep.tile([P, last * DV], U32, name="v_head", align_bytes=64)
-                nc.vector.tensor_copy(v_head[:], v_pool[:].bitcast(U32).indirect(entries_of(voffs_sb, 0, last)))
 
-        v_last = laid.tile([P, DV], U32, name="v_last", offset=AT_VS + 4 * PAGE * last, align_bytes=64)
-        nc.vector.tensor_copy(v_last[:], v_pool[:].bitcast(U32).indirect(entries_of(voffs_sb, last)))
-        acc = psum.tile([P, DV], F32, name="acc")
-        for pg in range(PAGES):
-            grouped = laid.tile([P, NQ * 4], BF16, name="grouped%d" % pg, offset=AT_FIRST + 8 * NQ * pg if pg < last else AT_VS + 4 * PAGE * last + 4 * DV, align_bytes=64)
+        def quantise(pg):
+            tag = "grouped%d" % pg if pg else "k_codes%d" % last
+            grouped = keep.tile([P, NQ * PARTS], BF16, name="grouped", tag=tag, align_bytes=64)
             nc.scalar.copy(grouped[:].bitcast(F32).rearrange("p (q u) -> p q u", u=2), turned[pg][:].rearrange("p u q -> p q u"))
-            v_got = v_head[:, pg * DV : (pg + 1) * DV] if pg < last else v_last[:]
             w_codes = keep.tile([P, NQ], U32, name="w_codes%d" % pg, align_bytes=64)
             w_plane = keep.tile([P, NQ], U8, name="w_plane%d" % pg, align_bytes=64)
             nc.vector.quantize_mx(out=w_codes[:].bitcast(FP8X4), scales=w_plane[:], in_=grouped[:])
+            return w_codes, w_plane
+
+        weights = [quantise(pg) for pg in range(last)]
+        v_got = keep.tile([P, PAGES, DV], U32, name="v_got", tag="p%d" % last, align_bytes=64)
+        for pg in range(PAGES):
+            nc.vector.tensor_copy(v_got[:, pg, :], v_pool[:].bitcast(U32).indirect(entries_of(voffs_sb, pg)))
+        weights.append(quantise(last))
+        acc = psum.tile([P, DV], F32, name="acc")
+        for pg in range(PAGES):
+            w_codes, w_plane = weights[pg]
             nc.tensor.matmul_mx(
                 out=acc[:],
                 lhsT=w_codes[:].bitcast(FP8X4),
                 lhsT_scale=w_plane[:],
-                rhs=v_got.bitcast(FP8X4),
+                rhs=v_got[:, pg, :].bitcast(FP8X4),
                 rhs_scale=vsc_plane[:, pg * DV : (pg + 1) * DV],
                 start=(pg == 0),
                 stop=(pg == last),

@@ -1,7 +1,6 @@
 from contextlib import ExitStack
 
 import concourse.mybir as mybir
-from concourse.masks import make_identity
 
 NQ, N, T, D, DV = 128, 1536, 4096, 1024, 256
 P = 128
@@ -15,9 +14,7 @@ BLOCKS = 16
 LIST_ROWS = 16
 QUAD = P // QUADS
 ROWS = BLOCKS // QUADS
-BANK_TURNS = 4
-TURN_BANKS = PAGES
-VS_HEAD = N // 2
+RUN = 4
 OUT_SCALE = 1.0 / 16.0
 FLOPS = 2 * NQ * N * (D + DV)
 
@@ -38,38 +35,36 @@ def tile_attend_pkv4q_silu_kernel(tc, q_words, q_scales, k_words, k_scales, v_wo
     last = PAGES - 1
     with ExitStack() as ctx:
         keep = ctx.enter_context(tc.tile_pool(name="keep", bufs=1))
+        laid = ctx.enter_context(tc.tile_pool(name="laid", bufs=1))
         psum = ctx.enter_context(tc.psum_pool(name="psum", bufs=1))
 
         offs_sb = keep.tile([P, N // LIST_ROWS], U16, name="offs_sb")
         voffs_sb = keep.tile([P, PAGES * DV // LIST_ROWS], U16, name="voffs_sb")
-        vs_rows = keep.tile([P, T // P], F32, name="vs_rows")
+        vs_parts = keep.tile([P, POOL_PAGES, PARTS], F32, name="vs_parts")
         k_pool = keep.tile([P, T], I32, name="k_pool", tag="key_pool", align_bytes=64)
         ks_pool = keep.tile([P, T], U8, name="ks_pool")
-        vsc_pool = keep.tile([P, POOL_PAGES * DV], U8, name="vsc_pool", tag="value_pool", align_bytes=64)
-        vsc_plane = keep.tile([P, PAGES * DV], U8, name="vsc_plane", align_bytes=64)
+        vsc_pool = keep.tile([P, POOL_PAGES * DV], U8, name="vsc_pool", align_bytes=64)
         ks_planes = keep.tile([P, PASSES, N], U8, name="ks_planes", align_bytes=64)
         vs_pool = keep.tile([P, T], F32, name="vs_pool", align_bytes=64)
         q_codes = keep.tile([P, PASSES, NQ], I32, name="q_codes", align_bytes=64)
         q_planes = keep.tile([P, PASSES * NQ], U8, name="q_planes", align_bytes=64)
-        ident = keep.tile([P, P], F32, name="ident")
 
-        vsc_first = P - BLOCKS
+        ks_first = P - QUAD
+        vsc_first = 2 * QUAD - BLOCKS
         warm_in = keep.tile([P, 1], F32, name="warm_in")
         nc.vector.memset(warm_in[:], 0.0)
-        nc.vector.memset(q_planes[:].bitcast(I32), 0)
-        nc.vector.memset(ks_pool[QUAD : 2 * QUAD, :].bitcast(I32), 0)
-        nc.vector.memset(ks_pool[2 * QUAD : P, :].bitcast(I32), 0)
         nc.vector.memset(vsc_pool[0:vsc_first, :].bitcast(I32), 0)
-        make_identity(nc, ident[:])
+        nc.vector.memset(vsc_pool[2 * QUAD : P, :].bitcast(I32), 0)
+        nc.vector.memset(ks_pool[0:ks_first, :].bitcast(I32), 0)
 
-        nc.sync.dma_start(vs_rows[:], vs[0].rearrange("(p c) -> p c", p=P))
-        nc.sync.dma_start(offs_sb[:], offs)
-        nc.scalar.dma_start(ks_pool[0:QUAD, :].bitcast(I32), k_scales.bitcast(I32).rearrange("o f t -> f o t"))
         nc.sync.dma_start(voffs_sb[:], voffs)
         nc.scalar.dma_start(
-            vsc_pool[vsc_first:P, :].bitcast(I32).rearrange("f (u e) -> f u e", u=POOL_PAGES),
+            vsc_pool[vsc_first : 2 * QUAD, :].bitcast(I32).rearrange("f (u e) -> f u e", u=POOL_PAGES),
             v_scales.bitcast(I32).rearrange("u f e -> f u e"),
         )
+        nc.sync.dma_start(vs_parts[:], vs[0].rearrange("(u p t) -> p u t", p=P, t=PARTS))
+        nc.scalar.dma_start(ks_pool[ks_first:P, :].bitcast(I32), k_scales.bitcast(I32).rearrange("o f t -> f o t"))
+        nc.sync.dma_start(offs_sb[:], offs)
         nc.sync.dma_start(k_pool[:], k_words[0].rearrange("g t b -> g (t b)").bitcast(I32))
         nc.sync.dma_start(q_codes[:], q_words[0].rearrange("o g q r -> g o (q r)").bitcast(I32))
         for quad in range(QUADS):
@@ -82,95 +77,87 @@ def tile_attend_pkv4q_silu_kernel(tc, q_words, q_scales, k_words, k_scales, v_wo
         warm = keep.tile([P, 1], F32, name="warm")
         nc.scalar.activation(warm[:], warm_in[:], ACT.Silu)
 
-        vs_by_bank = vs_pool[:].rearrange("p (n b m) -> p b n m", b=T // P // BANK_TURNS, m=BANK_TURNS)
-        for b in range(T // P // BANK_TURNS):
-            spread = psum.tile([P, BANK_TURNS, P], F32, name="spread", tag="bank%d" % (b % TURN_BANKS))
-            for m in range(BANK_TURNS):
-                c = BANK_TURNS * b + m
-                nc.tensor.transpose(spread[:, m, :], vs_rows[:, c : c + 1].to_broadcast([P, P]), ident[:])
-            nc.scalar.activation(vs_by_bank[:, b], spread[:].rearrange("p m n -> p n m"), ACT.Copy)
+        nc.scalar.activation(
+            vs_pool[:].rearrange("p (u q t) -> p u q t", u=POOL_PAGES, t=PARTS),
+            vs_parts[:].unsqueeze(2).to_broadcast([P, POOL_PAGES, NQ, PARTS]),
+            ACT.Copy,
+        )
 
-        ks_got = keep.tile([P, N], U8, name="ks_got", align_bytes=64)
-        nc.vector.tensor_copy(ks_got[:], ks_pool[:].indirect(offs_sb[:]))
-        for quad in range(QUADS):
-            rows = slice(PASSES * ROWS * quad, PASSES * ROWS * (quad + 1))
-            nc.sync.dma_start(ks_planes[QUAD * quad : QUAD * quad + ROWS].bitcast(I32), ks_got[rows, :].bitcast(I32))
         vsc_got = keep.tile([P, PAGES * DV], U8, name="vsc_got", align_bytes=64)
         nc.vector.tensor_copy(vsc_got[:], vsc_pool[:].indirect(voffs_sb[:]))
-        v_pool = keep.tile([P, POOL_PAGES * DV], I32, name="v_pool", tag="value_pool", align_bytes=64)
+        ks_got = keep.tile([P, N], U8, name="ks_got", align_bytes=64)
+        nc.vector.tensor_copy(ks_got[:], ks_pool[:].indirect(offs_sb[:]))
+        ks_dealt = keep.tile([P, N], U8, name="ks_dealt", align_bytes=64)
+        nc.vector.tensor_copy(
+            ks_dealt[:].rearrange("p (g t s) -> p t g s", g=PAGES, t=PARTS),
+            ks_got[:].rearrange("p (g s t) -> p t g s", g=PAGES, t=PARTS),
+        )
+        for quad in range(QUADS):
+            rows = slice(ks_first + PASSES * ROWS * quad, ks_first + PASSES * ROWS * (quad + 1))
+            nc.sync.dma_start(ks_planes[QUAD * quad : QUAD * quad + ROWS].bitcast(I32), ks_dealt[rows, :].bitcast(I32))
+        v_pool = keep.tile([P, POOL_PAGES * DV], I32, name="v_pool", tag="ks_got", align_bytes=64)
         nc.sync.dma_start(v_pool[:].rearrange("p (u e) -> p u e", e=DV), v_words.rearrange("u g e r -> g u (e r)").bitcast(I32))
+        vsc_plane = keep.tile([P, PAGES * DV], U8, name="vsc_plane", tag="ks_dealt", align_bytes=64)
         for quad in range(QUADS):
             rows = slice(vsc_first + ROWS * quad, vsc_first + ROWS * (quad + 1))
             nc.sync.dma_start(vsc_plane[QUAD * quad : QUAD * quad + ROWS, :].bitcast(I32), vsc_got[rows, :].bitcast(I32))
 
-        def entries_of(list_sb, pg, count=1):
+        def entries_of(list_sb, pg):
             width = list_sb.shape[1] // PAGES
-            return list_sb[:, pg * width : (pg + count) * width]
+            return list_sb[:, pg * width : (pg + 1) * width]
 
-        k_gots = []
+        vs_got = keep.tile([P, N], F32, name="vs_got", align_bytes=64)
+        nc.scalar.activation(vs_got[:], vs_pool[:].indirect(offs_sb[:]), ACT.Copy)
+
+        p_all = keep.tile([P, PAGES, NQ * PARTS], F32, name="p_all", tag="vs_pool", align_bytes=64)
         for pg in range(PAGES):
-            k_got = keep.tile([P, PAGE], U32, name="k_got%d" % pg, align_bytes=64)
+            k_got = laid.tile([P, PAGE], U32, name="k_got%d" % pg, offset=pg * 4 * PAGE, align_bytes=64)
             nc.vector.tensor_copy(k_got[:], k_pool[:].bitcast(U32).indirect(entries_of(offs_sb, pg)))
-            k_gots.append(k_got)
-        vs_head = keep.tile([P, VS_HEAD], F32, name="vs_head", tag="key_pool", align_bytes=64)
-        nc.scalar.activation(vs_head[:], vs_pool[:].indirect(offs_sb[:, : VS_HEAD // LIST_ROWS]), ACT.Copy)
-
-        p_tiles = []
-        for pg in range(PAGES):
-            by_pass = k_gots[pg][:].bitcast(U16).rearrange("p (n o) -> p o n", o=PASSES)
-            k_codes = keep.tile([P, PASSES, 2 * PAGE], U8, name="k_codes%d" % pg, align_bytes=64)
-            if pg in (0, last):
+            k_codes = keep.tile([P, PARTS, PASSES, 2 * P], U8, name="k_codes%d" % pg, align_bytes=64)
+            dealt = k_codes[:].bitcast(U16).rearrange("p t o (b s) -> p t b o s", s=RUN)
+            words = k_got[:].bitcast(U16).rearrange("p (b s t o) -> p t b o s", s=RUN, t=PARTS, o=PASSES)
+            halves = 2 if pg == last else 1
+            for h in range(halves):
+                ts = slice(h * PARTS // halves, (h + 1) * PARTS // halves)
+                nc.vector.tensor_copy(dealt[:, ts], words[:, ts])
+            scores = psum.tile([P, PARTS, NQ], F32, name="scores%d" % pg)
+            for t in range(PARTS):
                 for o in range(PASSES):
-                    nc.vector.tensor_copy(k_codes[:, o, :].bitcast(U16), by_pass[:, o, :])
-            else:
-                nc.vector.tensor_copy(k_codes[:].bitcast(U16), by_pass)
-            scores = psum.tile([P, PAGE], F32, name="scores", tag="scores%d" % pg)
-            for o in range(PASSES):
-                nc.tensor.matmul_mx(
-                    out=scores[:],
-                    lhsT=q_codes[:, o, :].bitcast(FP8X4),
-                    lhsT_scale=q_planes[:, o * NQ : (o + 1) * NQ],
-                    rhs=k_codes[:, o, :].bitcast(FP4X4),
-                    rhs_scale=ks_planes[:, o, pg * PAGE : (pg + 1) * PAGE],
-                    start=(o == 0),
-                    stop=(o == PASSES - 1),
-                )
-            p_sb = keep.tile([P, PAGE], F32, name="p%d" % pg, align_bytes=64)
-            nc.scalar.activation(p_sb[:], scores[:], ACT.Silu)
-            p_tiles.append(p_sb)
+                    first = pg * PAGE + t * P
+                    nc.tensor.matmul_mx(
+                        out=scores[:, t, :],
+                        lhsT=k_codes[:, t, o, :].bitcast(FP4X4),
+                        lhsT_scale=ks_planes[:, o, first : first + P],
+                        rhs=q_codes[:, o, :].bitcast(FP8X4),
+                        rhs_scale=q_planes[:, o * NQ : (o + 1) * NQ],
+                        start=(o == 0),
+                        stop=(o == PASSES - 1),
+                    )
+            nc.scalar.activation(p_all[:, pg].rearrange("p (q t) -> p q t", t=PARTS), scores[:].rearrange("p t q -> p q t"), ACT.Silu)
 
-        vs_tail = keep.tile([P, N - VS_HEAD], F32, name="vs_tail", tag="k_got1", align_bytes=64)
-        nc.vector.tensor_copy(vs_tail[:], vs_pool[:].indirect(offs_sb[:, VS_HEAD // LIST_ROWS :]))
+        def weigh(pg):
+            w_bf = keep.tile([P, PAGE], BF16, name="w_bf%d" % pg, align_bytes=64)
+            nc.vector.tensor_tensor(w_bf[:], p_all[:, pg], vs_got[:, pg * PAGE : (pg + 1) * PAGE], MULT)
+            return w_bf
 
-        turned = []
-        for pg in range(PAGES):
-            w_bf = keep.tile([P, PAGE], BF16, name="w_bf", tag="w_bf%d" % pg if pg else "k_got%d" % last, align_bytes=64)
-            first, end = pg * PAGE, (pg + 1) * PAGE
-            cut = min(max(VS_HEAD, first), end)
-            if cut > first:
-                nc.vector.tensor_tensor(w_bf[:, : cut - first], p_tiles[pg][:, : cut - first], vs_head[:, first:cut], MULT)
-            if cut < end:
-                nc.vector.tensor_tensor(w_bf[:, cut - first :], p_tiles[pg][:, cut - first :], vs_tail[:, cut - VS_HEAD : end - VS_HEAD], MULT)
-            words = w_bf[:].bitcast(F32).rearrange("p (s u) -> p u s", u=2)
-            bank = psum.tile([P, 2, NQ], F32, name="bank", tag="bank%d" % pg)
-            for u in range(2):
-                nc.tensor.transpose(bank[:, u, :], words[:, u, :], ident[:])
-            turned.append(bank)
-
-        def quantise(pg):
-            tag = "grouped%d" % pg if pg else "k_codes%d" % last
-            grouped = keep.tile([P, NQ * PARTS], BF16, name="grouped", tag=tag, align_bytes=64)
-            nc.scalar.copy(grouped[:].bitcast(F32).rearrange("p (q u) -> p q u", u=2), turned[pg][:].rearrange("p u q -> p q u"))
+        def quantise(pg, w_bf):
             w_codes = keep.tile([P, NQ], U32, name="w_codes%d" % pg, align_bytes=64)
             w_plane = keep.tile([P, NQ], U8, name="w_plane%d" % pg, align_bytes=64)
-            nc.vector.quantize_mx(out=w_codes[:].bitcast(FP8X4), scales=w_plane[:], in_=grouped[:])
+            nc.vector.quantize_mx(out=w_codes[:].bitcast(FP8X4), scales=w_plane[:], in_=w_bf[:])
             return w_codes, w_plane
 
-        weights = [quantise(pg) for pg in range(last)]
-        v_got = keep.tile([P, PAGES, DV], U32, name="v_got", tag="p%d" % last, align_bytes=64)
-        for pg in range(PAGES):
+        v_got = laid.tile([P, PAGES, DV], U32, name="v_got", offset=last * 4 * PAGE, align_bytes=64)
+
+        def values(pg):
             nc.vector.tensor_copy(v_got[:, pg, :], v_pool[:].bitcast(U32).indirect(entries_of(voffs_sb, pg)))
-        weights.append(quantise(last))
+
+        values(0)
+        w_0 = weigh(0)
+        values(1)
+        weights = [quantise(0, w_0)]
+        values(2)
+        w_bfs = [weigh(pg) for pg in range(1, PAGES)]
+        weights.extend(quantise(pg, w_bfs[pg - 1]) for pg in range(1, PAGES))
         acc = psum.tile([P, DV], F32, name="acc")
         for pg in range(PAGES):
             w_codes, w_plane = weights[pg]

@@ -84,9 +84,11 @@ def tile_attend_pkv4q_silu_kernel(tc, q_words, q_scales, k_words, k_scales, v_wo
         )
 
         vsc_got = keep.tile([P, PAGES * DV], U8, name="vsc_got", align_bytes=64)
-        nc.vector.tensor_copy(vsc_got[:], vsc_pool[:].indirect(voffs_sb[:]))
+        half = PAGES * DV // 2
+        nc.vector.tensor_copy(vsc_got[:, :half], vsc_pool[:].indirect(voffs_sb[:, : half // LIST_ROWS]))
         ks_got = keep.tile([P, N], U8, name="ks_got", align_bytes=64)
         nc.vector.tensor_copy(ks_got[:], ks_pool[:].indirect(offs_sb[:]))
+        nc.vector.tensor_copy(vsc_got[:, half:], vsc_pool[:].indirect(voffs_sb[:, half // LIST_ROWS :]))
         ks_dealt = keep.tile([P, N], U8, name="ks_dealt", align_bytes=64)
         nc.vector.tensor_copy(
             ks_dealt[:].rearrange("p (g t s) -> p t g s", g=PAGES, t=PARTS),
@@ -114,12 +116,13 @@ def tile_attend_pkv4q_silu_kernel(tc, q_words, q_scales, k_words, k_scales, v_wo
             k_got = laid.tile([P, PAGE], U32, name="k_got%d" % pg, offset=pg * 4 * PAGE, align_bytes=64)
             nc.vector.tensor_copy(k_got[:], k_pool[:].bitcast(U32).indirect(entries_of(offs_sb, pg)))
             k_codes = keep.tile([P, PARTS, PASSES, 2 * P], U8, name="k_codes%d" % pg, align_bytes=64)
-            dealt = k_codes[:].bitcast(U16).rearrange("p t o (b s) -> p t b o s", s=RUN)
-            words = k_got[:].bitcast(U16).rearrange("p (b s t o) -> p t b o s", s=RUN, t=PARTS, o=PASSES)
-            halves = 2 if pg == last else 1
-            for h in range(halves):
-                ts = slice(h * PARTS // halves, (h + 1) * PARTS // halves)
-                nc.vector.tensor_copy(dealt[:, ts], words[:, ts])
+            dealt = k_codes[:].bitcast(U16).rearrange("p (h t) o s -> p h s (t o)", h=2)
+            words = k_got[:].bitcast(U16).rearrange("p (s h r) -> p h s r", h=2, r=RUN)
+            if pg == last:
+                for h in range(2):
+                    nc.vector.tensor_copy(dealt[:, h], words[:, h])
+            else:
+                nc.vector.tensor_copy(dealt, words)
             scores = psum.tile([P, PARTS, NQ], F32, name="scores%d" % pg)
             for t in range(PARTS):
                 for o in range(PASSES):
@@ -146,7 +149,7 @@ def tile_attend_pkv4q_silu_kernel(tc, q_words, q_scales, k_words, k_scales, v_wo
             nc.vector.quantize_mx(out=w_codes[:].bitcast(FP8X4), scales=w_plane[:], in_=w_bf[:])
             return w_codes, w_plane
 
-        v_got = laid.tile([P, PAGES, DV], U32, name="v_got", offset=last * 4 * PAGE, align_bytes=64)
+        v_got = laid.tile([P, PAGES, DV], U32, name="v_got", offset=0, align_bytes=64)
 
         def values(pg):
             nc.vector.tensor_copy(v_got[:, pg, :], v_pool[:].bitcast(U32).indirect(entries_of(voffs_sb, pg)))

@@ -1,6 +1,7 @@
 from contextlib import ExitStack
 
 import concourse.mybir as mybir
+from concourse.masks import make_identity
 
 NQ, N, T, D, DV = 128, 1536, 4096, 1024, 256
 P = 128
@@ -40,7 +41,9 @@ def tile_attend_pkv4q_silu_kernel(tc, q_words, q_scales, k_words, k_scales, v_wo
 
         offs_sb = keep.tile([P, N // LIST_ROWS], U16, name="offs_sb")
         voffs_sb = keep.tile([P, PAGES * DV // LIST_ROWS], U16, name="voffs_sb")
-        vs_parts = keep.tile([P, POOL_PAGES, PARTS], F32, name="vs_parts")
+        vs_rows = keep.tile([P, PAGE], F32, name="vs_rows")
+        ident = keep.tile([P, P], F32, name="ident")
+        make_identity(nc, ident[:])
         k_pool = keep.tile([P, T], I32, name="k_pool", tag="key_pool", align_bytes=64)
         ks_pool = keep.tile([P, T], U8, name="ks_pool")
         vsc_pool = keep.tile([P, POOL_PAGES * DV], U8, name="vsc_pool", align_bytes=64)
@@ -57,12 +60,12 @@ def tile_attend_pkv4q_silu_kernel(tc, q_words, q_scales, k_words, k_scales, v_wo
         nc.vector.memset(vsc_pool[2 * QUAD : P, :].bitcast(I32), 0)
         nc.vector.memset(ks_pool[0:ks_first, :].bitcast(I32), 0)
 
+        nc.sync.dma_start(vs_rows[0:POOL_PAGES, :], vs[0].rearrange("(u n) -> u n", n=PAGE))
         nc.sync.dma_start(voffs_sb[:], voffs)
         nc.scalar.dma_start(
             vsc_pool[vsc_first : 2 * QUAD, :].bitcast(I32).rearrange("f (u e) -> f u e", u=POOL_PAGES),
             v_scales.bitcast(I32).rearrange("u f e -> f u e"),
         )
-        nc.sync.dma_start(vs_parts[:], vs[0].rearrange("(u p t) -> p u t", p=P, t=PARTS))
         nc.scalar.dma_start(ks_pool[ks_first:P, :].bitcast(I32), k_scales.bitcast(I32).rearrange("o f t -> f o t"))
         nc.sync.dma_start(offs_sb[:], offs)
         nc.sync.dma_start(k_pool[:], k_words[0].rearrange("g t b -> g (t b)").bitcast(I32))
@@ -77,9 +80,12 @@ def tile_attend_pkv4q_silu_kernel(tc, q_words, q_scales, k_words, k_scales, v_wo
         warm = keep.tile([P, 1], F32, name="warm")
         nc.scalar.activation(warm[:], warm_in[:], ACT.Silu)
 
+        vs_cols = psum.tile([P, PARTS, P], F32, name="vs_cols")
+        for t in range(PARTS):
+            nc.tensor.transpose(vs_cols[:, t, :], vs_rows[:].rearrange("p (s t) -> p t s", t=PARTS)[:, t, :], ident[:])
         nc.scalar.activation(
             vs_pool[:].rearrange("p (u q t) -> p u q t", u=POOL_PAGES, t=PARTS),
-            vs_parts[:].unsqueeze(2).to_broadcast([P, POOL_PAGES, NQ, PARTS]),
+            vs_cols[:, :, 0:POOL_PAGES].rearrange("p t u -> p u t").unsqueeze(2).to_broadcast([P, POOL_PAGES, NQ, PARTS]),
             ACT.Copy,
         )
 

@@ -118,9 +118,16 @@ def tile_attend_pkv4q_silu_kernel(tc, q_words, q_scales, k_words, k_scales, v_wo
         nc.scalar.activation(vs_got[:], vs_pool[:].indirect(offs_sb[:]), ACT.Copy)
 
         p_all = keep.tile([P, PAGES, NQ * PARTS], F32, name="p_all", tag="vs_pool", align_bytes=64)
-        for pg in range(PAGES):
+        def gather_keys(pg):
             k_got = laid.tile([P, PAGE], U32, name="k_got%d" % pg, offset=pg * 4 * PAGE, align_bytes=64)
             nc.vector.tensor_copy(k_got[:], k_pool[:].bitcast(U32).indirect(entries_of(offs_sb, pg)))
+            return k_got
+
+        k_gots = [gather_keys(0)]
+        for pg in range(PAGES):
+            if pg < last:
+                k_gots.append(gather_keys(pg + 1))
+            k_got = k_gots[pg]
             k_codes = keep.tile([P, PARTS, PASSES, 2 * P], U8, name="k_codes%d" % pg, align_bytes=64)
             dealt = k_codes[:].bitcast(U16).rearrange("p (h t) o s -> p h s (t o)", h=2)
             words = k_got[:].bitcast(U16).rearrange("p (s h r) -> p h s r", h=2, r=RUN)

@@ -46,7 +46,7 @@ def tile_attend_pkv4q_silu_kernel(tc, q_words, q_scales, k_words, k_scales, v_wo
         make_identity(nc, ident[:])
         k_pool = keep.tile([P, T], I32, name="k_pool", tag="key_pool", align_bytes=64)
         ks_pool = keep.tile([P, T], U8, name="ks_pool")
-        vsc_pool = keep.tile([P, POOL_PAGES * DV], U8, name="vsc_pool", align_bytes=64)
+        vsc_pool = keep.tile([P, POOL_PAGES * DV], U8, name="vsc_pool", tag="value_pool", align_bytes=64)
         ks_planes = keep.tile([P, PASSES, N], U8, name="ks_planes", align_bytes=64)
         vs_pool = keep.tile([P, T], F32, name="vs_pool", align_bytes=64)
         q_codes = keep.tile([P, PASSES, NQ], I32, name="q_codes", align_bytes=64)
@@ -56,18 +56,18 @@ def tile_attend_pkv4q_silu_kernel(tc, q_words, q_scales, k_words, k_scales, v_wo
         vsc_first = 2 * QUAD - BLOCKS
         warm_in = keep.tile([P, 1], F32, name="warm_in")
         nc.vector.memset(warm_in[:], 0.0)
+        nc.vector.memset(ks_pool[0:ks_first, :].bitcast(I32), 0)
         nc.vector.memset(vsc_pool[0:vsc_first, :].bitcast(I32), 0)
         nc.vector.memset(vsc_pool[2 * QUAD : P, :].bitcast(I32), 0)
-        nc.vector.memset(ks_pool[0:ks_first, :].bitcast(I32), 0)
 
         nc.sync.dma_start(vs_rows[0:POOL_PAGES, :], vs[0].rearrange("(u n) -> u n", n=PAGE))
-        nc.sync.dma_start(voffs_sb[:], voffs)
+        nc.scalar.dma_start(ks_pool[ks_first:P, :].bitcast(I32), k_scales.bitcast(I32).rearrange("o f t -> f o t"))
+        nc.sync.dma_start(offs_sb[:], offs)
         nc.scalar.dma_start(
             vsc_pool[vsc_first : 2 * QUAD, :].bitcast(I32).rearrange("f (u e) -> f u e", u=POOL_PAGES),
             v_scales.bitcast(I32).rearrange("u f e -> f u e"),
         )
-        nc.scalar.dma_start(ks_pool[ks_first:P, :].bitcast(I32), k_scales.bitcast(I32).rearrange("o f t -> f o t"))
-        nc.sync.dma_start(offs_sb[:], offs)
+        nc.sync.dma_start(voffs_sb[:], voffs)
         nc.sync.dma_start(k_pool[:], k_words[0].rearrange("g t b -> g (t b)").bitcast(I32))
         nc.sync.dma_start(q_codes[:], q_words[0].rearrange("o g q r -> g o (q r)").bitcast(I32))
         for quad in range(QUADS):
@@ -89,23 +89,24 @@ def tile_attend_pkv4q_silu_kernel(tc, q_words, q_scales, k_words, k_scales, v_wo
             ACT.Copy,
         )
 
-        vsc_got = keep.tile([P, PAGES * DV], U8, name="vsc_got", align_bytes=64)
-        half = PAGES * DV // 2
-        nc.vector.tensor_copy(vsc_got[:, :half], vsc_pool[:].indirect(voffs_sb[:, : half // LIST_ROWS]))
         ks_got = keep.tile([P, N], U8, name="ks_got", align_bytes=64)
-        nc.vector.tensor_copy(ks_got[:], ks_pool[:].indirect(offs_sb[:]))
-        nc.vector.tensor_copy(vsc_got[:, half:], vsc_pool[:].indirect(voffs_sb[:, half // LIST_ROWS :]))
         ks_dealt = keep.tile([P, N], U8, name="ks_dealt", align_bytes=64)
-        nc.vector.tensor_copy(
-            ks_dealt[:].rearrange("p (g t s) -> p t g s", g=PAGES, t=PARTS),
-            ks_got[:].rearrange("p (g s t) -> p t g s", g=PAGES, t=PARTS),
-        )
+        pieces = [slice(0, PAGE), slice(PAGE, N)]
+        for piece in pieces:
+            nc.vector.tensor_copy(ks_got[:, piece], ks_pool[:].indirect(offs_sb[:, piece.start // LIST_ROWS : piece.stop // LIST_ROWS]))
+        for piece in pieces:
+            nc.vector.tensor_copy(
+                ks_dealt[:, piece].rearrange("p (g t s) -> p t g s", s=P, t=PARTS),
+                ks_got[:, piece].rearrange("p (g s t) -> p t g s", s=P, t=PARTS),
+            )
         for quad in range(QUADS):
             rows = slice(ks_first + PASSES * ROWS * quad, ks_first + PASSES * ROWS * (quad + 1))
             nc.sync.dma_start(ks_planes[QUAD * quad : QUAD * quad + ROWS].bitcast(I32), ks_dealt[rows, :].bitcast(I32))
-        v_pool = keep.tile([P, POOL_PAGES * DV], I32, name="v_pool", tag="ks_got", align_bytes=64)
+        vsc_got = keep.tile([P, PAGES * DV], U8, name="vsc_got", align_bytes=64)
+        nc.vector.tensor_copy(vsc_got[:], vsc_pool[:].indirect(voffs_sb[:]))
+        v_pool = keep.tile([P, POOL_PAGES * DV], I32, name="v_pool", tag="value_pool", align_bytes=64)
         nc.sync.dma_start(v_pool[:].rearrange("p (u e) -> p u e", e=DV), v_words.rearrange("u g e r -> g u (e r)").bitcast(I32))
-        vsc_plane = keep.tile([P, PAGES * DV], U8, name="vsc_plane", tag="ks_dealt", align_bytes=64)
+        vsc_plane = keep.tile([P, PAGES * DV], U8, name="vsc_plane", align_bytes=64)
         for quad in range(QUADS):
             rows = slice(vsc_first + ROWS * quad, vsc_first + ROWS * (quad + 1))
             nc.sync.dma_start(vsc_plane[QUAD * quad : QUAD * quad + ROWS, :].bitcast(I32), vsc_got[rows, :].bitcast(I32))

@@ -56,18 +56,18 @@ def tile_attend_pkv4q_silu_kernel(tc, q_words, q_scales, k_words, k_scales, v_wo
         vsc_first = 2 * QUAD - BLOCKS
         warm_in = keep.tile([P, 1], F32, name="warm_in")
         nc.vector.memset(warm_in[:], 0.0)
-        nc.vector.memset(ks_pool[0:ks_first, :].bitcast(I32), 0)
         nc.vector.memset(vsc_pool[0:vsc_first, :].bitcast(I32), 0)
         nc.vector.memset(vsc_pool[2 * QUAD : P, :].bitcast(I32), 0)
+        nc.vector.memset(ks_pool[0:ks_first, :].bitcast(I32), 0)
 
-        nc.sync.dma_start(vs_rows[0:POOL_PAGES, :], vs[0].rearrange("(u n) -> u n", n=PAGE))
-        nc.scalar.dma_start(ks_pool[ks_first:P, :].bitcast(I32), k_scales.bitcast(I32).rearrange("o f t -> f o t"))
-        nc.sync.dma_start(offs_sb[:], offs)
+        nc.sync.dma_start(voffs_sb[:], voffs)
         nc.scalar.dma_start(
             vsc_pool[vsc_first : 2 * QUAD, :].bitcast(I32).rearrange("f (u e) -> f u e", u=POOL_PAGES),
             v_scales.bitcast(I32).rearrange("u f e -> f u e"),
         )
-        nc.sync.dma_start(voffs_sb[:], voffs)
+        nc.sync.dma_start(offs_sb[:], offs)
+        nc.scalar.dma_start(ks_pool[ks_first:P, :].bitcast(I32), k_scales.bitcast(I32).rearrange("o f t -> f o t"))
+        nc.sync.dma_start(vs_rows[0:POOL_PAGES, :], vs[0].rearrange("(u n) -> u n", n=PAGE))
         nc.sync.dma_start(k_pool[:], k_words[0].rearrange("g t b -> g (t b)").bitcast(I32))
         nc.sync.dma_start(q_codes[:], q_words[0].rearrange("o g q r -> g o (q r)").bitcast(I32))
         for quad in range(QUADS):
@@ -89,27 +89,30 @@ def tile_attend_pkv4q_silu_kernel(tc, q_words, q_scales, k_words, k_scales, v_wo
             ACT.Copy,
         )
 
-        ks_got = keep.tile([P, N], U8, name="ks_got", align_bytes=64)
+        vsc_head = keep.tile([P, DV], U8, name="vsc_head", align_bytes=64)
+        nc.vector.tensor_copy(vsc_head[:], vsc_pool[:].indirect(voffs_sb[:, : DV // LIST_ROWS]))
         ks_dealt = keep.tile([P, N], U8, name="ks_dealt", align_bytes=64)
         pieces = [slice(0, PAGE), slice(PAGE, N)]
-        for piece in pieces:
-            nc.vector.tensor_copy(ks_got[:, piece], ks_pool[:].indirect(offs_sb[:, piece.start // LIST_ROWS : piece.stop // LIST_ROWS]))
-        for piece in pieces:
+        ks_gots = [keep.tile([P, piece.stop - piece.start], U8, name="ks_got%d" % i, align_bytes=64) for i, piece in enumerate(pieces)]
+        for piece, ks_got in zip(pieces, ks_gots):
+            nc.vector.tensor_copy(ks_got[:], ks_pool[:].indirect(offs_sb[:, piece.start // LIST_ROWS : piece.stop // LIST_ROWS]))
+        for piece, ks_got in zip(pieces, ks_gots):
             nc.vector.tensor_copy(
                 ks_dealt[:, piece].rearrange("p (g t s) -> p t g s", s=P, t=PARTS),
-                ks_got[:, piece].rearrange("p (g s t) -> p t g s", s=P, t=PARTS),
+                ks_got[:].rearrange("p (g s t) -> p t g s", s=P, t=PARTS),
             )
         for quad in range(QUADS):
             rows = slice(ks_first + PASSES * ROWS * quad, ks_first + PASSES * ROWS * (quad + 1))
             nc.sync.dma_start(ks_planes[QUAD * quad : QUAD * quad + ROWS].bitcast(I32), ks_dealt[rows, :].bitcast(I32))
-        vsc_got = keep.tile([P, PAGES * DV], U8, name="vsc_got", align_bytes=64)
-        nc.vector.tensor_copy(vsc_got[:], vsc_pool[:].indirect(voffs_sb[:]))
+        vsc_tail = keep.tile([P, last * DV], U8, name="vsc_tail", tag="ks_got0", align_bytes=64)
+        nc.vector.tensor_copy(vsc_tail[:], vsc_pool[:].indirect(voffs_sb[:, DV // LIST_ROWS :]))
         v_pool = keep.tile([P, POOL_PAGES * DV], I32, name="v_pool", tag="value_pool", align_bytes=64)
         nc.sync.dma_start(v_pool[:].rearrange("p (u e) -> p u e", e=DV), v_words.rearrange("u g e r -> g u (e r)").bitcast(I32))
-        vsc_plane = keep.tile([P, PAGES * DV], U8, name="vsc_plane", align_bytes=64)
-        for quad in range(QUADS):
-            rows = slice(vsc_first + ROWS * quad, vsc_first + ROWS * (quad + 1))
-            nc.sync.dma_start(vsc_plane[QUAD * quad : QUAD * quad + ROWS, :].bitcast(I32), vsc_got[rows, :].bitcast(I32))
+        vsc_plane = keep.tile([P, PAGES * DV], U8, name="vsc_plane", tag="ks_dealt", align_bytes=64)
+        for got, cols in ((vsc_head, slice(0, DV)), (vsc_tail, slice(DV, PAGES * DV))):
+            for quad in range(QUADS):
+                rows = slice(vsc_first + ROWS * quad, vsc_first + ROWS * (quad + 1))
+                nc.sync.dma_start(vsc_plane[QUAD * quad : QUAD * quad + ROWS, cols].bitcast(I32), got[rows, :].bitcast(I32))
 
         def entries_of(list_sb, pg):
             width = list_sb.shape[1] // PAGES
@@ -119,6 +122,10 @@ def tile_attend_pkv4q_silu_kernel(tc, q_words, q_scales, k_words, k_scales, v_wo
         nc.scalar.activation(vs_got[:], vs_pool[:].indirect(offs_sb[:]), ACT.Copy)
 
         p_all = keep.tile([P, PAGES, NQ * PARTS], F32, name="p_all", tag="vs_pool", align_bytes=64)
+
+        def query_runs(pg):
+            return [slice(0, NQ // 2), slice(NQ // 2, NQ)] if pg == last else [slice(0, NQ)]
+
         def gather_keys(pg):
             k_got = laid.tile([P, PAGE], U32, name="k_got%d" % pg, offset=pg * 4 * PAGE, align_bytes=64)
             nc.vector.tensor_copy(k_got[:], k_pool[:].bitcast(U32).indirect(entries_of(offs_sb, pg)))
@@ -132,7 +139,7 @@ def tile_attend_pkv4q_silu_kernel(tc, q_words, q_scales, k_words, k_scales, v_wo
             k_codes = keep.tile([P, PARTS, PASSES, 2 * P], U8, name="k_codes%d" % pg, align_bytes=64)
             dealt = k_codes[:].bitcast(U16).rearrange("p (h t) o s -> p h s (t o)", h=2)
             words = k_got[:].bitcast(U16).rearrange("p (s h r) -> p h s r", h=2, r=RUN)
-            if pg == last:
+            if pg != 1:
                 for h in range(2):
                     nc.vector.tensor_copy(dealt[:, h], words[:, h])
             else:
@@ -150,11 +157,18 @@ def tile_attend_pkv4q_silu_kernel(tc, q_words, q_scales, k_words, k_scales, v_wo
                         start=(o == 0),
                         stop=(o == PASSES - 1),
                     )
-            nc.scalar.activation(p_all[:, pg].rearrange("p (q t) -> p q t", t=PARTS), scores[:].rearrange("p t q -> p q t"), ACT.Silu)
+            for qs in query_runs(pg):
+                nc.scalar.activation(
+                    p_all[:, pg, qs.start * PARTS : qs.stop * PARTS].rearrange("p (q t) -> p q t", t=PARTS),
+                    scores[:, :, qs].rearrange("p t q -> p q t"),
+                    ACT.Silu,
+                )
 
         def weigh(pg):
             w_bf = keep.tile([P, PAGE], BF16, name="w_bf%d" % pg, align_bytes=64)
-            nc.vector.tensor_tensor(w_bf[:], p_all[:, pg], vs_got[:, pg * PAGE : (pg + 1) * PAGE], MULT)
+            for qs in query_runs(pg):
+                cols = slice(qs.start * PARTS, qs.stop * PARTS)
+                nc.vector.tensor_tensor(w_bf[:, cols], p_all[:, pg, cols], vs_got[:, pg * PAGE : (pg + 1) * PAGE][:, cols], MULT)
             return w_bf
 
         def quantise(pg, w_bf):

@@ -46,7 +46,7 @@ def tile_attend_pkv4q_silu_kernel(tc, q_words, q_scales, k_words, k_scales, v_wo
         make_identity(nc, ident[:])
         k_pool = keep.tile([P, T], I32, name="k_pool", tag="key_pool", align_bytes=64)
         ks_pool = keep.tile([P, T], U8, name="ks_pool")
-        vsc_pool = keep.tile([P, POOL_PAGES * DV], U8, name="vsc_pool", tag="value_pool", align_bytes=64)
+        vsc_pool = keep.tile([P, POOL_PAGES * DV], U8, name="vsc_pool", align_bytes=64)
         ks_planes = keep.tile([P, PASSES, N], U8, name="ks_planes", align_bytes=64)
         vs_pool = keep.tile([P, T], F32, name="vs_pool", align_bytes=64)
         q_codes = keep.tile([P, PASSES, NQ], I32, name="q_codes", align_bytes=64)
@@ -68,14 +68,19 @@ def tile_attend_pkv4q_silu_kernel(tc, q_words, q_scales, k_words, k_scales, v_wo
         nc.sync.dma_start(offs_sb[:], offs)
         nc.scalar.dma_start(ks_pool[ks_first:P, :].bitcast(I32), k_scales.bitcast(I32).rearrange("o f t -> f o t"))
         nc.sync.dma_start(vs_rows[0:POOL_PAGES, :], vs[0].rearrange("(u n) -> u n", n=PAGE))
-        nc.sync.dma_start(k_pool[:], k_words[0].rearrange("g t b -> g (t b)").bitcast(I32))
-        nc.sync.dma_start(q_codes[:], q_words[0].rearrange("o g q r -> g o (q r)").bitcast(I32))
-        for quad in range(QUADS):
-            queue = nc.sync if quad % 2 else nc.gpsimd
+
+        def load_q_scales(quad, queue):
             queue.dma_start(
                 q_planes[QUAD * quad : QUAD * quad + ROWS, :].bitcast(I32).rearrange("f (o q) -> f o q", o=PASSES),
                 q_scales[0, :, ROWS * quad : ROWS * (quad + 1), :].bitcast(I32).rearrange("o f q -> f o q"),
             )
+
+        load_q_scales(0, nc.scalar)
+        nc.sync.dma_start(k_pool[:], k_words[0].rearrange("g t b -> g (t b)").bitcast(I32))
+        nc.sync.dma_start(q_codes[:], q_words[0].rearrange("o g q r -> g o (q r)").bitcast(I32))
+        load_q_scales(1, nc.sync)
+        load_q_scales(2, nc.gpsimd)
+        load_q_scales(3, nc.gpsimd)
 
         warm = keep.tile([P, 1], F32, name="warm")
         nc.scalar.activation(warm[:], warm_in[:], ACT.Silu)
@@ -104,10 +109,10 @@ def tile_attend_pkv4q_silu_kernel(tc, q_words, q_scales, k_words, k_scales, v_wo
         for quad in range(QUADS):
             rows = slice(ks_first + PASSES * ROWS * quad, ks_first + PASSES * ROWS * (quad + 1))
             nc.sync.dma_start(ks_planes[QUAD * quad : QUAD * quad + ROWS].bitcast(I32), ks_dealt[rows, :].bitcast(I32))
+        v_pool = keep.tile([P, POOL_PAGES * DV], I32, name="v_pool", tag="ks_got1", align_bytes=64)
+        nc.sync.dma_start(v_pool[:].rearrange("p (u e) -> p u e", e=DV), v_words.rearrange("u g e r -> g u (e r)").bitcast(I32))
         vsc_tail = keep.tile([P, last * DV], U8, name="vsc_tail", tag="ks_got0", align_bytes=64)
         nc.vector.tensor_copy(vsc_tail[:], vsc_pool[:].indirect(voffs_sb[:, DV // LIST_ROWS :]))
-        v_pool = keep.tile([P, POOL_PAGES * DV], I32, name="v_pool", tag="value_pool", align_bytes=64)
-        nc.sync.dma_start(v_pool[:].rearrange("p (u e) -> p u e", e=DV), v_words.rearrange("u g e r -> g u (e r)").bitcast(I32))
         vsc_plane = keep.tile([P, PAGES * DV], U8, name="vsc_plane", tag="ks_dealt", align_bytes=64)
         for got, cols in ((vsc_head, slice(0, DV)), (vsc_tail, slice(DV, PAGES * DV))):
             for quad in range(QUADS):

@@ -183,17 +183,13 @@ def tile_attend_pkv4q_silu_kernel(tc, q_words, q_scales, k_words, k_scales, v_wo
             return w_codes, w_plane
 
         v_got = laid.tile([P, PAGES, DV], U32, name="v_got", offset=0, align_bytes=64)
-
-        def values(pg):
-            nc.vector.tensor_copy(v_got[:, pg, :], v_pool[:].bitcast(U32).indirect(entries_of(voffs_sb, pg)))
-
-        values(0)
-        w_0 = weigh(0)
-        values(1)
+        nc.vector.tensor_copy(v_got[:].rearrange("p g e -> p (g e)"), v_pool[:].bitcast(U32).indirect(voffs_sb[:]))
+        w_0 = laid.tile([P, PAGE], BF16, name="w_0", offset=last * 4 * PAGE, align_bytes=64)
+        nc.gpsimd.tensor_tensor(w_0[:], p_all[:, 0], vs_got[:, :PAGE], MULT)
+        w_1 = weigh(1)
         weights = [quantise(0, w_0)]
-        values(2)
-        w_bfs = [weigh(pg) for pg in range(1, PAGES)]
-        weights.extend(quantise(pg, w_bfs[pg - 1]) for pg in range(1, PAGES))
+        w_2 = weigh(last)
+        weights.extend([quantise(1, w_1), quantise(last, w_2)])
         acc = psum.tile([P, DV], F32, name="acc")
         for pg in range(PAGES):
             w_codes, w_plane = weights[pg]

@@ -6,6 +6,7 @@ from concourse.masks import make_identity
 NQ, N, T, D, DV = 128, 1536, 4096, 1024, 256
 P = 128
 PAGE = 512
+HALF = PAGE // 2
 PAGES = N // PAGE
 POOL_PAGES = T // PAGE
 PASSES = D // 512
@@ -15,6 +16,7 @@ BLOCKS = 16
 LIST_ROWS = 16
 QUAD = P // QUADS
 ROWS = BLOCKS // QUADS
+FILLED = 6
 RUN = 4
 OUT_SCALE = 1.0 / 16.0
 FLOPS = 2 * NQ * N * (D + DV)
@@ -88,11 +90,11 @@ def tile_attend_pkv4q_silu_kernel(tc, q_words, q_scales, k_words, k_scales, v_wo
         vs_cols = psum.tile([P, PARTS, P], F32, name="vs_cols")
         for t in range(PARTS):
             nc.tensor.transpose(vs_cols[:, t, :], vs_rows[:].rearrange("p (s t) -> p t s", t=PARTS)[:, t, :], ident[:])
-        nc.scalar.activation(
-            vs_pool[:].rearrange("p (u q t) -> p u q t", u=POOL_PAGES, t=PARTS),
-            vs_cols[:, :, 0:POOL_PAGES].rearrange("p t u -> p u t").unsqueeze(2).to_broadcast([P, POOL_PAGES, NQ, PARTS]),
-            ACT.Copy,
-        )
+        vs_by_page = vs_cols[:, :, 0:POOL_PAGES].rearrange("p t u -> p u t")
+        vs_pages = vs_pool[:].rearrange("p (u q t) -> p u q t", u=POOL_PAGES, t=PARTS)
+        vs_rest = laid.tile([P, POOL_PAGES - FILLED, 2 * PARTS], F32, name="vs_rest", offset=4 * (HALF - 2 * PARTS))[:, :, :PARTS]
+        nc.scalar.activation(vs_rest, vs_by_page[:, FILLED:], ACT.Copy)
+        nc.scalar.activation(vs_pages[:, :FILLED], vs_by_page[:, :FILLED].unsqueeze(2).to_broadcast([P, FILLED, NQ, PARTS]), ACT.Copy)
 
         vsc_head = keep.tile([P, DV], U8, name="vsc_head", align_bytes=64)
         nc.vector.tensor_copy(vsc_head[:], vsc_pool[:].indirect(voffs_sb[:, : DV // LIST_ROWS]))
@@ -113,6 +115,7 @@ def tile_attend_pkv4q_silu_kernel(tc, q_words, q_scales, k_words, k_scales, v_wo
         nc.sync.dma_start(v_pool[:].rearrange("p (u e) -> p u e", e=DV), v_words.rearrange("u g e r -> g u (e r)").bitcast(I32))
         vsc_tail = keep.tile([P, last * DV], U8, name="vsc_tail", tag="ks_got0", align_bytes=64)
         nc.vector.tensor_copy(vsc_tail[:], vsc_pool[:].indirect(voffs_sb[:, DV // LIST_ROWS :]))
+        nc.vector.tensor_copy(vs_pages[:, FILLED:], vs_rest.unsqueeze(2).to_broadcast([P, POOL_PAGES - FILLED, NQ, PARTS]))
         vsc_plane = keep.tile([P, PAGES * DV], U8, name="vsc_plane", tag="ks_dealt", align_bytes=64)
         for got, cols in ((vsc_head, slice(0, DV)), (vsc_tail, slice(DV, PAGES * DV))):
             for quad in range(QUADS):
@@ -131,24 +134,17 @@ def tile_attend_pkv4q_silu_kernel(tc, q_words, q_scales, k_words, k_scales, v_wo
         def query_runs(pg):
             return [slice(0, NQ // 2), slice(NQ // 2, NQ)] if pg == last else [slice(0, NQ)]
 
-        def gather_keys(pg):
-            k_got = laid.tile([P, PAGE], U32, name="k_got%d" % pg, offset=pg * 4 * PAGE, align_bytes=64)
-            nc.vector.tensor_copy(k_got[:], k_pool[:].bitcast(U32).indirect(entries_of(offs_sb, pg)))
-            return k_got
-
-        k_gots = [gather_keys(0)]
         for pg in range(PAGES):
-            if pg < last:
-                k_gots.append(gather_keys(pg + 1))
-            k_got = k_gots[pg]
+            k_gots = []
+            for c in range(2):
+                k_got = laid.tile([P, HALF], U32, name="k_got%d_%d" % (pg, c), offset=(1 - c) * 4 * HALF, align_bytes=64)
+                entries = entries_of(offs_sb, pg)[:, c * HALF // LIST_ROWS : (c + 1) * HALF // LIST_ROWS]
+                nc.vector.tensor_copy(k_got[:], k_pool[:].bitcast(U32).indirect(entries))
+                k_gots.append(k_got)
             k_codes = keep.tile([P, PARTS, PASSES, 2 * P], U8, name="k_codes%d" % pg, align_bytes=64)
-            dealt = k_codes[:].bitcast(U16).rearrange("p (h t) o s -> p h s (t o)", h=2)
-            words = k_got[:].bitcast(U16).rearrange("p (s h r) -> p h s r", h=2, r=RUN)
-            if pg != 1:
-                for h in range(2):
-                    nc.vector.tensor_copy(dealt[:, h], words[:, h])
-            else:
-                nc.vector.tensor_copy(dealt, words)
+            dealt = k_codes[:].bitcast(U16).rearrange("p (h t) o (c s) -> p c h s (t o)", h=2, c=2)
+            for c in range(2):
+                nc.vector.tensor_copy(dealt[:, c], k_gots[c][:].bitcast(U16).rearrange("p (s h r) -> p h s r", h=2, r=RUN))
             scores = psum.tile([P, PARTS, NQ], F32, name="scores%d" % pg)
             for t in range(PARTS):
                 for o in range(PASSES):
@@ -162,6 +158,13 @@ def tile_attend_pkv4q_silu_kernel(tc, q_words, q_scales, k_words, k_scales, v_wo
                         start=(o == 0),
                         stop=(o == PASSES - 1),
                     )
+            if pg == 0:
+                p_parts = p_all[:, 0].rearrange("p (t q) -> p t q", t=PARTS)
+                nc.scalar.activation(p_parts, scores[:], ACT.Silu)
+                w_parts = keep.tile([P, PARTS, NQ], BF16, name="w_parts", align_bytes=64)
+                for t in range(PARTS):
+                    nc.scalar.activation(w_parts[:, t, :], p_parts[:, t, :], ACT.Copy, scale=vs_got[:, t : t + 1])
+                continue
             for qs in query_runs(pg):
                 nc.scalar.activation(
                     p_all[:, pg, qs.start * PARTS : qs.stop * PARTS].rearrange("p (q t) -> p q t", t=PARTS),
@@ -169,12 +172,9 @@ def tile_attend_pkv4q_silu_kernel(tc, q_words, q_scales, k_words, k_scales, v_wo
                     ACT.Silu,
                 )
 
-        def weigh(pg):
-            w_bf = keep.tile([P, PAGE], BF16, name="w_bf%d" % pg, align_bytes=64)
-            for qs in query_runs(pg):
-                cols = slice(qs.start * PARTS, qs.stop * PARTS)
-                nc.vector.tensor_tensor(w_bf[:, cols], p_all[:, pg, cols], vs_got[:, pg * PAGE : (pg + 1) * PAGE][:, cols], MULT)
-            return w_bf
+        def weigh(pg, w_bf, qs):
+            cols = slice(qs.start * PARTS, qs.stop * PARTS)
+            nc.vector.tensor_tensor(w_bf[:, cols], p_all[:, pg, cols], vs_got[:, pg * PAGE : (pg + 1) * PAGE][:, cols], MULT)
 
         def quantise(pg, w_bf):
             w_codes = keep.tile([P, NQ], U32, name="w_codes%d" % pg, align_bytes=64)
@@ -182,16 +182,21 @@ def tile_attend_pkv4q_silu_kernel(tc, q_words, q_scales, k_words, k_scales, v_wo
             nc.vector.quantize_mx(out=w_codes[:].bitcast(FP8X4), scales=w_plane[:], in_=w_bf[:])
             return w_codes, w_plane
 
-        v_got = laid.tile([P, PAGES, DV], U32, name="v_got", offset=0, align_bytes=64)
+        v_got = laid.tile([P, PAGES, DV], U32, name="v_got", offset=4 * HALF, align_bytes=64)
         nc.vector.tensor_copy(v_got[:].rearrange("p g e -> p (g e)"), v_pool[:].bitcast(U32).indirect(voffs_sb[:]))
-        w_0 = laid.tile([P, PAGE], BF16, name="w_0", offset=last * 4 * PAGE, align_bytes=64)
-        nc.gpsimd.tensor_tensor(w_0[:], p_all[:, 0], vs_got[:, :PAGE], MULT)
-        w_1 = weigh(1)
-        weights = [quantise(0, w_0)]
-        w_2 = weigh(last)
-        weights.extend([quantise(1, w_1), quantise(last, w_2)])
+        w_0 = keep.tile([P, PAGE], BF16, name="w_0", tag="k_codes%d" % last, align_bytes=64)
+        nc.scalar.copy(w_0[:].rearrange("p (q t) -> p q t", t=PARTS), w_parts[:].rearrange("p t q -> p q t"))
+        w_1 = keep.tile([P, PAGE], BF16, name="w_1", align_bytes=64)
+        w_2 = keep.tile([P, PAGE], BF16, name="w_2", align_bytes=64)
+        weigh(1, w_1, query_runs(1)[0])
+        weigh(last, w_2, query_runs(last)[0])
+        weights = {1: quantise(1, w_1)}
+        weigh(last, w_2, query_runs(last)[1])
+        weights[0] = quantise(0, w_0)
+        weights[last] = quantise(last, w_2)
+        order = [1, 0, last]
         acc = psum.tile([P, DV], F32, name="acc")
-        for pg in range(PAGES):
+        for pg in order:
             w_codes, w_plane = weights[pg]
             nc.tensor.matmul_mx(
                 out=acc[:],
@@ -199,8 +204,8 @@ def tile_attend_pkv4q_silu_kernel(tc, q_words, q_scales, k_words, k_scales, v_wo
                 lhsT_scale=w_plane[:],
                 rhs=v_got[:, pg, :].bitcast(FP8X4),
                 rhs_scale=vsc_plane[:, pg * DV : (pg + 1) * DV],
-                start=(pg == 0),
-                stop=(pg == last),
+                start=(pg == order[0]),
+                stop=(pg == order[-1]),
             )
         result = keep.tile([P, DV], F32, name="result")
         nc.scalar.activation(result[:], acc[:], ACT.Copy, scale=OUT_SCALE)

@@ -16,7 +16,6 @@ BLOCKS = 16
 LIST_ROWS = 16
 QUAD = P // QUADS
 ROWS = BLOCKS // QUADS
-FILLED = 6
 RUN = 4
 OUT_SCALE = 1.0 / 16.0
 FLOPS = 2 * NQ * N * (D + DV)
@@ -87,14 +86,14 @@ def tile_attend_pkv4q_silu_kernel(tc, q_words, q_scales, k_words, k_scales, v_wo
         warm = keep.tile([P, 1], F32, name="warm")
         nc.scalar.activation(warm[:], warm_in[:], ACT.Silu)
 
-        vs_cols = psum.tile([P, PARTS, P], F32, name="vs_cols")
+        vs_cols = psum.tile([P, P, PARTS], F32, name="vs_cols")
         for t in range(PARTS):
-            nc.tensor.transpose(vs_cols[:, t, :], vs_rows[:].rearrange("p (s t) -> p t s", t=PARTS)[:, t, :], ident[:])
-        vs_by_page = vs_cols[:, :, 0:POOL_PAGES].rearrange("p t u -> p u t")
-        vs_pages = vs_pool[:].rearrange("p (u q t) -> p u q t", u=POOL_PAGES, t=PARTS)
-        vs_rest = laid.tile([P, POOL_PAGES - FILLED, 2 * PARTS], F32, name="vs_rest", offset=4 * (HALF - 2 * PARTS))[:, :, :PARTS]
-        nc.scalar.activation(vs_rest, vs_by_page[:, FILLED:], ACT.Copy)
-        nc.scalar.activation(vs_pages[:, :FILLED], vs_by_page[:, :FILLED].unsqueeze(2).to_broadcast([P, FILLED, NQ, PARTS]), ACT.Copy)
+            nc.tensor.transpose(vs_cols[:, :, t], vs_rows[:].rearrange("p (s t) -> p t s", t=PARTS)[:, t, :], ident[:])
+        nc.scalar.activation(
+            vs_pool[:].rearrange("p (u q t) -> p u q t", u=POOL_PAGES, t=PARTS),
+            vs_cols[:, 0:POOL_PAGES, :].unsqueeze(2).to_broadcast([P, POOL_PAGES, NQ, PARTS]),
+            ACT.Copy,
+        )
 
         vsc_head = keep.tile([P, DV], U8, name="vsc_head", align_bytes=64)
         nc.vector.tensor_copy(vsc_head[:], vsc_pool[:].indirect(voffs_sb[:, : DV // LIST_ROWS]))
@@ -115,7 +114,6 @@ def tile_attend_pkv4q_silu_kernel(tc, q_words, q_scales, k_words, k_scales, v_wo
         nc.sync.dma_start(v_pool[:].rearrange("p (u e) -> p u e", e=DV), v_words.rearrange("u g e r -> g u (e r)").bitcast(I32))
         vsc_tail = keep.tile([P, last * DV], U8, name="vsc_tail", tag="ks_got0", align_bytes=64)
         nc.vector.tensor_copy(vsc_tail[:], vsc_pool[:].indirect(voffs_sb[:, DV // LIST_ROWS :]))
-        nc.vector.tensor_copy(vs_pages[:, FILLED:], vs_rest.unsqueeze(2).to_broadcast([P, POOL_PAGES - FILLED, NQ, PARTS]))
         vsc_plane = keep.tile([P, PAGES * DV], U8, name="vsc_plane", tag="ks_dealt", align_bytes=64)
         for got, cols in ((vsc_head, slice(0, DV)), (vsc_tail, slice(DV, PAGES * DV))):
             for quad in range(QUADS):

@@ -17,6 +17,7 @@ LIST_ROWS = 16
 QUAD = P // QUADS
 ROWS = BLOCKS // QUADS
 RUN = 4
+WARM_PASSES = 3
 OUT_SCALE = 1.0 / 16.0
 FLOPS = 2 * NQ * N * (D + DV)
 
@@ -143,6 +144,18 @@ def tile_attend_pkv4q_silu_kernel(tc, q_words, q_scales, k_words, k_scales, v_wo
             dealt = k_codes[:].bitcast(U16).rearrange("p (h t) o (c s) -> p c h s (t o)", h=2, c=2)
             for c in range(2):
                 nc.vector.tensor_copy(dealt[:, c], k_gots[c][:].bitcast(U16).rearrange("p (s h r) -> p h s r", h=2, r=RUN))
+            if pg == 0:
+                unread = psum.tile([P, WARM_PASSES, NQ], F32, name="unread")
+                for i in range(WARM_PASSES):
+                    nc.tensor.matmul_mx(
+                        out=unread[:, i, :],
+                        lhsT=k_codes[:, i, 0, :].bitcast(FP4X4),
+                        lhsT_scale=q_planes[:, 0:P],
+                        rhs=q_codes[:, 0, :].bitcast(FP8X4),
+                        rhs_scale=q_planes[:, 0:NQ],
+                        start=True,
+                        stop=True,
+                    )
             scores = psum.tile([P, PARTS, NQ], F32, name="scores%d" % pg)
             for t in range(PARTS):
                 for o in range(PASSES):

@@ -11,6 +11,7 @@ PAGES = N // PAGE
 POOL_PAGES = T // PAGE
 PASSES = D // 512
 PARTS = 4
+PAIR = 2
 QUADS = 4
 BLOCKS = 16
 LIST_ROWS = 16
@@ -156,12 +157,13 @@ def tile_attend_pkv4q_silu_kernel(tc, q_words, q_scales, k_words, k_scales, v_wo
                         start=True,
                         stop=True,
                     )
-            scores = psum.tile([P, PARTS, NQ], F32, name="scores%d" % pg)
+            per_bank = PARTS if pg == 1 else PAIR
+            banks = [psum.tile([P, per_bank, NQ], F32, name="scores%d_%d" % (pg, h)) for h in range(PARTS // per_bank)]
             for t in range(PARTS):
                 for o in range(PASSES):
                     first = pg * PAGE + t * P
                     nc.tensor.matmul_mx(
-                        out=scores[:, t, :],
+                        out=banks[t // per_bank][:, t % per_bank, :],
                         lhsT=k_codes[:, t, o, :].bitcast(FP4X4),
                         lhsT_scale=ks_planes[:, o, first : first + P],
                         rhs=q_codes[:, o, :].bitcast(FP8X4),
@@ -171,21 +173,26 @@ def tile_attend_pkv4q_silu_kernel(tc, q_words, q_scales, k_words, k_scales, v_wo
                     )
             if pg == 0:
                 p_parts = p_all[:, 0].rearrange("p (t q) -> p t q", t=PARTS)
-                nc.scalar.activation(p_parts, scores[:], ACT.Silu)
+                for h, bank in enumerate(banks):
+                    nc.scalar.activation(p_parts[:, h * PAIR : (h + 1) * PAIR, :], bank[:], ACT.Silu)
                 w_parts = keep.tile([P, PARTS, NQ], BF16, name="w_parts", align_bytes=64)
                 for t in range(PARTS):
                     nc.scalar.activation(w_parts[:, t, :], p_parts[:, t, :], ACT.Copy, scale=vs_got[:, t : t + 1])
                 continue
-            for qs in query_runs(pg):
-                nc.scalar.activation(
-                    p_all[:, pg, qs.start * PARTS : qs.stop * PARTS].rearrange("p (q t) -> p q t", t=PARTS),
-                    scores[:, :, qs].rearrange("p t q -> p q t"),
-                    ACT.Silu,
-                )
+            p_banks = p_all[:, pg].rearrange("p (h q t) -> p h q t", q=NQ, t=per_bank)
+            for h, bank in enumerate(banks):
+                for qs in query_runs(pg) if h == len(banks) - 1 else [slice(0, NQ)]:
+                    nc.scalar.activation(p_banks[:, h, qs, :], bank[:, :, qs].rearrange("p t q -> p q t"), ACT.Silu)
 
         def weigh(pg, w_bf, qs):
             cols = slice(qs.start * PARTS, qs.stop * PARTS)
-            nc.vector.tensor_tensor(w_bf[:, cols], p_all[:, pg, cols], vs_got[:, pg * PAGE : (pg + 1) * PAGE][:, cols], MULT)
+            per_bank = PARTS if pg == 1 else PAIR
+            nc.vector.tensor_tensor(
+                w_bf[:, cols].rearrange("p (q h t) -> p q h t", h=PARTS // per_bank, t=per_bank),
+                p_all[:, pg].rearrange("p (h q t) -> p q h t", q=NQ, t=per_bank)[:, qs],
+                vs_got[:, pg * PAGE : (pg + 1) * PAGE][:, cols].rearrange("p (q h t) -> p q h t", h=PARTS // per_bank, t=per_bank),
+                MULT,
+            )
 
         def quantise(pg, w_bf):
             w_codes = keep.tile([P, NQ], U32, name="w_codes%d" % pg, align_bytes=64)

@@ -18,7 +18,6 @@ LIST_ROWS = 16
 QUAD = P // QUADS
 ROWS = BLOCKS // QUADS
 RUN = 4
-WARM_PASSES = 3
 OUT_SCALE = 1.0 / 16.0
 FLOPS = 2 * NQ * N * (D + DV)
 
@@ -51,7 +50,8 @@ def tile_attend_pkv4q_silu_kernel(tc, q_words, q_scales, k_words, k_scales, v_wo
         ks_pool = keep.tile([P, T], U8, name="ks_pool")
         vsc_pool = keep.tile([P, POOL_PAGES * DV], U8, name="vsc_pool", align_bytes=64)
         ks_planes = keep.tile([P, PASSES, N], U8, name="ks_planes", align_bytes=64)
-        vs_pool = keep.tile([P, T], F32, name="vs_pool", align_bytes=64)
+        vs_at = 16 * PAGE
+        vs_pool = laid.tile([P, T], F32, name="vs_pool", offset=vs_at, align_bytes=64)
         q_codes = keep.tile([P, PASSES, NQ], I32, name="q_codes", align_bytes=64)
         q_planes = keep.tile([P, PASSES * NQ], U8, name="q_planes", align_bytes=64)
 
@@ -129,10 +129,11 @@ def tile_attend_pkv4q_silu_kernel(tc, q_words, q_scales, k_words, k_scales, v_wo
         vs_got = keep.tile([P, N], F32, name="vs_got", align_bytes=64)
         nc.scalar.activation(vs_got[:], vs_pool[:].indirect(offs_sb[:]), ACT.Copy)
 
-        p_all = keep.tile([P, PAGES, NQ * PARTS], F32, name="p_all", tag="vs_pool", align_bytes=64)
+        p_all = laid.tile([P, PAGES, NQ * PARTS], F32, name="p_all", offset=vs_at, align_bytes=64)
+        p_runs = [laid.tile([P, HALF], F32, name="p_run%d" % i, offset=vs_at + 4 * (N + (1 - i) * HALF), align_bytes=64) for i in range(2)]
 
         def query_runs(pg):
-            return [slice(0, NQ // 2), slice(NQ // 2, NQ)] if pg == last else [slice(0, NQ)]
+            return [slice(0, NQ // 2), slice(NQ // 2, NQ)]
 
         for pg in range(PAGES):
             k_gots = []
@@ -145,19 +146,7 @@ def tile_attend_pkv4q_silu_kernel(tc, q_words, q_scales, k_words, k_scales, v_wo
             dealt = k_codes[:].bitcast(U16).rearrange("p (h t) o (c s) -> p c h s (t o)", h=2, c=2)
             for c in range(2):
                 nc.vector.tensor_copy(dealt[:, c], k_gots[c][:].bitcast(U16).rearrange("p (s h r) -> p h s r", h=2, r=RUN))
-            if pg == 0:
-                unread = psum.tile([P, WARM_PASSES, NQ], F32, name="unread")
-                for i in range(WARM_PASSES):
-                    nc.tensor.matmul_mx(
-                        out=unread[:, i, :],
-                        lhsT=k_codes[:, i, 0, :].bitcast(FP4X4),
-                        lhsT_scale=q_planes[:, 0:P],
-                        rhs=q_codes[:, 0, :].bitcast(FP8X4),
-                        rhs_scale=q_planes[:, 0:NQ],
-                        start=True,
-                        stop=True,
-                    )
-            per_bank = PARTS if pg == 1 else PAIR
+            per_bank = PARTS if pg == 0 else PAIR
             banks = [psum.tile([P, per_bank, NQ], F32, name="scores%d_%d" % (pg, h)) for h in range(PARTS // per_bank)]
             for t in range(PARTS):
                 for o in range(PASSES):
@@ -171,13 +160,19 @@ def tile_attend_pkv4q_silu_kernel(tc, q_words, q_scales, k_words, k_scales, v_wo
                         start=(o == 0),
                         stop=(o == PASSES - 1),
                     )
-            if pg == 0:
-                p_parts = p_all[:, 0].rearrange("p (t q) -> p t q", t=PARTS)
+            if pg == 1:
+                p_parts = p_all[:, 1].rearrange("p (t q) -> p t q", t=PARTS)
                 for h, bank in enumerate(banks):
                     nc.scalar.activation(p_parts[:, h * PAIR : (h + 1) * PAIR, :], bank[:], ACT.Silu)
                 w_parts = keep.tile([P, PARTS, NQ], BF16, name="w_parts", align_bytes=64)
                 for t in range(PARTS):
-                    nc.scalar.activation(w_parts[:, t, :], p_parts[:, t, :], ACT.Copy, scale=vs_got[:, t : t + 1])
+                    nc.scalar.activation(w_parts[:, t, :], p_parts[:, t, :], ACT.Copy, scale=vs_got[:, PAGE + t : PAGE + t + 1])
+                continue
+            if pg == 0:
+                for p_run, qs in zip(p_runs, query_runs(pg)):
+                    nc.scalar.activation(
+                        p_run[:].rearrange("p (q t) -> p q t", t=PARTS), banks[0][:, :, qs].rearrange("p t q -> p q t"), ACT.Silu
+                    )
                 continue
             p_banks = p_all[:, pg].rearrange("p (h q t) -> p h q t", q=NQ, t=per_bank)
             for h, bank in enumerate(banks):
@@ -186,7 +181,7 @@ def tile_attend_pkv4q_silu_kernel(tc, q_words, q_scales, k_words, k_scales, v_wo
 
         def weigh(pg, w_bf, qs):
             cols = slice(qs.start * PARTS, qs.stop * PARTS)
-            per_bank = PARTS if pg == 1 else PAIR
+            per_bank = PARTS if pg == 0 else PAIR
             nc.vector.tensor_tensor(
                 w_bf[:, cols].rearrange("p (q h t) -> p q h t", h=PARTS // per_bank, t=per_bank),
                 p_all[:, pg].rearrange("p (h q t) -> p q h t", q=NQ, t=per_bank)[:, qs],
@@ -194,25 +189,27 @@ def tile_attend_pkv4q_silu_kernel(tc, q_words, q_scales, k_words, k_scales, v_wo
                 MULT,
             )
 
-        def quantise(pg, w_bf):
+        def quantise(pg, w_bf, runs):
             w_codes = keep.tile([P, NQ], U32, name="w_codes%d" % pg, align_bytes=64)
             w_plane = keep.tile([P, NQ], U8, name="w_plane%d" % pg, align_bytes=64)
-            nc.vector.quantize_mx(out=w_codes[:].bitcast(FP8X4), scales=w_plane[:], in_=w_bf[:])
+            for qs in runs:
+                nc.vector.quantize_mx(out=w_codes[:, qs].bitcast(FP8X4), scales=w_plane[:, qs], in_=w_bf[:, qs.start * PARTS : qs.stop * PARTS])
             return w_codes, w_plane
 
-        v_got = laid.tile([P, PAGES, DV], U32, name="v_got", offset=4 * HALF, align_bytes=64)
+        w_0 = laid.tile([P, PAGE], BF16, name="w_0", offset=4 * HALF, align_bytes=64)
+        for i in range(2):
+            nc.vector.tensor_tensor(w_0[:, i * HALF : (i + 1) * HALF], p_runs[i][:], vs_got[:, i * HALF : (i + 1) * HALF], MULT)
+        weights = {0: quantise(0, w_0, query_runs(0))}
+        v_got = laid.tile([P, PAGES, DV], U32, name="v_got", offset=vs_at + 4 * (N + HALF), align_bytes=64)
         nc.vector.tensor_copy(v_got[:].rearrange("p g e -> p (g e)"), v_pool[:].bitcast(U32).indirect(voffs_sb[:]))
-        w_0 = keep.tile([P, PAGE], BF16, name="w_0", tag="k_codes%d" % last, align_bytes=64)
-        nc.scalar.copy(w_0[:].rearrange("p (q t) -> p q t", t=PARTS), w_parts[:].rearrange("p t q -> p q t"))
-        w_1 = keep.tile([P, PAGE], BF16, name="w_1", align_bytes=64)
+        w_1 = keep.tile([P, PAGE], BF16, name="w_1", tag="k_codes%d" % last, align_bytes=64)
+        nc.scalar.copy(w_1[:].rearrange("p (q t) -> p q t", t=PARTS), w_parts[:].rearrange("p t q -> p q t"))
         w_2 = keep.tile([P, PAGE], BF16, name="w_2", align_bytes=64)
-        weigh(1, w_1, query_runs(1)[0])
-        weigh(last, w_2, query_runs(last)[0])
-        weights = {1: quantise(1, w_1)}
-        weigh(last, w_2, query_runs(last)[1])
-        weights[0] = quantise(0, w_0)
-        weights[last] = quantise(last, w_2)
-        order = [1, 0, last]
+        for qs in query_runs(last):
+            weigh(last, w_2, qs)
+        weights[1] = quantise(1, w_1, [slice(0, NQ)])
+        weights[last] = quantise(last, w_2, [slice(0, NQ)])
+        order = [0, 1, last]
         acc = psum.tile([P, DV], F32, name="acc")
         for pg in order:
             w_codes, w_plane = weights[pg]

from contextlib import ExitStack

import concourse.mybir as mybir
from concourse.masks import make_identity

NQ, N, T, D, DV = 128, 1536, 4096, 1024, 256
P = 128
PAGE = 512
HALF = PAGE // 2
PAGES = N // PAGE
POOL_PAGES = T // PAGE
PASSES = D // 512
PARTS = 4
PAIR = 2
QUADS = 4
BLOCKS = 16
LIST_ROWS = 16
QUAD = P // QUADS
ROWS = BLOCKS // QUADS
RUN = 4
OUT_SCALE = 1.0 / 16.0
FLOPS = 2 * NQ * N * (D + DV)

F32 = mybir.dt.float32
BF16 = mybir.dt.bfloat16
I32 = mybir.dt.int32
U32 = mybir.dt.uint32
U16 = mybir.dt.uint16
U8 = mybir.dt.uint8
FP8X4 = mybir.dt.float8_e4m3fn_x4
FP4X4 = mybir.dt.float4_e2m1fn_x4
ACT = mybir.ActivationFunctionType
MULT = mybir.AluOpType.mult


def tile_attend_pkv4q_silu_kernel(tc, q_words, q_scales, k_words, k_scales, v_words, v_scales, vs, offs, voffs, out):
    nc = tc.nc
    last = PAGES - 1
    with ExitStack() as ctx:
        keep = ctx.enter_context(tc.tile_pool(name="keep", bufs=1))
        laid = ctx.enter_context(tc.tile_pool(name="laid", bufs=1))
        psum = ctx.enter_context(tc.psum_pool(name="psum", bufs=1))

        offs_sb = keep.tile([P, N // LIST_ROWS], U16, name="offs_sb")
        voffs_sb = keep.tile([P, PAGES * DV // LIST_ROWS], U16, name="voffs_sb")
        vs_rows = keep.tile([P, PAGE], F32, name="vs_rows")
        ident = keep.tile([P, P], F32, name="ident")
        make_identity(nc, ident[:])
        k_pool = keep.tile([P, T], I32, name="k_pool", tag="key_pool", align_bytes=64)
        ks_pool = keep.tile([P, T], U8, name="ks_pool")
        vsc_pool = keep.tile([P, POOL_PAGES * DV], U8, name="vsc_pool", align_bytes=64)
        ks_planes = keep.tile([P, PASSES, N], U8, name="ks_planes", align_bytes=64)
        vs_at = 16 * PAGE
        vs_pool = laid.tile([P, T], F32, name="vs_pool", offset=vs_at, align_bytes=64)
        q_codes = keep.tile([P, PASSES, NQ], I32, name="q_codes", align_bytes=64)
        q_planes = keep.tile([P, PASSES * NQ], U8, name="q_planes", align_bytes=64)

        ks_first = P - QUAD
        vsc_first = 2 * QUAD - BLOCKS
        warm_in = keep.tile([P, 1], F32, name="warm_in")
        nc.vector.memset(warm_in[:], 0.0)
        nc.vector.memset(vsc_pool[0:vsc_first, :].bitcast(I32), 0)
        nc.vector.memset(vsc_pool[2 * QUAD : P, :].bitcast(I32), 0)
        nc.vector.memset(ks_pool[0:ks_first, :].bitcast(I32), 0)

        nc.sync.dma_start(voffs_sb[:], voffs)
        nc.scalar.dma_start(
            vsc_pool[vsc_first : 2 * QUAD, :].bitcast(I32).rearrange("f (u e) -> f u e", u=POOL_PAGES),
            v_scales.bitcast(I32).rearrange("u f e -> f u e"),
        )
        nc.sync.dma_start(offs_sb[:], offs)
        nc.scalar.dma_start(ks_pool[ks_first:P, :].bitcast(I32), k_scales.bitcast(I32).rearrange("o f t -> f o t"))
        nc.sync.dma_start(vs_rows[0:POOL_PAGES, :], vs[0].rearrange("(u n) -> u n", n=PAGE))

        def load_q_scales(quad, queue):
            queue.dma_start(
                q_planes[QUAD * quad : QUAD * quad + ROWS, :].bitcast(I32).rearrange("f (o q) -> f o q", o=PASSES),
                q_scales[0, :, ROWS * quad : ROWS * (quad + 1), :].bitcast(I32).rearrange("o f q -> f o q"),
            )

        load_q_scales(0, nc.scalar)
        nc.sync.dma_start(k_pool[:], k_words[0].rearrange("g t b -> g (t b)").bitcast(I32))
        nc.sync.dma_start(q_codes[:], q_words[0].rearrange("o g q r -> g o (q r)").bitcast(I32))
        load_q_scales(1, nc.sync)
        load_q_scales(2, nc.gpsimd)
        load_q_scales(3, nc.gpsimd)

        warm = keep.tile([P, 1], F32, name="warm")
        nc.scalar.activation(warm[:], warm_in[:], ACT.Silu)

        vs_cols = psum.tile([P, P, PARTS], F32, name="vs_cols")
        for t in range(PARTS):
            nc.tensor.transpose(vs_cols[:, :, t], vs_rows[:].rearrange("p (s t) -> p t s", t=PARTS)[:, t, :], ident[:])
        nc.scalar.activation(
            vs_pool[:].rearrange("p (u q t) -> p u q t", u=POOL_PAGES, t=PARTS),
            vs_cols[:, 0:POOL_PAGES, :].unsqueeze(2).to_broadcast([P, POOL_PAGES, NQ, PARTS]),
            ACT.Copy,
        )

        vsc_head = keep.tile([P, DV], U8, name="vsc_head", align_bytes=64)
        nc.vector.tensor_copy(vsc_head[:], vsc_pool[:].indirect(voffs_sb[:, : DV // LIST_ROWS]))
        ks_dealt = keep.tile([P, N], U8, name="ks_dealt", align_bytes=64)
        pieces = [slice(0, PAGE), slice(PAGE, N)]
        ks_gots = [keep.tile([P, piece.stop - piece.start], U8, name="ks_got%d" % i, align_bytes=64) for i, piece in enumerate(pieces)]
        for piece, ks_got in zip(pieces, ks_gots):
            nc.vector.tensor_copy(ks_got[:], ks_pool[:].indirect(offs_sb[:, piece.start // LIST_ROWS : piece.stop // LIST_ROWS]))
        for piece, ks_got in zip(pieces, ks_gots):
            nc.vector.tensor_copy(
                ks_dealt[:, piece].rearrange("p (g t s) -> p t g s", s=P, t=PARTS),
                ks_got[:].rearrange("p (g s t) -> p t g s", s=P, t=PARTS),
            )
        for quad in range(QUADS):
            rows = slice(ks_first + PASSES * ROWS * quad, ks_first + PASSES * ROWS * (quad + 1))
            nc.sync.dma_start(ks_planes[QUAD * quad : QUAD * quad + ROWS].bitcast(I32), ks_dealt[rows, :].bitcast(I32))
        v_pool = keep.tile([P, POOL_PAGES * DV], I32, name="v_pool", tag="ks_got1", align_bytes=64)
        nc.sync.dma_start(v_pool[:].rearrange("p (u e) -> p u e", e=DV), v_words.rearrange("u g e r -> g u (e r)").bitcast(I32))
        vsc_tail = keep.tile([P, last * DV], U8, name="vsc_tail", tag="ks_got0", align_bytes=64)
        nc.vector.tensor_copy(vsc_tail[:], vsc_pool[:].indirect(voffs_sb[:, DV // LIST_ROWS :]))
        vsc_plane = keep.tile([P, PAGES * DV], U8, name="vsc_plane", tag="ks_dealt", align_bytes=64)
        for got, cols in ((vsc_head, slice(0, DV)), (vsc_tail, slice(DV, PAGES * DV))):
            for quad in range(QUADS):
                rows = slice(vsc_first + ROWS * quad, vsc_first + ROWS * (quad + 1))
                nc.sync.dma_start(vsc_plane[QUAD * quad : QUAD * quad + ROWS, cols].bitcast(I32), got[rows, :].bitcast(I32))

        def entries_of(list_sb, pg):
            width = list_sb.shape[1] // PAGES
            return list_sb[:, pg * width : (pg + 1) * width]

        vs_got = keep.tile([P, N], F32, name="vs_got", align_bytes=64)
        nc.scalar.activation(vs_got[:], vs_pool[:].indirect(offs_sb[:]), ACT.Copy)

        p_all = laid.tile([P, PAGES, NQ * PARTS], F32, name="p_all", offset=vs_at, align_bytes=64)
        p_runs = [laid.tile([P, HALF], F32, name="p_run%d" % i, offset=vs_at + 4 * (N + (1 - i) * HALF), align_bytes=64) for i in range(2)]

        def query_runs(pg):
            return [slice(0, NQ // 2), slice(NQ // 2, NQ)]

        for pg in range(PAGES):
            k_gots = []
            for c in range(2):
                k_got = laid.tile([P, HALF], U32, name="k_got%d_%d" % (pg, c), offset=(1 - c) * 4 * HALF, align_bytes=64)
                entries = entries_of(offs_sb, pg)[:, c * HALF // LIST_ROWS : (c + 1) * HALF // LIST_ROWS]
                nc.vector.tensor_copy(k_got[:], k_pool[:].bitcast(U32).indirect(entries))
                k_gots.append(k_got)
            k_codes = keep.tile([P, PARTS, PASSES, 2 * P], U8, name="k_codes%d" % pg, align_bytes=64)
            dealt = k_codes[:].bitcast(U16).rearrange("p (h t) o (c s) -> p c h s (t o)", h=2, c=2)
            for c in range(2):
                nc.vector.tensor_copy(dealt[:, c], k_gots[c][:].bitcast(U16).rearrange("p (s h r) -> p h s r", h=2, r=RUN))
            per_bank = PARTS if pg == 0 else PAIR
            banks = [psum.tile([P, per_bank, NQ], F32, name="scores%d_%d" % (pg, h)) for h in range(PARTS // per_bank)]
            for t in range(PARTS):
                for o in range(PASSES):
                    first = pg * PAGE + t * P
                    nc.tensor.matmul_mx(
                        out=banks[t // per_bank][:, t % per_bank, :],
                        lhsT=k_codes[:, t, o, :].bitcast(FP4X4),
                        lhsT_scale=ks_planes[:, o, first : first + P],
                        rhs=q_codes[:, o, :].bitcast(FP8X4),
                        rhs_scale=q_planes[:, o * NQ : (o + 1) * NQ],
                        start=(o == 0),
                        stop=(o == PASSES - 1),
                    )
            if pg == 1:
                p_parts = p_all[:, 1].rearrange("p (t q) -> p t q", t=PARTS)
                for h, bank in enumerate(banks):
                    nc.scalar.activation(p_parts[:, h * PAIR : (h + 1) * PAIR, :], bank[:], ACT.Silu)
                w_parts = keep.tile([P, PARTS, NQ], BF16, name="w_parts", align_bytes=64)
                for t in range(PARTS):
                    nc.scalar.activation(w_parts[:, t, :], p_parts[:, t, :], ACT.Copy, scale=vs_got[:, PAGE + t : PAGE + t + 1])
                continue
            if pg == 0:
                for p_run, qs in zip(p_runs, query_runs(pg)):
                    nc.scalar.activation(
                        p_run[:].rearrange("p (q t) -> p q t", t=PARTS), banks[0][:, :, qs].rearrange("p t q -> p q t"), ACT.Silu
                    )
                continue
            p_banks = p_all[:, pg].rearrange("p (h q t) -> p h q t", q=NQ, t=per_bank)
            for h, bank in enumerate(banks):
                for qs in query_runs(pg) if h == len(banks) - 1 else [slice(0, NQ)]:
                    nc.scalar.activation(p_banks[:, h, qs, :], bank[:, :, qs].rearrange("p t q -> p q t"), ACT.Silu)

        def weigh(pg, w_bf, qs):
            cols = slice(qs.start * PARTS, qs.stop * PARTS)
            per_bank = PARTS if pg == 0 else PAIR
            nc.vector.tensor_tensor(
                w_bf[:, cols].rearrange("p (q h t) -> p q h t", h=PARTS // per_bank, t=per_bank),
                p_all[:, pg].rearrange("p (h q t) -> p q h t", q=NQ, t=per_bank)[:, qs],
                vs_got[:, pg * PAGE : (pg + 1) * PAGE][:, cols].rearrange("p (q h t) -> p q h t", h=PARTS // per_bank, t=per_bank),
                MULT,
            )

        def quantise(pg, w_bf, runs):
            w_codes = keep.tile([P, NQ], U32, name="w_codes%d" % pg, align_bytes=64)
            w_plane = keep.tile([P, NQ], U8, name="w_plane%d" % pg, align_bytes=64)
            for qs in runs:
                nc.vector.quantize_mx(out=w_codes[:, qs].bitcast(FP8X4), scales=w_plane[:, qs], in_=w_bf[:, qs.start * PARTS : qs.stop * PARTS])
            return w_codes, w_plane

        w_0 = laid.tile([P, PAGE], BF16, name="w_0", offset=4 * HALF, align_bytes=64)
        for i in range(2):
            nc.vector.tensor_tensor(w_0[:, i * HALF : (i + 1) * HALF], p_runs[i][:], vs_got[:, i * HALF : (i + 1) * HALF], MULT)
        weights = {0: quantise(0, w_0, query_runs(0))}
        v_got = laid.tile([P, PAGES, DV], U32, name="v_got", offset=vs_at + 4 * (N + HALF), align_bytes=64)
        nc.vector.tensor_copy(v_got[:].rearrange("p g e -> p (g e)"), v_pool[:].bitcast(U32).indirect(voffs_sb[:]))
        w_1 = keep.tile([P, PAGE], BF16, name="w_1", tag="k_codes%d" % last, align_bytes=64)
        nc.scalar.copy(w_1[:].rearrange("p (q t) -> p q t", t=PARTS), w_parts[:].rearrange("p t q -> p q t"))
        w_2 = keep.tile([P, PAGE], BF16, name="w_2", align_bytes=64)
        for qs in query_runs(last):
            weigh(last, w_2, qs)
        weights[1] = quantise(1, w_1, [slice(0, NQ)])
        weights[last] = quantise(last, w_2, [slice(0, NQ)])
        order = [0, 1, last]
        acc = psum.tile([P, DV], F32, name="acc")
        for pg in order:
            w_codes, w_plane = weights[pg]
            nc.tensor.matmul_mx(
                out=acc[:],
                lhsT=w_codes[:].bitcast(FP8X4),
                lhsT_scale=w_plane[:],
                rhs=v_got[:, pg, :].bitcast(FP8X4),
                rhs_scale=vsc_plane[:, pg * DV : (pg + 1) * DV],
                start=(pg == order[0]),
                stop=(pg == order[-1]),
            )
        result = keep.tile([P, DV], F32, name="result")
        nc.scalar.activation(result[:], acc[:], ACT.Copy, scale=OUT_SCALE)
        nc.sync.dma_start(out[0], result[:])
